import numpy as np
import ml_dtypes


def mxq(x, axis, fmt="e4m3"):
    dtype, down = {"e4m3": (ml_dtypes.float8_e4m3fn, 7), "e5m2": (ml_dtypes.float8_e5m2, 14)}[fmt]
    v = np.moveaxis(np.asarray(x, np.float32).astype(ml_dtypes.bfloat16).astype(np.float64), axis, -1)
    blocks = v.reshape(v.shape[:-1] + (-1, 32))
    amax = np.abs(blocks).max(-1, keepdims=True)
    byte = np.maximum(np.where(amax > 0, np.frexp(amax)[1] - 1 + 127, 0) - down, 1)
    scale = np.exp2(byte - 127.0)
    codes = (blocks / scale).astype(np.float32).astype(dtype).astype(np.float64)
    return np.moveaxis((codes * scale).reshape(v.shape), -1, axis)


WIDE = False


def mx_kscale(k):
    if not WIDE:
        return np.ones(k)
    levels = np.array([18, -18])
    if k % 512:
        return np.exp2(np.random.permutation(np.resize(levels, k // 32))).repeat(32)
    a = np.empty((k // 512, 16))
    for p in range(k // 512):
        a[p, :8] = np.random.permutation(np.resize(levels, 8))
        for g in range(8):
            far = levels[np.abs(levels - a[p, g]) >= 10]
            a[p, g + 8] = far[np.random.randint(len(far))]
    return np.exp2(a.ravel()).repeat(32)


def f64(x):
    return np.asarray(x).astype(np.float64)


def striped(idx):
    return np.tile(np.asarray(idx).reshape(-1, 16).T, (8, 1)).astype(np.uint16)


def unstriped(offs):
    return offs[:16].T.reshape(-1).astype(np.int64)


B, N, T, D, R = 2, 512, 2048, 512, 512


def setup_inputs():
    n = np.random.standard_normal
    idx = np.random.permutation(T)[:B * N]
    s = mx_kscale(D)[:, None]
    z = mx_kscale(R)[:, None]
    u = np.ones(T)
    u[idx] = mx_kscale(B * N)
    r = np.random.uniform(0.5, 2.0, T) * u
    x = n((B, D, R))
    return {
        "xT": (x * s).astype(np.float32),
        "wT": (n((D, T)) * (1.00 / np.sqrt(D)) / s / r).astype(np.float32),
        "y": n((B, R, N)).astype(np.float32),
        "wt": (np.random.uniform(0.5, 1.5, (B, R, 1)) * 1.0 / np.sqrt(R) * z).astype(np.float32),
        "ts": np.tile(r, (128, 1)).astype(np.float32),
        "xm": (x.transpose(0, 2, 1) / z).astype(np.float32),
        "offs": striped(idx),
    }


def reference(xT, wT, y, wt, ts, xm, offs):
    idx = unstriped(offs)
    pick = lambda x: x[:, idx].reshape(x.shape[0], B, N).transpose(1, 0, 2)
    w = pick(f64(wT))
    a = mxq(f64(xT), 1, "e4m3").transpose(0, 2, 1) @ mxq(w, 1, "e4m3")
    ts_ = pick(f64(ts))[:, :1, :]
    a = a * ts_
    g = f64(wt) * (a - f64(y))
    g = g * ts_
    dw = mxq(f64(xm), 1, "e4m3").transpose(0, 2, 1) @ mxq(g, 1, "e5m2")
    gw = np.zeros((D, T))
    gw[:, idx] = dw.transpose(1, 0, 2).reshape(D, B * N)
    gx = mxq(g, 2, "e5m2") @ mxq(w, 2, "e4m3").transpose(0, 2, 1)
    return gw, gx

@@ -1,0 +1,292 @@
+from contextlib import ExitStack
+
+import concourse.mybir as mybir
+from concourse.masks import make_identity
+
+B, N, T, D, R = 2, 512, 2048, 512, 512
+FLOPS = 3 * 2 * B * N * D * R
+
+F32 = mybir.dt.float32
+BF16 = mybir.dt.bfloat16
+U32 = mybir.dt.uint32
+U16 = mybir.dt.uint16
+U8 = mybir.dt.uint8
+E4M3 = mybir.dt.float8_e4m3fn_x4
+E5M2 = mybir.dt.float8_e5m2_x4
+MULT = mybir.AluOpType.mult
+ADD = mybir.AluOpType.add
+COPY = mybir.ActivationFunctionType.Copy
+
+P = 128
+PACK = 4
+LIST_COLS = N // 16
+HALF = N // 2
+
+
+def tile_attend_gsq_wx_ts_kernel(tc, xT, wT, y, wt, ts, xm, offs, out_0, out_1):
+    nc = tc.nc
+    with ExitStack() as ctx:
+        sbuf = ctx.enter_context(tc.tile_pool(name="sbuf", bufs=1))
+        psum = ctx.enter_context(tc.psum_pool(name="psum", bufs=1))
+
+        def flat(ap):
+            return ap.rearrange("p a c -> p (a c)")
+
+        def block(k):
+            return slice(k * P, (k + 1) * P)
+
+        def grouped_tile(name):
+            return sbuf.tile([P, N, PACK], BF16, name=name, align_bytes=64)
+
+        def move(engine, out, in_):
+            if engine == "V":
+                nc.vector.tensor_copy(out=out, in_=in_)
+            elif engine == "G":
+                nc.gpsimd.tensor_scalar(out=out, in0=in_, scalar1=1.0, scalar2=0.0, op0=MULT, op1=ADD)
+            else:
+                nc.scalar.copy(out=out, in_=in_)
+
+        def interleave(engine, grouped, rows, cols):
+            move(engine, grouped[:, cols, :], rows[:, :, cols].rearrange("p t c -> p c t"))
+
+        def operand(name):
+            codes = sbuf.tile([P, N], U32, name=name + "_codes", align_bytes=64)
+            scales = sbuf.tile([P, N], U8, name=name + "_scales", align_bytes=64)
+            return codes, scales
+
+        def quantise(op, fmt, grouped, cols):
+            nc.vector.quantize_mx(out=op[0][:, cols].bitcast(fmt), scales=op[1][:, cols],
+                                  in_=flat(grouped[:, cols, :]))
+
+        def product(out, still, still_fmt, k, moving, moving_fmt):
+            nc.tensor.matmul_mx(out=flat(out[:]),
+                                lhsT=still[0][:, block(k)].bitcast(still_fmt), lhsT_scale=still[1][:, block(k)],
+                                rhs=moving[0][:].bitcast(moving_fmt), rhs_scale=moving[1][:],
+                                start=True, stop=True)
+
+        everything = slice(0, N)
+        halves = [slice(0, HALF), slice(HALF, N)]
+
+        offsets = sbuf.tile([P, B * LIST_COLS], U16, name="offsets")
+        nc.sync.dma_start(offsets[:], offs)
+        ts_cols = sbuf.tile([P, T // P + P], F32, name="ts_cols")
+        nc.gpsimd.memset(ts_cols[:, T // P:], 0.0)
+        nc.sync.dma_start(out=ts_cols[:, 0:T // P], in_=ts[0:1, :].rearrange("o (p c) -> (o p) c", p=P))
+        wt_rows = sbuf.tile([P, B, PACK], F32, name="wt_rows")
+        nc.sync.dma_start(out=wt_rows[:], in_=wt.rearrange("b (p t) o -> p b (t o)", t=PACK))
+        ident = sbuf.tile([P, P], F32, name="ident")
+        make_identity(nc, ident[:])
+
+        def load(src, name):
+            raw = sbuf.tile([P, PACK, N], F32, name=name)
+            nc.sync.dma_start(out=raw[:], in_=src.rearrange("(p t) c -> p t c", t=PACK))
+            return raw
+
+        def load_plane(t):
+            plane = sbuf.tile([P, T], F32, name="plane%d" % t, tag="wide%d" % t)
+            nc.sync.dma_start(out=plane[:], in_=wT.rearrange("(p t) c -> p t c", t=PACK)[:, t, :])
+            return plane
+
+        planes, x_raw, y_raw, xm_raw = {}, {}, {}, {}
+        planes[2] = load_plane(2)
+        planes[3] = load_plane(3)
+        x_raw[0] = load(xT[0], "x_raw0")
+        planes[0] = load_plane(0)
+        planes[1] = load_plane(1)
+        y_raw[0] = load(y[0], "y_raw0")
+        xm_raw[0] = load(xm[0], "xm_raw0")
+        x_raw[1] = load(xT[1], "x_raw1")
+        y_raw[1] = load(y[1], "y_raw1")
+        xm_raw[1] = load(xm[1], "xm_raw1")
+
+        windows = []
+        for c in range(PACK):
+            window = sbuf.tile([P, T], F32, name="window%d" % c)
+            nc.gpsimd.memset(window[:], 0.0)
+            windows.append(window)
+
+        ts_window = sbuf.tile([P, T], F32, name="ts_window", tag="wide4")
+        for k in range(PACK):
+            ts_bank = psum.tile([P, PACK, P], F32, name="ts_bank", tag="bank%d" % k)
+            for c in range(PACK):
+                col = PACK * k + c
+                nc.tensor.transpose(ts_bank[:, c, :], ts_cols[:, col:col + P], ident[:])
+            nc.scalar.activation(out=ts_window[:].rearrange("m (p c) -> m p c", p=P)[:, :, PACK * k:PACK * (k + 1)],
+                                 in_=ts_bank[:].rearrange("m c p -> m p c"), func=COPY)
+        banks = [psum.tile([P, PACK, P], F32, name="bank%d" % k, tag="bank%d" % k) for k in range(8)]
+
+        listed = sbuf.tile([P, PACK + 2, N], F32, name="listed")
+        w_listed = [listed[:, 0:PACK, :], listed[:, 2:PACK + 2, :]]
+
+        def gather(b, t, cols):
+            first = (b * N + cols.start) // 16
+            last = (b * N + cols.stop) // 16
+            nc.vector.tensor_copy(w_listed[b][:, t, cols], planes[t][:].indirect(offsets[:, first:last]))
+
+        w_slots = [grouped_tile("w_slots%d" % b) for b in range(B)]
+
+        def turn_plane(b, t, bank):
+            for s in range(PACK):
+                nc.tensor.transpose(bank[:, s, :], w_listed[b][:, t, s:N:PACK], ident[:])
+            nc.scalar.copy(out=w_slots[b][:, block(t), :], in_=bank[:].rearrange("p s m -> p m s"))
+
+        for t in (2, 3):
+            for b in range(B):
+                gather(b, t, everything)
+        ts_listed = sbuf.tile([P, B * N], F32, name="ts_listed")
+        nc.vector.tensor_copy(ts_listed[:], ts_window[:].indirect(offsets[:]))
+
+        x_grouped = grouped_tile("x_grouped")
+        x_op = [operand("x%d" % b) for b in range(B)]
+        interleave("S", x_grouped, x_raw[0], everything)
+        quantise(x_op[0], E4M3, x_grouped, everything)
+        for t in (2, 3):
+            for b in range(B):
+                turn_plane(b, t, banks[4 + 2 * (t - 2) + b])
+
+        minus_ts = sbuf.tile([P, B, PACK], F32, name="minus_ts")
+        ts_squared = sbuf.tile([P, B, PACK], F32, name="ts_squared")
+        for b in range(B):
+            for j in range(PACK):
+                nc.tensor.transpose(banks[b][:, j, :], ts_listed[:, b * N + j * P:b * N + (j + 1) * P], ident[:])
+            nc.scalar.activation(out=minus_ts[:, b, :], in_=banks[b][:, :, 0], func=COPY, scale=-1.0)
+        nc.gpsimd.tensor_tensor(out=ts_squared[:], in0=minus_ts[:], in1=minus_ts[:], op=MULT)
+
+        w_grouped = grouped_tile("w_grouped")
+        w_op = [operand("w_d%d" % b) for b in range(B)]
+        gather(0, 0, everything)
+        for cols in halves:
+            gather(0, 1, cols)
+        turn_plane(0, 0, banks[2])
+        interleave("S", w_grouped, w_listed[0], halves[0])
+        interleave("V", w_grouped, w_listed[0], halves[1])
+        for cols in halves:
+            quantise(w_op[0], E4M3, w_grouped, cols)
+
+        a_parts = sbuf.tile([P, PACK, PACK, P], F32, name="a_parts", align_bytes=64)
+        a_part = [a_parts[:, j, :, :] for j in range(PACK)]
+        y_part = [sbuf.tile([P, PACK, P], F32, name="y_part%d" % j) for j in range(PACK)]
+
+        def target_part(b, j):
+            bank = banks[4 * b + j % 2]
+            for t in range(PACK):
+                nc.tensor.transpose(bank[:, t, :], y_raw[b][:, t, block(j)], ident[:])
+            nc.scalar.activation(out=y_part[j][:], in_=bank[:], func=COPY, scale=minus_ts[:, b, j:j + 1])
+
+        def score_part(b, j):
+            bank = banks[((2, 3, 6, 7), (2, 3, 0, 1))[b][j]]
+            product(bank, w_op[b], E4M3, j, x_op[b], E4M3)
+            nc.scalar.activation(out=a_part[j], in_=flat(bank[:]).rearrange("p (m t) -> p t m", t=PACK),
+                                 func=COPY, scale=ts_squared[:, b, j:j + 1])
+
+        def add_parts(out, j, t):
+            nc.tensor.matmul(out, lhsT=a_part[j][:, t, :], rhs=ident[:], start=True, stop=False, is_transpose=True)
+            nc.tensor.matmul(out, lhsT=y_part[j][:, t, :], rhs=ident[:], start=False, stop=True, is_transpose=True)
+
+        h_grouped = [grouped_tile("h_grouped%d" % b) for b in range(B)]
+        h_op = [operand("h_r%d" % b) for b in range(B)]
+        for j in range(PACK):
+            target_part(0, j)
+            score_part(0, j)
+            bank = banks[4 + j % 2]
+            for t in range(PACK):
+                add_parts(bank[:, t, :], j, t)
+            nc.vector.tensor_tensor(out=h_grouped[0][:, block(j), :], in0=bank[:].rearrange("p t i -> p i t"),
+                                    in1=wt_rows[:, 0:1, :].to_broadcast([P, P, PACK]), op=MULT)
+            quantise(h_op[0], E5M2, h_grouped[0], block(j))
+
+        xm_grouped = grouped_tile("xm_grouped")
+        xm_op = [operand("xm%d" % b) for b in range(B)]
+        dw = [sbuf.tile([P, PACK, N], F32, name="dw%d" % b, tag="wide%d" % (4 - b)) for b in range(B)]
+
+        def xm_block(b, c):
+            interleave("S", xm_grouped, xm_raw[b], block(c))
+            quantise(xm_op[b], E4M3, xm_grouped, block(c))
+
+        def table_gradient(b, c):
+            bank = banks[6 + c % 2]
+            product(bank, xm_op[b], E4M3, c, h_op[b], E5M2)
+            nc.scalar.copy(out=dw[b][:, c, :], in_=flat(bank[:]))
+            nc.vector.tensor_copy(windows[c][:].indirect(offsets[:, b * LIST_COLS:(b + 1) * LIST_COLS]),
+                                  dw[b][:, c, :])
+            if b == B - 1:
+                nc.sync.dma_start(out=out_0[block(c), :], in_=windows[c][:])
+
+        xm_block(0, 0)
+        xm_block(0, 1)
+        turn_plane(0, 1, banks[3])
+        for t in (0, 1):
+            for cols in halves:
+                gather(1, t, cols)
+        interleave("V", w_grouped, w_listed[1], everything)
+        quantise(w_op[1], E4M3, w_grouped, everything)
+        table_gradient(0, 0)
+        x_grouped = (a_parts[:, 2:PACK, :, :].rearrange("p j t m -> p (j t m)").bitcast(BF16)
+                     .rearrange("p (c k) -> p c k", k=PACK))
+        for k in range(PACK):
+            interleave("S", x_grouped, x_raw[1], block(k))
+        quantise(x_op[1], E4M3, x_grouped, everything)
+        xm_block(0, 2)
+        table_gradient(0, 1)
+        for j in range(PACK):
+            target_part(1, j)
+        xm_block(0, 3)
+        table_gradient(0, 2)
+        for j in range(PACK):
+            score_part(1, j)
+        table_gradient(0, 3)
+        h_rows = sbuf.tile([P, PACK, N], BF16, name="h_rows")
+        for t in range(PACK):
+            bank = banks[4 + t % 2]
+            for j in range(PACK):
+                add_parts(bank[:, j, :], j, t)
+            nc.scalar.activation(out=h_rows[:, t, :], in_=flat(bank[:]), func=COPY, scale=wt_rows[:, 1, t:t + 1])
+        xm_block(1, 0)
+        interleave("S", h_grouped[1], h_rows, halves[0])
+        interleave("V", h_grouped[1], h_rows, halves[1])
+        quantise(h_op[1], E5M2, h_grouped[1], everything)
+        xm_block(1, 1)
+        table_gradient(1, 0)
+
+        w_slot_op = [operand("w_i%d" % b) for b in range(B)]
+        h_slot_op = [operand("h_i%d" % b) for b in range(B)]
+        h_slots = [grouped_tile("h_slots%d" % b) for b in range(B)]
+
+        def row_gradient(b):
+            gx = sbuf.tile([P, PACK, D], F32, name="gx%d" % b, tag="wide%d" % b)
+            for t in range(PACK):
+                bank = banks[6 + t % 2]
+                product(bank, h_slot_op[b], E5M2, t, w_slot_op[b], E4M3)
+                nc.scalar.copy(out=gx[:, t, :].rearrange("p (m k) -> p m k", k=PACK),
+                               in_=bank[:].rearrange("p k m -> p m k"))
+            nc.scalar.dma_start(out=out_1[b].rearrange("(p t) c -> p t c", t=PACK), in_=gx[:])
+
+        h_words = flat(h_grouped[0][:]).bitcast(F32)
+        for u in range(2):
+            for s in range(PACK):
+                nc.tensor.transpose(banks[5 - u][:, s, :], h_words[:, 2 * s + u:2 * N:2 * PACK], ident[:])
+            nc.scalar.copy(
+                out=h_slots[0][:, u * HALF:(u + 1) * HALF, :].rearrange("p (e m) s -> p e m s", e=2),
+                in_=flat(banks[5 - u][:]).bitcast(BF16).rearrange("p (s m e) -> p e m s", s=PACK, e=2))
+        quantise(w_slot_op[0], E4M3, w_slots[0], everything)
+        quantise(h_slot_op[0], E5M2, h_slots[0], everything)
+        xm_block(1, 2)
+        table_gradient(1, 1)
+        for t in (0, 1):
+            turn_plane(1, t, banks[6 + t])
+        h_slot_words = flat(h_slots[1][:]).bitcast(F32)
+        for k in range(2):
+            for t in range(2):
+                row_words = h_rows[:, 2 * k + t, :].bitcast(F32)
+                for u in range(2):
+                    nc.tensor.transpose(banks[k][:, 2 * t + u, :], row_words[:, u:HALF:2], ident[:])
+            nc.scalar.copy(
+                out=h_slot_words[:, k * N:(k + 1) * N].rearrange("p (t m u) -> p t m u", t=2, u=2),
+                in_=banks[k][:].rearrange("p (t u) m -> p t m u", u=2))
+        quantise(w_slot_op[1], E4M3, w_slots[1], everything)
+        quantise(h_slot_op[1], E5M2, h_slots[1], everything)
+        row_gradient(0)
+        xm_block(1, 3)
+        table_gradient(1, 2)
+        row_gradient(1)
+        table_gradient(1, 3)

@@ -36,7 +36,7 @@ def tile_attend_gsq_wx_ts_kernel(tc, xT, wT, y, wt, ts, xm, offs, out_0, out_1):
             return slice(k * P, (k + 1) * P)
 
         def grouped_tile(name):
-            return sbuf.tile([P, N, PACK], BF16, name=name, align_bytes=64)
+            return sbuf.tile([P, N, PACK], BF16, name=name, tag=name, align_bytes=64)
 
         def move(engine, out, in_):
             if engine == "V":
@@ -69,30 +69,31 @@ def tile_attend_gsq_wx_ts_kernel(tc, xT, wT, y, wt, ts, xm, offs, out_0, out_1):
 
         offsets = sbuf.tile([P, B * LIST_COLS], U16, name="offsets")
         nc.sync.dma_start(offsets[:], offs)
-        ts_cols = sbuf.tile([P, T // P + P], F32, name="ts_cols")
-        nc.gpsimd.memset(ts_cols[:, T // P:], 0.0)
-        nc.sync.dma_start(out=ts_cols[:, 0:T // P], in_=ts[0:1, :].rearrange("o (p c) -> (o p) c", p=P))
+        ts_window = sbuf.tile([P, T], F32, name="ts_window")
+        nc.vector.memset(ts_window[:], 0.0)
+        nc.scalar.dma_start(out=ts_window[0:1, :], in_=ts[0:1, :])
         wt_rows = sbuf.tile([P, B, PACK], F32, name="wt_rows")
         nc.sync.dma_start(out=wt_rows[:], in_=wt.rearrange("b (p t) o -> p b (t o)", t=PACK))
         ident = sbuf.tile([P, P], F32, name="ident")
         make_identity(nc, ident[:])
 
         def load(src, name):
-            raw = sbuf.tile([P, PACK, N], F32, name=name)
+            raw = sbuf.tile([P, PACK, N], F32, name=name, tag="raw", bufs=4)
             nc.sync.dma_start(out=raw[:], in_=src.rearrange("(p t) c -> p t c", t=PACK))
             return raw
 
-        def load_plane(t):
-            plane = sbuf.tile([P, T], F32, name="plane%d" % t, tag="wide%d" % t)
-            nc.sync.dma_start(out=plane[:], in_=wT.rearrange("(p t) c -> p t c", t=PACK)[:, t, :])
-            return plane
+        def load_chunk(u, k):
+            chunk = sbuf.tile([P, 2, T // 2], F32, name="chunk%d%d" % (u, k), tag="raw", bufs=4)
+            rows = wT.rearrange("(p t) c -> p t c", t=PACK)
+            nc.sync.dma_start(out=chunk[:], in_=rows[:, 2 * u:2 * u + 2, k * (T // 2):(k + 1) * (T // 2)])
+            return chunk
 
-        planes, x_raw, y_raw, xm_raw = {}, {}, {}, {}
-        planes[2] = load_plane(2)
-        planes[3] = load_plane(3)
+        chunks, x_raw, y_raw, xm_raw = {}, {}, {}, {}
+        chunks[0, 0] = load_chunk(0, 0)
+        chunks[0, 1] = load_chunk(0, 1)
         x_raw[0] = load(xT[0], "x_raw0")
-        planes[0] = load_plane(0)
-        planes[1] = load_plane(1)
+        chunks[1, 0] = load_chunk(1, 0)
+        chunks[1, 1] = load_chunk(1, 1)
         y_raw[0] = load(y[0], "y_raw0")
         xm_raw[0] = load(xm[0], "xm_raw0")
         x_raw[1] = load(xT[1], "x_raw1")
@@ -105,44 +106,52 @@ def tile_attend_gsq_wx_ts_kernel(tc, xT, wT, y, wt, ts, xm, offs, out_0, out_1):
             nc.gpsimd.memset(window[:], 0.0)
             windows.append(window)
 
-        ts_window = sbuf.tile([P, T], F32, name="ts_window", tag="wide4")
-        for k in range(PACK):
-            ts_bank = psum.tile([P, PACK, P], F32, name="ts_bank", tag="bank%d" % k)
-            for c in range(PACK):
-                col = PACK * k + c
-                nc.tensor.transpose(ts_bank[:, c, :], ts_cols[:, col:col + P], ident[:])
-            nc.scalar.activation(out=ts_window[:].rearrange("m (p c) -> m p c", p=P)[:, :, PACK * k:PACK * (k + 1)],
-                                 in_=ts_bank[:].rearrange("m c p -> m p c"), func=COPY)
-        banks = [psum.tile([P, PACK, P], F32, name="bank%d" % k, tag="bank%d" % k) for k in range(8)]
+        banks = [psum.tile([P, PACK, P], F32, name="bank%d" % k) for k in range(8)]
 
-        listed = sbuf.tile([P, PACK + 2, N], F32, name="listed")
-        w_listed = [listed[:, 0:PACK, :], listed[:, 2:PACK + 2, :]]
+        pairs = [sbuf.tile([P, T, 2], BF16, name="pairs%d" % u) for u in range(2)]
 
-        def gather(b, t, cols):
+        def cast_chunk(engine, u, k, first, last):
+            out = pairs[u][:, k * (T // 2) + first:k * (T // 2) + last, :]
+            in_ = chunks[u, k][:, :, first:last].rearrange("p e c -> p c e")
+            if engine == "V":
+                nc.vector.tensor_copy(out=out, in_=in_)
+            else:
+                nc.scalar.activation(out=out, in_=in_, func=COPY)
+
+        listed = [sbuf.tile([P, 2, N, 2], BF16, name="listed%d" % b) for b in range(B)]
+
+        def gather(b, u, cols):
             first = (b * N + cols.start) // 16
             last = (b * N + cols.stop) // 16
-            nc.vector.tensor_copy(w_listed[b][:, t, cols], planes[t][:].indirect(offsets[:, first:last]))
+            nc.vector.tensor_copy(flat(listed[b][:, u, cols, :]).bitcast(U32),
+                                  flat(pairs[u][:]).bitcast(U32).indirect(offsets[:, first:last]))
+
+        def join_pairs(b, cols):
+            nc.vector.tensor_copy(out=w_grouped[:, cols, :].rearrange("p c (u e) -> p c u e", u=2),
+                                  in_=listed[b][:, :, cols, :].rearrange("p u c e -> p c u e"))
 
         w_slots = [grouped_tile("w_slots%d" % b) for b in range(B)]
 
-        def turn_plane(b, t, bank):
+        def turn_pairs(b, u, bank):
+            words = flat(listed[b][:, u, :, :]).bitcast(F32)
             for s in range(PACK):
-                nc.tensor.transpose(bank[:, s, :], w_listed[b][:, t, s:N:PACK], ident[:])
-            nc.scalar.copy(out=w_slots[b][:, block(t), :], in_=bank[:].rearrange("p s m -> p m s"))
+                nc.tensor.transpose(bank[:, s, :], words[:, s:N:PACK], ident[:])
+            nc.scalar.copy(out=w_slots[b][:, halves[u], :].rearrange("p (m e) s -> p m e s", e=2),
+                           in_=flat(bank[:]).bitcast(BF16).rearrange("p (s m e) -> p m e s", s=PACK, e=2))
 
-        for t in (2, 3):
-            for b in range(B):
-                gather(b, t, everything)
         ts_listed = sbuf.tile([P, B * N], F32, name="ts_listed")
         nc.vector.tensor_copy(ts_listed[:], ts_window[:].indirect(offsets[:]))
-
+        cast_chunk("V", 0, 0, 0, T // 2)
+        cast_chunk("S", 0, 1, 0, T // 2)
         x_grouped = grouped_tile("x_grouped")
         x_op = [operand("x%d" % b) for b in range(B)]
         interleave("S", x_grouped, x_raw[0], everything)
+        for b in range(B):
+            gather(b, 0, everything)
+        cast_chunk("S", 1, 0, 0, T // 2)
         quantise(x_op[0], E4M3, x_grouped, everything)
-        for t in (2, 3):
-            for b in range(B):
-                turn_plane(b, t, banks[4 + 2 * (t - 2) + b])
+        cast_chunk("S", 1, 1, 0, 384)
+        cast_chunk("V", 1, 1, 384, T // 2)
 
         minus_ts = sbuf.tile([P, B, PACK], F32, name="minus_ts")
         ts_squared = sbuf.tile([P, B, PACK], F32, name="ts_squared")
@@ -154,57 +163,61 @@ def tile_attend_gsq_wx_ts_kernel(tc, xT, wT, y, wt, ts, xm, offs, out_0, out_1):
 
         w_grouped = grouped_tile("w_grouped")
         w_op = [operand("w_d%d" % b) for b in range(B)]
-        gather(0, 0, everything)
         for cols in halves:
             gather(0, 1, cols)
-        turn_plane(0, 0, banks[2])
-        interleave("S", w_grouped, w_listed[0], halves[0])
-        interleave("V", w_grouped, w_listed[0], halves[1])
+        for cols in halves:
+            join_pairs(0, cols)
         for cols in halves:
             quantise(w_op[0], E4M3, w_grouped, cols)
+        gather(1, 1, everything)
+        join_pairs(1, everything)
+        quantise(w_op[1], E4M3, w_grouped, everything)
 
-        a_parts = sbuf.tile([P, PACK, PACK, P], F32, name="a_parts", align_bytes=64)
-        a_part = [a_parts[:, j, :, :] for j in range(PACK)]
-        y_part = [sbuf.tile([P, PACK, P], F32, name="y_part%d" % j) for j in range(PACK)]
+        for b in range(B):
+            turn_pairs(b, 0, banks[2 + b])
 
-        def target_part(b, j):
-            bank = banks[4 * b + j % 2]
+        def part(name, j):
+            return sbuf.tile([P, PACK, P], F32, name=name, tag="%s%d" % (name, j), align_bytes=64)
+
+        def by_row_slot(bank):
+            return flat(bank[:]).rearrange("p (m t) -> p t m", t=PACK)
+
+        def target_part(b, j, bank):
             for t in range(PACK):
                 nc.tensor.transpose(bank[:, t, :], y_raw[b][:, t, block(j)], ident[:])
-            nc.scalar.activation(out=y_part[j][:], in_=bank[:], func=COPY, scale=minus_ts[:, b, j:j + 1])
+            out = part("y_part", j)
+            nc.scalar.activation(out=out[:], in_=bank[:], func=COPY, scale=minus_ts[:, b, j:j + 1])
+            return out
 
-        def score_part(b, j):
-            bank = banks[((2, 3, 6, 7), (2, 3, 0, 1))[b][j]]
-            product(bank, w_op[b], E4M3, j, x_op[b], E4M3)
-            nc.scalar.activation(out=a_part[j], in_=flat(bank[:]).rearrange("p (m t) -> p t m", t=PACK),
-                                 func=COPY, scale=ts_squared[:, b, j:j + 1])
-
-        def add_parts(out, j, t):
-            nc.tensor.matmul(out, lhsT=a_part[j][:, t, :], rhs=ident[:], start=True, stop=False, is_transpose=True)
-            nc.tensor.matmul(out, lhsT=y_part[j][:, t, :], rhs=ident[:], start=False, stop=True, is_transpose=True)
+        def residual(b, j, scores, targets):
+            out = part("z_part", j)
+            nc.vector.scalar_tensor_tensor(out=out[:], in0=by_row_slot(scores), scalar=ts_squared[:, b, j:j + 1],
+                                           in1=targets[:], op0=MULT, op1=ADD)
+            return out
 
         h_grouped = [grouped_tile("h_grouped%d" % b) for b in range(B)]
         h_op = [operand("h_r%d" % b) for b in range(B)]
+        y_part = [target_part(0, j, banks[4 + j]) for j in range(PACK)]
         for j in range(PACK):
-            target_part(0, j)
-            score_part(0, j)
-            bank = banks[4 + j % 2]
-            for t in range(PACK):
-                add_parts(bank[:, t, :], j, t)
-            nc.vector.tensor_tensor(out=h_grouped[0][:, block(j), :], in0=bank[:].rearrange("p t i -> p i t"),
-                                    in1=wt_rows[:, 0:1, :].to_broadcast([P, P, PACK]), op=MULT)
-            quantise(h_op[0], E5M2, h_grouped[0], block(j))
+            product(banks[j], w_op[0], E4M3, j, x_op[0], E4M3)
+        z_part = {}
+        for j in range(PACK + 2):
+            if j < PACK:
+                z_part[j] = residual(0, j, banks[j], y_part[j])
+                for t in range(PACK):
+                    nc.tensor.transpose(banks[4 + j % 2][:, t, :], z_part[j][:, t, :], ident[:])
+            if 1 <= j <= PACK:
+                nc.vector.tensor_tensor(out=h_grouped[0][:, block(j - 1), :],
+                                        in0=banks[4 + (j - 1) % 2][:].rearrange("p t i -> p i t"),
+                                        in1=wt_rows[:, 0:1, :].to_broadcast([P, P, PACK]), op=MULT)
+            if j >= 2:
+                quantise(h_op[0], E5M2, h_grouped[0], block(j - 2))
 
         xm_grouped = grouped_tile("xm_grouped")
         xm_op = [operand("xm%d" % b) for b in range(B)]
-        dw = [sbuf.tile([P, PACK, N], F32, name="dw%d" % b, tag="wide%d" % (4 - b)) for b in range(B)]
+        dw = [sbuf.tile([P, PACK, N], F32, name="dw%d" % b) for b in range(B)]
 
-        def xm_block(b, c):
-            interleave("S", xm_grouped, xm_raw[b], block(c))
-            quantise(xm_op[b], E4M3, xm_grouped, block(c))
-
-        def table_gradient(b, c):
-            bank = banks[6 + c % 2]
+        def table_gradient(b, c, bank):
             product(bank, xm_op[b], E4M3, c, h_op[b], E5M2)
             nc.scalar.copy(out=dw[b][:, c, :], in_=flat(bank[:]))
             nc.vector.tensor_copy(windows[c][:].indirect(offsets[:, b * LIST_COLS:(b + 1) * LIST_COLS]),
@@ -212,81 +225,73 @@ def tile_attend_gsq_wx_ts_kernel(tc, xT, wT, y, wt, ts, xm, offs, out_0, out_1):
             if b == B - 1:
                 nc.sync.dma_start(out=out_0[block(c), :], in_=windows[c][:])
 
-        xm_block(0, 0)
-        xm_block(0, 1)
-        turn_plane(0, 1, banks[3])
-        for t in (0, 1):
-            for cols in halves:
-                gather(1, t, cols)
-        interleave("V", w_grouped, w_listed[1], everything)
-        quantise(w_op[1], E4M3, w_grouped, everything)
-        table_gradient(0, 0)
-        x_grouped = (a_parts[:, 2:PACK, :, :].rearrange("p j t m -> p (j t m)").bitcast(BF16)
-                     .rearrange("p (c k) -> p c k", k=PACK))
-        for k in range(PACK):
-            interleave("S", x_grouped, x_raw[1], block(k))
+        for cols in halves:
+            interleave("S", xm_grouped, xm_raw[0], cols)
+            quantise(xm_op[0], E4M3, xm_grouped, cols)
+        for cols in halves:
+            interleave("S", x_grouped, x_raw[1], cols)
         quantise(x_op[1], E4M3, x_grouped, everything)
-        xm_block(0, 2)
-        table_gradient(0, 1)
+        turn_pairs(0, 1, banks[7])
+        table_gradient(0, 0, banks[6])
         for j in range(PACK):
-            target_part(1, j)
-        xm_block(0, 3)
-        table_gradient(0, 2)
+            y_part[j] = target_part(1, j, banks[4 + j % 2])
+            product(banks[j], w_op[1], E4M3, j, x_op[1], E4M3)
+            z_part[j] = residual(1, j, banks[j], y_part[j])
+        table_gradient(0, 1, banks[5])
+        table_gradient(0, 2, banks[5])
         for j in range(PACK):
-            score_part(1, j)
-        table_gradient(0, 3)
+            for t in range(PACK):
+                nc.tensor.transpose(banks[t][:, j, :], z_part[j][:, t, :], ident[:])
         h_rows = sbuf.tile([P, PACK, N], BF16, name="h_rows")
         for t in range(PACK):
-            bank = banks[4 + t % 2]
-            for j in range(PACK):
-                add_parts(bank[:, j, :], j, t)
-            nc.scalar.activation(out=h_rows[:, t, :], in_=flat(bank[:]), func=COPY, scale=wt_rows[:, 1, t:t + 1])
-        xm_block(1, 0)
-        interleave("S", h_grouped[1], h_rows, halves[0])
-        interleave("V", h_grouped[1], h_rows, halves[1])
+            nc.scalar.activation(out=h_rows[:, t, :], in_=flat(banks[t][:]), func=COPY, scale=wt_rows[:, 1, t:t + 1])
+        for cols in halves:
+            interleave("S", h_grouped[1], h_rows, cols)
         quantise(h_op[1], E5M2, h_grouped[1], everything)
-        xm_block(1, 1)
-        table_gradient(1, 0)
+        table_gradient(0, 3, banks[3])
+        for c in range(PACK):
+            stage = sbuf.tile([P, P, PACK], BF16, name="xm_stage", tag="y_part%d" % c, align_bytes=64)
+            move("S", stage[:], xm_raw[1][:, :, block(c)].rearrange("p t c -> p c t"))
+            nc.vector.quantize_mx(out=xm_op[1][0][:, block(c)].bitcast(E4M3), scales=xm_op[1][1][:, block(c)],
+                                  in_=flat(stage[:]))
+        table_gradient(1, 0, banks[6])
+        table_gradient(1, 1, banks[7])
 
         w_slot_op = [operand("w_i%d" % b) for b in range(B)]
         h_slot_op = [operand("h_i%d" % b) for b in range(B)]
         h_slots = [grouped_tile("h_slots%d" % b) for b in range(B)]
 
         def row_gradient(b):
-            gx = sbuf.tile([P, PACK, D], F32, name="gx%d" % b, tag="wide%d" % b)
+            gx = sbuf.tile([P, PACK, D], F32, name="gx%d" % b)
             for t in range(PACK):
-                bank = banks[6 + t % 2]
+                bank = banks[t]
                 product(bank, h_slot_op[b], E5M2, t, w_slot_op[b], E4M3)
-                nc.scalar.copy(out=gx[:, t, :].rearrange("p (m k) -> p m k", k=PACK),
-                               in_=bank[:].rearrange("p k m -> p m k"))
+                nc.scalar.copy(out=gx[:, t, :].rearrange("p (m u e) -> p m u e", u=2, e=2),
+                               in_=flat(bank[:]).rearrange("p (u m e) -> p m u e", u=2, e=2))
             nc.scalar.dma_start(out=out_1[b].rearrange("(p t) c -> p t c", t=PACK), in_=gx[:])
 
         h_words = flat(h_grouped[0][:]).bitcast(F32)
         for u in range(2):
             for s in range(PACK):
-                nc.tensor.transpose(banks[5 - u][:, s, :], h_words[:, 2 * s + u:2 * N:2 * PACK], ident[:])
+                nc.tensor.transpose(banks[4 + u][:, s, :], h_words[:, 2 * s + u:2 * N:2 * PACK], ident[:])
             nc.scalar.copy(
                 out=h_slots[0][:, u * HALF:(u + 1) * HALF, :].rearrange("p (e m) s -> p e m s", e=2),
-                in_=flat(banks[5 - u][:]).bitcast(BF16).rearrange("p (s m e) -> p e m s", s=PACK, e=2))
+                in_=flat(banks[4 + u][:]).bitcast(BF16).rearrange("p (s m e) -> p e m s", s=PACK, e=2))
         quantise(w_slot_op[0], E4M3, w_slots[0], everything)
         quantise(h_slot_op[0], E5M2, h_slots[0], everything)
-        xm_block(1, 2)
-        table_gradient(1, 1)
-        for t in (0, 1):
-            turn_plane(1, t, banks[6 + t])
+        turn_pairs(1, 1, banks[0])
+        quantise(w_slot_op[1], E4M3, w_slots[1], everything)
         h_slot_words = flat(h_slots[1][:]).bitcast(F32)
         for k in range(2):
             for t in range(2):
                 row_words = h_rows[:, 2 * k + t, :].bitcast(F32)
                 for u in range(2):
-                    nc.tensor.transpose(banks[k][:, 2 * t + u, :], row_words[:, u:HALF:2], ident[:])
+                    nc.tensor.transpose(banks[4 + k][:, 2 * t + u, :], row_words[:, u:HALF:2], ident[:])
             nc.scalar.copy(
                 out=h_slot_words[:, k * N:(k + 1) * N].rearrange("p (t m u) -> p t m u", t=2, u=2),
-                in_=banks[k][:].rearrange("p (t u) m -> p t m u", u=2))
-        quantise(w_slot_op[1], E4M3, w_slots[1], everything)
+                in_=banks[4 + k][:].rearrange("p (t u) m -> p t m u", u=2))
         quantise(h_slot_op[1], E5M2, h_slots[1], everything)
         row_gradient(0)
-        xm_block(1, 3)
-        table_gradient(1, 2)
+        table_gradient(1, 2, banks[6])
+        table_gradient(1, 3, banks[7])
         row_gradient(1)
-        table_gradient(1, 3)

@@ -1,26 +1,33 @@
 from contextlib import ExitStack
 
 import concourse.mybir as mybir
-from concourse.masks import make_identity
-
-B, N, T, D, R = 2, 512, 2048, 512, 512
-FLOPS = 3 * 2 * B * N * D * R
 
 F32 = mybir.dt.float32
 BF16 = mybir.dt.bfloat16
+I32 = mybir.dt.int32
 U32 = mybir.dt.uint32
 U16 = mybir.dt.uint16
 U8 = mybir.dt.uint8
 E4M3 = mybir.dt.float8_e4m3fn_x4
 E5M2 = mybir.dt.float8_e5m2_x4
+COPY = mybir.ActivationFunctionType.Copy
 MULT = mybir.AluOpType.mult
 ADD = mybir.AluOpType.add
-COPY = mybir.ActivationFunctionType.Copy
+IS_EQUAL = mybir.AluOpType.is_equal
 
 P = 128
 PACK = 4
-LIST_COLS = N // 16
-HALF = N // 2
+B = 2
+N = 512
+T = 2048
+BANKS = 8
+RAW_BUFS = 5
+OFFSET_ROWS = 16
+LIST_COLS = N // OFFSET_ROWS
+TS_COLS = T // P
+CHUNK = T // 2
+WHOLE = slice(0, N)
+HALVES = (slice(0, N // 2), slice(N // 2, N))
 
 
 def tile_attend_gsq_wx_ts_kernel(tc, xT, wT, y, wt, ts, xm, offs, out_0, out_1):
@@ -35,151 +42,129 @@ def tile_attend_gsq_wx_ts_kernel(tc, xT, wT, y, wt, ts, xm, offs, out_0, out_1):
         def block(k):
             return slice(k * P, (k + 1) * P)
 
-        def grouped_tile(name):
-            return sbuf.tile([P, N, PACK], BF16, name=name, tag=name, align_bytes=64)
+        def by_partition(rows):
+            return rows.rearrange("(p t) c -> p t c", t=PACK)
 
-        def move(engine, out, in_):
-            if engine == "V":
-                nc.vector.tensor_copy(out=out, in_=in_)
-            elif engine == "G":
-                nc.gpsimd.tensor_scalar(out=out, in0=in_, scalar1=1.0, scalar2=0.0, op0=MULT, op1=ADD)
-            else:
-                nc.scalar.copy(out=out, in_=in_)
+        def grouped_tile(name, tag=None):
+            return sbuf.tile([P, N, PACK], BF16, name=name, tag=tag or name, align_bytes=64)
 
-        def interleave(engine, grouped, rows, cols):
-            move(engine, grouped[:, cols, :], rows[:, :, cols].rearrange("p t c -> p c t"))
+        def scales_tile(name):
+            return sbuf.tile([P, N], U8, name=name + "_scales", align_bytes=64)
 
         def operand(name):
-            codes = sbuf.tile([P, N], U32, name=name + "_codes", align_bytes=64)
-            scales = sbuf.tile([P, N], U8, name=name + "_scales", align_bytes=64)
-            return codes, scales
+            return sbuf.tile([P, N], U32, name=name + "_codes", align_bytes=64), scales_tile(name)
+
+        def interleave(copy, grouped, rows, cols):
+            copy(out=grouped[:, cols, :], in_=rows[:, :, cols].rearrange("p t c -> p c t"))
 
         def quantise(op, fmt, grouped, cols):
             nc.vector.quantize_mx(out=op[0][:, cols].bitcast(fmt), scales=op[1][:, cols],
                                   in_=flat(grouped[:, cols, :]))
 
-        def product(out, still, still_fmt, k, moving, moving_fmt):
-            nc.tensor.matmul_mx(out=flat(out[:]),
+        def product(bank, still, still_fmt, k, moving, moving_fmt):
+            nc.tensor.matmul_mx(out=flat(bank[:]),
                                 lhsT=still[0][:, block(k)].bitcast(still_fmt), lhsT_scale=still[1][:, block(k)],
                                 rhs=moving[0][:].bitcast(moving_fmt), rhs_scale=moving[1][:],
                                 start=True, stop=True)
 
-        everything = slice(0, N)
-        halves = [slice(0, HALF), slice(HALF, N)]
+        on_vector = nc.vector.tensor_copy
+        on_scalar = nc.scalar.copy
 
         offsets = sbuf.tile([P, B * LIST_COLS], U16, name="offsets")
         nc.sync.dma_start(offsets[:], offs)
-        ts_window = sbuf.tile([P, T], F32, name="ts_window")
-        nc.vector.memset(ts_window[:], 0.0)
-        nc.scalar.dma_start(out=ts_window[0:1, :], in_=ts[0:1, :])
+        ts_cols = sbuf.tile([P, TS_COLS + P], F32, name="ts_cols")
+        nc.vector.memset(ts_cols[:, TS_COLS:], 0.0)
+        nc.sync.dma_start(out=ts_cols[:, 0:TS_COLS], in_=ts[0:1, :].rearrange("o (p c) -> (o p) c", p=P))
         wt_rows = sbuf.tile([P, B, PACK], F32, name="wt_rows")
         nc.sync.dma_start(out=wt_rows[:], in_=wt.rearrange("b (p t) o -> p b (t o)", t=PACK))
         ident = sbuf.tile([P, P], F32, name="ident")
-        make_identity(nc, ident[:])
+        ramp = sbuf.tile([P, P], I32, name="ramp")
+        nc.gpsimd.iota(ramp[:], pattern=[[1, P]], base=0, channel_multiplier=-1)
+        nc.vector.tensor_scalar(out=ident[:], in0=ramp[:], scalar1=0.0, scalar2=None, op0=IS_EQUAL)
+
+        def load_chunk(tile, u, k):
+            nc.sync.dma_start(out=tile[:], in_=by_partition(wT)[:, 2 * u:2 * u + 2, k * CHUNK:(k + 1) * CHUNK])
+            return tile
+
+        def ring_tile(shape, name):
+            return sbuf.tile(shape, F32, name=name, tag="raw", bufs=RAW_BUFS)
 
         def load(src, name):
-            raw = sbuf.tile([P, PACK, N], F32, name=name, tag="raw", bufs=4)
-            nc.sync.dma_start(out=raw[:], in_=src.rearrange("(p t) c -> p t c", t=PACK))
+            raw = ring_tile([P, PACK, N], name)
+            nc.sync.dma_start(out=raw[:], in_=by_partition(src))
             return raw
 
-        def load_chunk(u, k):
-            chunk = sbuf.tile([P, 2, T // 2], F32, name="chunk%d%d" % (u, k), tag="raw", bufs=4)
-            rows = wT.rearrange("(p t) c -> p t c", t=PACK)
-            nc.sync.dma_start(out=chunk[:], in_=rows[:, 2 * u:2 * u + 2, k * (T // 2):(k + 1) * (T // 2)])
-            return chunk
+        chunks = {(0, 0): load_chunk(sbuf.tile([P, 2, CHUNK], F32, name="first_chunk"), 0, 0)}
+        for u, k in ((0, 1), (1, 0), (1, 1)):
+            chunks[u, k] = load_chunk(ring_tile([P, 2, CHUNK], "chunk"), u, k)
+        y_raw = [load(y[0], "y_raw")]
+        x_raw = [load(xT[0], "x_raw")]
+        xm_raw = [load(xm[0], "xm_raw")]
+        x_raw.append(load(xT[1], "x_raw"))
+        y_raw.append(load(y[1], "y_raw"))
+        xm_raw.append(load(xm[1], "xm_raw"))
 
-        chunks, x_raw, y_raw, xm_raw = {}, {}, {}, {}
-        chunks[0, 0] = load_chunk(0, 0)
-        chunks[0, 1] = load_chunk(0, 1)
-        x_raw[0] = load(xT[0], "x_raw0")
-        chunks[1, 0] = load_chunk(1, 0)
-        chunks[1, 1] = load_chunk(1, 1)
-        y_raw[0] = load(y[0], "y_raw0")
-        xm_raw[0] = load(xm[0], "xm_raw0")
-        x_raw[1] = load(xT[1], "x_raw1")
-        y_raw[1] = load(y[1], "y_raw1")
-        xm_raw[1] = load(xm[1], "xm_raw1")
-
-        windows = []
-        for c in range(PACK):
-            window = sbuf.tile([P, T], F32, name="window%d" % c)
+        windows = [sbuf.tile([P, T], F32, name="window%d" % c) for c in range(PACK)]
+        for window in windows:
             nc.gpsimd.memset(window[:], 0.0)
-            windows.append(window)
 
-        banks = [psum.tile([P, PACK, P], F32, name="bank%d" % k) for k in range(8)]
+        ts_window = sbuf.tile([P, T], F32, name="ts_window")
+        for k in range(PACK):
+            ts_bank = psum.tile([P, PACK, P], F32, name="ts_bank", tag="bank%d" % k)
+            for c in range(PACK):
+                col = PACK * k + c
+                nc.tensor.transpose(ts_bank[:, c, :], ts_cols[:, col:col + P], ident[:])
+            on_vector(out=ts_window[:].rearrange("m (p c) -> m p c", p=P)[:, :, PACK * k:PACK * (k + 1)],
+                      in_=ts_bank[:].rearrange("m c p -> m p c"))
+        banks = [psum.tile([P, PACK, P], F32, name="bank%d" % k, tag="bank%d" % k) for k in range(BANKS)]
 
-        pairs = [sbuf.tile([P, T, 2], BF16, name="pairs%d" % u) for u in range(2)]
+        pairs = [sbuf.tile([P, T, 2], BF16, name="pairs%d" % u, align_bytes=64) for u in range(2)]
+        listed = [sbuf.tile([P, 2, N, 2], BF16, name="listed%d" % b, tag="listed%d" % b, align_bytes=64)
+                  for b in range(B)]
+        ts_listed = sbuf.tile([P, B * N], F32, name="ts_listed")
+        minus_ts = sbuf.tile([P, B, PACK], F32, name="minus_ts")
+        ts_squared = sbuf.tile([P, B, PACK], F32, name="ts_squared")
+        x_grouped = grouped_tile("x_grouped", tag="listed0")
+        w_grouped = grouped_tile("w_grouped")
+        xm_grouped = grouped_tile("xm_grouped")
+        w_slots = [grouped_tile("w_slots%d" % b) for b in range(B)]
+        h_grouped = [grouped_tile("h_grouped%d" % b) for b in range(B)]
+        h_slots = [grouped_tile("h_slots%d" % b) for b in range(B)]
+        h_rows = sbuf.tile([P, PACK, N], BF16, name="h_rows")
+        x_op = [operand("x%d" % b) for b in range(B)]
+        w_op = [operand("w_d%d" % b) for b in range(B)]
+        h_op = [operand("h_r%d" % b) for b in range(B)]
+        xm_op = [operand("xm%d" % b) for b in range(B)]
+        w_slot_op = [operand("w_i0")]
+        h_slot_op = [operand("h_i0")]
+        dw = [sbuf.tile([P, PACK, N], F32, name="dw%d" % b) for b in range(B)]
+        gx = [sbuf.tile([P, PACK, N], F32, name="gx%d" % b) for b in range(B)]
 
-        def cast_chunk(engine, u, k, first, last):
-            out = pairs[u][:, k * (T // 2) + first:k * (T // 2) + last, :]
-            in_ = chunks[u, k][:, :, first:last].rearrange("p e c -> p c e")
-            if engine == "V":
-                nc.vector.tensor_copy(out=out, in_=in_)
-            else:
-                nc.scalar.activation(out=out, in_=in_, func=COPY)
-
-        listed = [sbuf.tile([P, 2, N, 2], BF16, name="listed%d" % b) for b in range(B)]
+        def cast_pairs(u):
+            for k in range(T // CHUNK):
+                nc.scalar.activation(out=pairs[u][:, k * CHUNK:(k + 1) * CHUNK, :],
+                                     in_=chunks[u, k][:].rearrange("p e c -> p c e"), func=COPY)
 
         def gather(b, u, cols):
-            first = (b * N + cols.start) // 16
-            last = (b * N + cols.stop) // 16
+            first, last = (b * N + cols.start) // OFFSET_ROWS, (b * N + cols.stop) // OFFSET_ROWS
             nc.vector.tensor_copy(flat(listed[b][:, u, cols, :]).bitcast(U32),
                                   flat(pairs[u][:]).bitcast(U32).indirect(offsets[:, first:last]))
 
         def join_pairs(b, cols):
-            nc.vector.tensor_copy(out=w_grouped[:, cols, :].rearrange("p c (u e) -> p c u e", u=2),
-                                  in_=listed[b][:, :, cols, :].rearrange("p u c e -> p c u e"))
-
-        w_slots = [grouped_tile("w_slots%d" % b) for b in range(B)]
+            on_vector(out=w_grouped[:, cols, :].rearrange("p c (u e) -> p c u e", u=2),
+                      in_=listed[b][:, :, cols, :].rearrange("p u c e -> p c u e"))
 
         def turn_pairs(b, u, bank):
             words = flat(listed[b][:, u, :, :]).bitcast(F32)
             for s in range(PACK):
                 nc.tensor.transpose(bank[:, s, :], words[:, s:N:PACK], ident[:])
-            nc.scalar.copy(out=w_slots[b][:, halves[u], :].rearrange("p (m e) s -> p m e s", e=2),
-                           in_=flat(bank[:]).bitcast(BF16).rearrange("p (s m e) -> p m e s", s=PACK, e=2))
-
-        ts_listed = sbuf.tile([P, B * N], F32, name="ts_listed")
-        nc.vector.tensor_copy(ts_listed[:], ts_window[:].indirect(offsets[:]))
-        cast_chunk("V", 0, 0, 0, T // 2)
-        cast_chunk("S", 0, 1, 0, T // 2)
-        x_grouped = grouped_tile("x_grouped")
-        x_op = [operand("x%d" % b) for b in range(B)]
-        interleave("S", x_grouped, x_raw[0], everything)
-        for b in range(B):
-            gather(b, 0, everything)
-        cast_chunk("S", 1, 0, 0, T // 2)
-        quantise(x_op[0], E4M3, x_grouped, everything)
-        cast_chunk("S", 1, 1, 0, 384)
-        cast_chunk("V", 1, 1, 384, T // 2)
-
-        minus_ts = sbuf.tile([P, B, PACK], F32, name="minus_ts")
-        ts_squared = sbuf.tile([P, B, PACK], F32, name="ts_squared")
-        for b in range(B):
-            for j in range(PACK):
-                nc.tensor.transpose(banks[b][:, j, :], ts_listed[:, b * N + j * P:b * N + (j + 1) * P], ident[:])
-            nc.scalar.activation(out=minus_ts[:, b, :], in_=banks[b][:, :, 0], func=COPY, scale=-1.0)
-        nc.gpsimd.tensor_tensor(out=ts_squared[:], in0=minus_ts[:], in1=minus_ts[:], op=MULT)
-
-        w_grouped = grouped_tile("w_grouped")
-        w_op = [operand("w_d%d" % b) for b in range(B)]
-        for cols in halves:
-            gather(0, 1, cols)
-        for cols in halves:
-            join_pairs(0, cols)
-        for cols in halves:
-            quantise(w_op[0], E4M3, w_grouped, cols)
-        gather(1, 1, everything)
-        join_pairs(1, everything)
-        quantise(w_op[1], E4M3, w_grouped, everything)
-
-        for b in range(B):
-            turn_pairs(b, 0, banks[2 + b])
+            on_scalar(out=w_slots[b][:, HALVES[u], :].rearrange("p (m e) s -> p m e s", e=2),
+                      in_=flat(bank[:]).bitcast(BF16).rearrange("p (s m e) -> p m e s", s=PACK, e=2))
 
         def part(name, j):
             return sbuf.tile([P, PACK, P], F32, name=name, tag="%s%d" % (name, j), align_bytes=64)
 
-        def by_row_slot(bank):
+        def by_row(bank):
             return flat(bank[:]).rearrange("p (m t) -> p t m", t=PACK)
 
         def target_part(b, j, bank):
@@ -189,109 +174,138 @@ def tile_attend_gsq_wx_ts_kernel(tc, xT, wT, y, wt, ts, xm, offs, out_0, out_1):
             nc.scalar.activation(out=out[:], in_=bank[:], func=COPY, scale=minus_ts[:, b, j:j + 1])
             return out
 
-        def residual(b, j, scores, targets):
-            out = part("z_part", j)
-            nc.vector.scalar_tensor_tensor(out=out[:], in0=by_row_slot(scores), scalar=ts_squared[:, b, j:j + 1],
-                                           in1=targets[:], op0=MULT, op1=ADD)
-            return out
-
-        h_grouped = [grouped_tile("h_grouped%d" % b) for b in range(B)]
-        h_op = [operand("h_r%d" % b) for b in range(B)]
-        y_part = [target_part(0, j, banks[4 + j]) for j in range(PACK)]
-        for j in range(PACK):
-            product(banks[j], w_op[0], E4M3, j, x_op[0], E4M3)
-        z_part = {}
-        for j in range(PACK + 2):
-            if j < PACK:
-                z_part[j] = residual(0, j, banks[j], y_part[j])
-                for t in range(PACK):
-                    nc.tensor.transpose(banks[4 + j % 2][:, t, :], z_part[j][:, t, :], ident[:])
-            if 1 <= j <= PACK:
-                nc.vector.tensor_tensor(out=h_grouped[0][:, block(j - 1), :],
-                                        in0=banks[4 + (j - 1) % 2][:].rearrange("p t i -> p i t"),
-                                        in1=wt_rows[:, 0:1, :].to_broadcast([P, P, PACK]), op=MULT)
-            if j >= 2:
-                quantise(h_op[0], E5M2, h_grouped[0], block(j - 2))
-
-        xm_grouped = grouped_tile("xm_grouped")
-        xm_op = [operand("xm%d" % b) for b in range(B)]
-        dw = [sbuf.tile([P, PACK, N], F32, name="dw%d" % b) for b in range(B)]
+        def scores(b, j, bank):
+            product(bank, w_op[b], E4M3, j, x_op[b], E4M3)
 
         def table_gradient(b, c, bank):
             product(bank, xm_op[b], E4M3, c, h_op[b], E5M2)
-            nc.scalar.copy(out=dw[b][:, c, :], in_=flat(bank[:]))
+            on_scalar(out=dw[b][:, c, :], in_=flat(bank[:]))
             nc.vector.tensor_copy(windows[c][:].indirect(offsets[:, b * LIST_COLS:(b + 1) * LIST_COLS]),
                                   dw[b][:, c, :])
             if b == B - 1:
                 nc.sync.dma_start(out=out_0[block(c), :], in_=windows[c][:])
 
-        for cols in halves:
-            interleave("S", xm_grouped, xm_raw[0], cols)
-            quantise(xm_op[0], E4M3, xm_grouped, cols)
-        for cols in halves:
-            interleave("S", x_grouped, x_raw[1], cols)
-        quantise(x_op[1], E4M3, x_grouped, everything)
-        turn_pairs(0, 1, banks[7])
-        table_gradient(0, 0, banks[6])
-        for j in range(PACK):
-            y_part[j] = target_part(1, j, banks[4 + j % 2])
-            product(banks[j], w_op[1], E4M3, j, x_op[1], E4M3)
-            z_part[j] = residual(1, j, banks[j], y_part[j])
-        table_gradient(0, 1, banks[5])
-        table_gradient(0, 2, banks[5])
-        for j in range(PACK):
-            for t in range(PACK):
-                nc.tensor.transpose(banks[t][:, j, :], z_part[j][:, t, :], ident[:])
-        h_rows = sbuf.tile([P, PACK, N], BF16, name="h_rows")
-        for t in range(PACK):
-            nc.scalar.activation(out=h_rows[:, t, :], in_=flat(banks[t][:]), func=COPY, scale=wt_rows[:, 1, t:t + 1])
-        for cols in halves:
-            interleave("S", h_grouped[1], h_rows, cols)
-        quantise(h_op[1], E5M2, h_grouped[1], everything)
-        table_gradient(0, 3, banks[3])
-        for c in range(PACK):
-            stage = sbuf.tile([P, P, PACK], BF16, name="xm_stage", tag="y_part%d" % c, align_bytes=64)
-            move("S", stage[:], xm_raw[1][:, :, block(c)].rearrange("p t c -> p c t"))
-            nc.vector.quantize_mx(out=xm_op[1][0][:, block(c)].bitcast(E4M3), scales=xm_op[1][1][:, block(c)],
-                                  in_=flat(stage[:]))
-        table_gradient(1, 0, banks[6])
-        table_gradient(1, 1, banks[7])
-
-        w_slot_op = [operand("w_i%d" % b) for b in range(B)]
-        h_slot_op = [operand("h_i%d" % b) for b in range(B)]
-        h_slots = [grouped_tile("h_slots%d" % b) for b in range(B)]
-
-        def row_gradient(b):
-            gx = sbuf.tile([P, PACK, D], F32, name="gx%d" % b)
-            for t in range(PACK):
-                bank = banks[t]
+        def row_gradient(b, half, bank_pair):
+            rows = slice(2 * half, 2 * half + 2)
+            for t, bank in zip(range(rows.start, rows.stop), bank_pair):
                 product(bank, h_slot_op[b], E5M2, t, w_slot_op[b], E4M3)
-                nc.scalar.copy(out=gx[:, t, :].rearrange("p (m u e) -> p m u e", u=2, e=2),
-                               in_=flat(bank[:]).rearrange("p (u m e) -> p m u e", u=2, e=2))
-            nc.scalar.dma_start(out=out_1[b].rearrange("(p t) c -> p t c", t=PACK), in_=gx[:])
+                on_scalar(out=gx[b][:, t, :].rearrange("p (m u e) -> p m u e", u=2, e=2),
+                          in_=flat(bank[:]).rearrange("p (u m e) -> p m u e", u=2, e=2))
+            nc.scalar.dma_start(out=by_partition(out_1[b])[:, rows, :], in_=gx[b][:, rows, :])
 
+        nc.vector.tensor_copy(ts_listed[:], ts_window[:].indirect(offsets[:]))
+        cast_pairs(0)
+        for b in range(B):
+            gather(b, 0, WHOLE)
+        cast_pairs(1)
+        for b in range(B):
+            for j in range(PACK):
+                nc.tensor.transpose(banks[b][:, j, :], ts_listed[:, b * N + j * P:b * N + (j + 1) * P], ident[:])
+            nc.scalar.activation(out=minus_ts[:, b, :], in_=banks[b][:, :, 0], func=COPY, scale=-1.0)
+        nc.gpsimd.tensor_tensor(out=ts_squared[:], in0=minus_ts[:], in1=minus_ts[:], op=MULT)
+        for b in range(B):
+            turn_pairs(b, 0, banks[2 + b])
+        for cols in HALVES:
+            gather(0, 1, cols)
+        for cols in HALVES:
+            join_pairs(0, cols)
+        for cols in HALVES:
+            quantise(w_op[0], E4M3, w_grouped, cols)
+        turn_pairs(0, 1, banks[4])
+        for cols in HALVES:
+            interleave(on_vector, x_grouped, x_raw[0], cols)
+        quantise(x_op[0], E4M3, x_grouped, WHOLE)
+        for cols in HALVES:
+            gather(1, 1, cols)
+        for cols in HALVES:
+            join_pairs(1, cols)
+        for cols in HALVES:
+            quantise(w_op[1], E4M3, w_grouped, cols)
+
+        y_part = [target_part(0, j, banks[j]) for j in range(PACK)]
+        for j in range(PACK):
+            scores(0, j, banks[PACK + j])
+        turned = [banks[(j + 1) % PACK] for j in range(PACK)]
+        for j in range(PACK):
+            residual = part("a_part", j)
+            nc.vector.scalar_tensor_tensor(out=residual[:], in0=by_row(banks[PACK + j]),
+                                           scalar=ts_squared[:, 0, j:j + 1], in1=y_part[j][:], op0=MULT, op1=ADD)
+            for t in range(PACK):
+                nc.tensor.transpose(turned[j][:, t, :], residual[:, t, :], ident[:])
+        for j in range(PACK + 1):
+            if j < PACK:
+                nc.vector.tensor_tensor(out=h_grouped[0][:, block(j), :],
+                                        in0=turned[j][:].rearrange("p t i -> p i t"),
+                                        in1=wt_rows[:, 0:1, :].to_broadcast([P, P, PACK]), op=MULT)
+            if j > 0:
+                quantise(h_op[0], E5M2, h_grouped[0], block(j - 1))
+        interleave(on_scalar, xm_grouped, xm_raw[0], HALVES[0])
+        quantise(xm_op[0], E4M3, xm_grouped, HALVES[0])
+        interleave(on_scalar, xm_grouped, xm_raw[0], HALVES[1])
+        for cols in HALVES:
+            interleave(on_scalar, x_grouped, x_raw[1], cols)
+        table_gradient(0, 0, banks[4])
+        quantise(x_op[1], E4M3, x_grouped, WHOLE)
+        quantise(xm_op[0], E4M3, xm_grouped, HALVES[1])
+        table_gradient(0, 1, banks[7])
+
+        a_part = []
+
+        def score_part(j, bank):
+            scores(1, j, bank)
+            a_part.append(part("a_part", j))
+            nc.scalar.activation(out=a_part[j][:], in_=by_row(bank), func=COPY, scale=ts_squared[:, 1, j:j + 1])
+
+        y_part = [target_part(1, 0, banks[3]), target_part(1, 1, banks[0])]
+        score_part(0, banks[5])
+        score_part(1, banks[6])
+        y_part.append(target_part(1, 2, banks[4]))
+        for c in range(PACK):
+            interleave(on_scalar, x_grouped, xm_raw[1], block(c))
+            quantise(xm_op[1], E4M3, x_grouped, block(c))
+        y_part.append(target_part(1, 3, banks[5]))
+        table_gradient(0, 2, banks[1])
+        score_part(2, banks[3])
+        score_part(3, banks[0])
         h_words = flat(h_grouped[0][:]).bitcast(F32)
-        for u in range(2):
+        for u, bank in enumerate((banks[6], banks[7])):
             for s in range(PACK):
-                nc.tensor.transpose(banks[4 + u][:, s, :], h_words[:, 2 * s + u:2 * N:2 * PACK], ident[:])
-            nc.scalar.copy(
-                out=h_slots[0][:, u * HALF:(u + 1) * HALF, :].rearrange("p (e m) s -> p e m s", e=2),
-                in_=flat(banks[4 + u][:]).bitcast(BF16).rearrange("p (s m e) -> p e m s", s=PACK, e=2))
-        quantise(w_slot_op[0], E4M3, w_slots[0], everything)
-        quantise(h_slot_op[0], E5M2, h_slots[0], everything)
-        turn_pairs(1, 1, banks[0])
-        quantise(w_slot_op[1], E4M3, w_slots[1], everything)
-        h_slot_words = flat(h_slots[1][:]).bitcast(F32)
-        for k in range(2):
+                nc.tensor.transpose(bank[:, s, :], h_words[:, 2 * s + u:2 * N:2 * PACK], ident[:])
+            on_scalar(out=h_slots[0][:, HALVES[u], :].rearrange("p (e m) s -> p e m s", e=2),
+                      in_=flat(bank[:]).bitcast(BF16).rearrange("p (s m e) -> p e m s", s=PACK, e=2))
+        quantise(w_slot_op[0], E4M3, w_slots[0], WHOLE)
+        quantise(h_slot_op[0], E5M2, h_slots[0], WHOLE)
+        table_gradient(0, 3, banks[2])
+        for t, bank in enumerate((banks[4], banks[5], banks[3], banks[0])):
+            for j in range(PACK):
+                nc.tensor.matmul(bank[:, j, :], lhsT=y_part[j][:, t, :], rhs=ident[:], start=True, stop=False,
+                                 is_transpose=True)
+                nc.tensor.matmul(bank[:, j, :], lhsT=a_part[j][:, t, :], rhs=ident[:], start=False, stop=True,
+                                 is_transpose=True)
+            nc.scalar.activation(out=h_rows[:, t, :], in_=flat(bank[:]), func=COPY, scale=wt_rows[:, 1, t:t + 1])
+        interleave(on_scalar, h_grouped[1], h_rows, HALVES[0])
+        interleave(on_vector, h_grouped[1], h_rows, HALVES[1])
+        quantise(h_op[1], E5M2, h_grouped[1], WHOLE)
+
+        late_codes = sbuf.tile([P, 2, N], U32, name="late_codes", tag="h_grouped1", align_bytes=64)
+        w_slot_op.append((late_codes[:, 0, :], scales_tile("w_i1")))
+        h_slot_op.append((late_codes[:, 1, :], scales_tile("h_i1")))
+        table_gradient(1, 0, banks[6])
+        turn_pairs(1, 1, banks[4])
+        for half, bank in enumerate((banks[5], banks[3])):
             for t in range(2):
-                row_words = h_rows[:, 2 * k + t, :].bitcast(F32)
+                words = h_rows[:, 2 * half + t, :].bitcast(F32)
                 for u in range(2):
-                    nc.tensor.transpose(banks[4 + k][:, 2 * t + u, :], row_words[:, u:HALF:2], ident[:])
-            nc.scalar.copy(
-                out=h_slot_words[:, k * N:(k + 1) * N].rearrange("p (t m u) -> p t m u", t=2, u=2),
-                in_=banks[4 + k][:].rearrange("p (t u) m -> p t m u", u=2))
-        quantise(h_slot_op[1], E5M2, h_slots[1], everything)
-        row_gradient(0)
-        table_gradient(1, 2, banks[6])
-        table_gradient(1, 3, banks[7])
-        row_gradient(1)
+                    nc.tensor.transpose(bank[:, 2 * t + u, :], words[:, u:N // 2:2], ident[:])
+            out_words = flat(h_slots[1][:, HALVES[half], :]).bitcast(F32)
+            on_scalar(out=out_words.rearrange("p (t m u) -> p t m u", t=2, u=2),
+                      in_=bank[:].rearrange("p (t u) m -> p t m u", u=2))
+        quantise(w_slot_op[1], E4M3, w_slots[1], WHOLE)
+        quantise(h_slot_op[1], E5M2, h_slots[1], WHOLE)
+        table_gradient(1, 1, banks[7])
+        row_gradient(0, 0, (banks[0], banks[1]))
+        row_gradient(0, 1, (banks[2], banks[6]))
+        table_gradient(1, 2, banks[4])
+        table_gradient(1, 3, banks[5])
+        row_gradient(1, 0, (banks[3], banks[7]))
+        row_gradient(1, 1, (banks[0], banks[1]))

@@ -1,6 +1,7 @@
 from contextlib import ExitStack
 
 import concourse.mybir as mybir
+from concourse.masks import make_identity
 
 F32 = mybir.dt.float32
 BF16 = mybir.dt.bfloat16
@@ -13,7 +14,6 @@ E5M2 = mybir.dt.float8_e5m2_x4
 COPY = mybir.ActivationFunctionType.Copy
 MULT = mybir.AluOpType.mult
 ADD = mybir.AluOpType.add
-IS_EQUAL = mybir.AluOpType.is_equal
 
 P = 128
 PACK = 4
@@ -21,11 +21,10 @@ B = 2
 N = 512
 T = 2048
 BANKS = 8
-RAW_BUFS = 5
 OFFSET_ROWS = 16
 LIST_COLS = N // OFFSET_ROWS
 TS_COLS = T // P
-CHUNK = T // 2
+CHUNK = T // 4
 WHOLE = slice(0, N)
 HALVES = (slice(0, N // 2), slice(N // 2, N))
 
@@ -48,11 +47,12 @@ def tile_attend_gsq_wx_ts_kernel(tc, xT, wT, y, wt, ts, xm, offs, out_0, out_1):
         def grouped_tile(name, tag=None):
             return sbuf.tile([P, N, PACK], BF16, name=name, tag=tag or name, align_bytes=64)
 
-        def scales_tile(name):
-            return sbuf.tile([P, N], U8, name=name + "_scales", align_bytes=64)
+        def scales_tile(name, width):
+            return sbuf.tile([P, width], U8, name=name + "_scales", align_bytes=64)
 
-        def operand(name):
-            return sbuf.tile([P, N], U32, name=name + "_codes", align_bytes=64), scales_tile(name)
+        def operand(name, width=N):
+            codes = sbuf.tile([P, width], U32, name=name + "_codes", tag=name + "_codes", align_bytes=64)
+            return codes, scales_tile(name, width)
 
         def interleave(copy, grouped, rows, cols):
             copy(out=grouped[:, cols, :], in_=rows[:, :, cols].rearrange("p t c -> p c t"))
@@ -70,45 +70,42 @@ def tile_attend_gsq_wx_ts_kernel(tc, xT, wT, y, wt, ts, xm, offs, out_0, out_1):
         on_vector = nc.vector.tensor_copy
         on_scalar = nc.scalar.copy
 
-        offsets = sbuf.tile([P, B * LIST_COLS], U16, name="offsets")
-        nc.sync.dma_start(offsets[:], offs)
         ts_cols = sbuf.tile([P, TS_COLS + P], F32, name="ts_cols")
-        nc.vector.memset(ts_cols[:, TS_COLS:], 0.0)
+        nc.gpsimd.memset(ts_cols[:, TS_COLS:], 0.0)
         nc.sync.dma_start(out=ts_cols[:, 0:TS_COLS], in_=ts[0:1, :].rearrange("o (p c) -> (o p) c", p=P))
-        wt_rows = sbuf.tile([P, B, PACK], F32, name="wt_rows")
-        nc.sync.dma_start(out=wt_rows[:], in_=wt.rearrange("b (p t) o -> p b (t o)", t=PACK))
         ident = sbuf.tile([P, P], F32, name="ident")
-        ramp = sbuf.tile([P, P], I32, name="ramp")
-        nc.gpsimd.iota(ramp[:], pattern=[[1, P]], base=0, channel_multiplier=-1)
-        nc.vector.tensor_scalar(out=ident[:], in0=ramp[:], scalar1=0.0, scalar2=None, op0=IS_EQUAL)
+        make_identity(nc, ident[:])
 
-        def load_chunk(tile, u, k):
+        def load_chunk(u, k):
+            tile = sbuf.tile([P, 2, CHUNK], F32, name="chunk%d%d" % (u, k), tag="chunk%d%d" % (u, k))
             nc.sync.dma_start(out=tile[:], in_=by_partition(wT)[:, 2 * u:2 * u + 2, k * CHUNK:(k + 1) * CHUNK])
             return tile
 
-        def ring_tile(shape, name):
-            return sbuf.tile(shape, F32, name=name, tag="raw", bufs=RAW_BUFS)
-
         def load(src, name):
-            raw = ring_tile([P, PACK, N], name)
+            raw = sbuf.tile([P, PACK, N], F32, name=name, tag=name, align_bytes=64)
             nc.sync.dma_start(out=raw[:], in_=by_partition(src))
             return raw
 
-        chunks = {(0, 0): load_chunk(sbuf.tile([P, 2, CHUNK], F32, name="first_chunk"), 0, 0)}
-        for u, k in ((0, 1), (1, 0), (1, 1)):
-            chunks[u, k] = load_chunk(ring_tile([P, 2, CHUNK], "chunk"), u, k)
-        y_raw = [load(y[0], "y_raw")]
-        x_raw = [load(xT[0], "x_raw")]
-        xm_raw = [load(xm[0], "xm_raw")]
-        x_raw.append(load(xT[1], "x_raw"))
-        y_raw.append(load(y[1], "y_raw"))
-        xm_raw.append(load(xm[1], "xm_raw"))
+        chunks = {(0, 0): load_chunk(0, 0)}
+        offsets = sbuf.tile([P, B * LIST_COLS], U16, name="offsets")
+        nc.sync.dma_start(offsets[:], offs)
+        for u in range(2):
+            for k in range(T // CHUNK):
+                if (u, k) not in chunks:
+                    chunks[u, k] = load_chunk(u, k)
+        x_raw = [load(xT[0], "x_raw0")]
+        wt_rows = sbuf.tile([P, B, PACK], F32, name="wt_rows")
+        nc.sync.dma_start(out=wt_rows[:], in_=wt.rearrange("b (p t) o -> p b (t o)", t=PACK))
+        y_raw = [sbuf.tile([P, PACK, N], F32, name="y_raw0", tag="y_raw0", align_bytes=64)]
+        for half in range(2):
+            rows = slice(2 * half, 2 * half + 2)
+            nc.sync.dma_start(out=y_raw[0][:, rows, :], in_=by_partition(y[0])[:, rows, :])
+        xm_raw = [load(xm[0], "xm_raw0")]
+        x_raw.append(load(xT[1], "x_raw1"))
+        y_raw.append(load(y[1], "y_raw1"))
+        xm_raw.append(load(xm[1], "xm_raw1"))
 
-        windows = [sbuf.tile([P, T], F32, name="window%d" % c) for c in range(PACK)]
-        for window in windows:
-            nc.gpsimd.memset(window[:], 0.0)
-
-        ts_window = sbuf.tile([P, T], F32, name="ts_window")
+        ts_window = sbuf.tile([P, T], F32, name="ts_window", tag="ts_window", align_bytes=64)
         for k in range(PACK):
             ts_bank = psum.tile([P, PACK, P], F32, name="ts_bank", tag="bank%d" % k)
             for c in range(PACK):
@@ -118,58 +115,84 @@ def tile_attend_gsq_wx_ts_kernel(tc, xT, wT, y, wt, ts, xm, offs, out_0, out_1):
                       in_=ts_bank[:].rearrange("m c p -> m p c"))
         banks = [psum.tile([P, PACK, P], F32, name="bank%d" % k, tag="bank%d" % k) for k in range(BANKS)]
 
-        pairs = [sbuf.tile([P, T, 2], BF16, name="pairs%d" % u, align_bytes=64) for u in range(2)]
-        listed = [sbuf.tile([P, 2, N, 2], BF16, name="listed%d" % b, tag="listed%d" % b, align_bytes=64)
-                  for b in range(B)]
+        windows = [sbuf.tile([P, T], F32, name="window%d" % c) for c in range(PACK)]
+        for window in windows:
+            nc.vector.memset(window[:].bitcast(I32), 0)
+
+        pairs = [sbuf.tile([P, T, 2], BF16, name="pairs%d" % u, tag="pairs%d" % u, align_bytes=64) for u in range(2)]
+        listed = sbuf.tile([P, 3, N], U32, name="listed", align_bytes=64)
+        listed_row = {(0, 0): 0, (0, 1): 1, (1, 0): 2, (1, 1): 1}
         ts_listed = sbuf.tile([P, B * N], F32, name="ts_listed")
         minus_ts = sbuf.tile([P, B, PACK], F32, name="minus_ts")
         ts_squared = sbuf.tile([P, B, PACK], F32, name="ts_squared")
-        x_grouped = grouped_tile("x_grouped", tag="listed0")
-        w_grouped = grouped_tile("w_grouped")
-        xm_grouped = grouped_tile("xm_grouped")
+        w_grouped = [grouped_tile("w_grouped0")]
         w_slots = [grouped_tile("w_slots%d" % b) for b in range(B)]
         h_grouped = [grouped_tile("h_grouped%d" % b) for b in range(B)]
-        h_slots = [grouped_tile("h_slots%d" % b) for b in range(B)]
-        h_rows = sbuf.tile([P, PACK, N], BF16, name="h_rows")
         x_op = [operand("x%d" % b) for b in range(B)]
         w_op = [operand("w_d%d" % b) for b in range(B)]
         h_op = [operand("h_r%d" % b) for b in range(B)]
-        xm_op = [operand("xm%d" % b) for b in range(B)]
-        w_slot_op = [operand("w_i0")]
-        h_slot_op = [operand("h_i0")]
-        dw = [sbuf.tile([P, PACK, N], F32, name="dw%d" % b) for b in range(B)]
-        gx = [sbuf.tile([P, PACK, N], F32, name="gx%d" % b) for b in range(B)]
+        xm_op = [[operand("xm%d%d" % (b, half), N // 2) for half in range(2)] for b in range(B)]
+        w_slot_op = [None, operand("w_i1")]
+        h_slot_op = [operand("h_i%d" % b) for b in range(B)]
 
-        def cast_pairs(u):
-            for k in range(T // CHUNK):
-                nc.scalar.activation(out=pairs[u][:, k * CHUNK:(k + 1) * CHUNK, :],
-                                     in_=chunks[u, k][:].rearrange("p e c -> p c e"), func=COPY)
+        def cast_pairs(copy, u, k, first, last):
+            copy(out=pairs[u][:, k * CHUNK + first:k * CHUNK + last, :],
+                 in_=chunks[u, k][:, :, first:last].rearrange("p e c -> p c e"))
 
-        def gather(b, u, cols):
-            first, last = (b * N + cols.start) // OFFSET_ROWS, (b * N + cols.stop) // OFFSET_ROWS
-            nc.vector.tensor_copy(flat(listed[b][:, u, cols, :]).bitcast(U32),
-                                  flat(pairs[u][:]).bitcast(U32).indirect(offsets[:, first:last]))
+        def activation_copy(out, in_):
+            nc.scalar.activation(out=out, in_=in_, func=COPY)
 
-        def join_pairs(b, cols):
-            on_vector(out=w_grouped[:, cols, :].rearrange("p c (u e) -> p c u e", u=2),
-                      in_=listed[b][:, :, cols, :].rearrange("p u c e -> p c u e"))
+        def gather(b, u):
+            nc.vector.tensor_copy(listed[:, listed_row[b, u], :],
+                                  flat(pairs[u][:]).bitcast(U32).indirect(offsets[:, b * LIST_COLS:(b + 1) * LIST_COLS]))
 
-        def turn_pairs(b, u, bank):
-            words = flat(listed[b][:, u, :, :]).bitcast(F32)
+        def join_pairs(b):
+            rows = listed[:, 0:2, :] if b == 0 else listed[:, 2:0:-1, :]
+            on_vector(out=flat(w_grouped[b][:]).bitcast(I32).rearrange("p (c u) -> p c u", u=2),
+                      in_=rows.bitcast(I32).rearrange("p u c -> p c u"))
+
+        def turn_words(words, bank):
             for s in range(PACK):
-                nc.tensor.transpose(bank[:, s, :], words[:, s:N:PACK], ident[:])
+                nc.tensor.transpose(bank[:, s, :], words[s], ident[:])
+
+        def turn_pairs(b, u, bank, early=False):
+            if early:
+                words = listed[:, listed_row[b, u], :].bitcast(F32)
+                turn_words([words[:, s:N:PACK] for s in range(PACK)], bank)
+            else:
+                words = flat(w_grouped[b][:]).bitcast(F32)
+                turn_words([words[:, 2 * s + u:2 * N:2 * PACK] for s in range(PACK)], bank)
             on_scalar(out=w_slots[b][:, HALVES[u], :].rearrange("p (m e) s -> p m e s", e=2),
                       in_=flat(bank[:]).bitcast(BF16).rearrange("p (s m e) -> p m e s", s=PACK, e=2))
 
-        def part(name, j):
-            return sbuf.tile([P, PACK, P], F32, name=name, tag="%s%d" % (name, j), align_bytes=64)
+        def half_stage(tag):
+            return sbuf.tile([P, N // 2, PACK], BF16, name="stage", tag=tag, align_bytes=64)
+
+        def stage_half(copy, stage, raw, half):
+            copy(out=stage, in_=raw[:, :, HALVES[half]].rearrange("p t c -> p c t"))
+
+        def quantise_half(op, stage, half):
+            nc.vector.quantize_mx(out=op[0][:, HALVES[half]].bitcast(E4M3), scales=op[1][:, HALVES[half]],
+                                  in_=flat(stage))
+
+        def quantise_rows(b, half, stage):
+            quantise(xm_op[b][half], E4M3, stage, slice(0, N // 2))
+
+        def table_gradient(b, c, bank):
+            product(bank, xm_op[b][c // 2], E4M3, c % 2, h_op[b], E5M2)
+
+        def part(name, j, tag=None):
+            return sbuf.tile([P, PACK, P], F32, name=name, tag=tag or "%s%d" % (name, j), align_bytes=64)
 
         def by_row(bank):
             return flat(bank[:]).rearrange("p (m t) -> p t m", t=PACK)
 
-        def target_part(b, j, bank):
-            for t in range(PACK):
+        def turn_target(b, j, bank, rows):
+            for t in rows:
                 nc.tensor.transpose(bank[:, t, :], y_raw[b][:, t, block(j)], ident[:])
+
+        def target_part(b, j, bank, rows=range(PACK)):
+            turn_target(b, j, bank, rows)
             out = part("y_part", j)
             nc.scalar.activation(out=out[:], in_=bank[:], func=COPY, scale=minus_ts[:, b, j:j + 1])
             return out
@@ -177,11 +200,11 @@ def tile_attend_gsq_wx_ts_kernel(tc, xT, wT, y, wt, ts, xm, offs, out_0, out_1):
         def scores(b, j, bank):
             product(bank, w_op[b], E4M3, j, x_op[b], E4M3)
 
-        def table_gradient(b, c, bank):
-            product(bank, xm_op[b], E4M3, c, h_op[b], E5M2)
-            on_scalar(out=dw[b][:, c, :], in_=flat(bank[:]))
+        def scatter(b, c, bank):
+            staged = dw[b][c // 2][:, c % 2, :]
+            on_scalar(out=staged, in_=flat(bank[:]))
             nc.vector.tensor_copy(windows[c][:].indirect(offsets[:, b * LIST_COLS:(b + 1) * LIST_COLS]),
-                                  dw[b][:, c, :])
+                                  staged)
             if b == B - 1:
                 nc.sync.dma_start(out=out_0[block(c), :], in_=windows[c][:])
 
@@ -189,110 +212,112 @@ def tile_attend_gsq_wx_ts_kernel(tc, xT, wT, y, wt, ts, xm, offs, out_0, out_1):
             rows = slice(2 * half, 2 * half + 2)
             for t, bank in zip(range(rows.start, rows.stop), bank_pair):
                 product(bank, h_slot_op[b], E5M2, t, w_slot_op[b], E4M3)
-                on_scalar(out=gx[b][:, t, :].rearrange("p (m u e) -> p m u e", u=2, e=2),
+                on_scalar(out=gx[b][half][:, t % 2, :].rearrange("p (m u e) -> p m u e", u=2, e=2),
                           in_=flat(bank[:]).rearrange("p (u m e) -> p m u e", u=2, e=2))
-            nc.scalar.dma_start(out=by_partition(out_1[b])[:, rows, :], in_=gx[b][:, rows, :])
+            nc.scalar.dma_start(out=by_partition(out_1[b])[:, rows, :], in_=gx[b][half][:])
 
         nc.vector.tensor_copy(ts_listed[:], ts_window[:].indirect(offsets[:]))
-        cast_pairs(0)
+        for k in range(T // CHUNK):
+            cast_pairs(activation_copy, 0, k, 0, CHUNK)
         for b in range(B):
-            gather(b, 0, WHOLE)
-        cast_pairs(1)
-        for b in range(B):
-            for j in range(PACK):
-                nc.tensor.transpose(banks[b][:, j, :], ts_listed[:, b * N + j * P:b * N + (j + 1) * P], ident[:])
-            nc.scalar.activation(out=minus_ts[:, b, :], in_=banks[b][:, :, 0], func=COPY, scale=-1.0)
+            gather(b, 0)
+        for k in range(T // CHUNK):
+            cast_pairs(activation_copy, 1, k, 0, CHUNK)
+        for k in range(PACK):
+            for j in range(2):
+                nc.tensor.transpose(banks[k][:, j, :], ts_listed[:, block(2 * k + j)], ident[:])
+            nc.scalar.activation(out=flat(minus_ts[:])[:, 2 * k:2 * k + 2], in_=banks[k][:, 0:2, 0], func=COPY,
+                                 scale=-1.0)
         nc.gpsimd.tensor_tensor(out=ts_squared[:], in0=minus_ts[:], in1=minus_ts[:], op=MULT)
-        for b in range(B):
-            turn_pairs(b, 0, banks[2 + b])
-        for cols in HALVES:
-            gather(0, 1, cols)
-        for cols in HALVES:
-            join_pairs(0, cols)
-        for cols in HALVES:
-            quantise(w_op[0], E4M3, w_grouped, cols)
-        turn_pairs(0, 1, banks[4])
-        for cols in HALVES:
-            interleave(on_vector, x_grouped, x_raw[0], cols)
-        quantise(x_op[0], E4M3, x_grouped, WHOLE)
-        for cols in HALVES:
-            gather(1, 1, cols)
-        for cols in HALVES:
-            join_pairs(1, cols)
-        for cols in HALVES:
-            quantise(w_op[1], E4M3, w_grouped, cols)
+        turn_pairs(0, 0, banks[6], early=True)
+        gather(0, 1)
+        join_pairs(0)
+        dw = [[sbuf.tile([P, 2, N], F32, name="dw%d" % b, tag="chunk0%d" % (2 * b + k)) for k in range(2)]
+              for b in range(B)]
+        gx = [[sbuf.tile([P, 2, N], F32, name="gx%d" % b, tag="chunk1%d" % (2 * b + k)) for k in range(2)]
+              for b in range(B)]
+        stage_a = half_stage("stage_a")
+        stage_half(on_scalar, stage_a[:], x_raw[0], 0)
+        stage_b = listed[:, 1, :].bitcast(BF16).rearrange("p (c t) -> p c t", t=PACK)
+        stage_half(on_vector, stage_b, x_raw[0], 1)
+        quantise(w_op[0], E4M3, w_grouped[0], WHOLE)
+        quantise_half(x_op[0], stage_a[:], 0)
+        quantise_half(x_op[0], stage_b, 1)
+        gather(1, 1)
 
-        y_part = [target_part(0, j, banks[j]) for j in range(PACK)]
+        for j in range(PACK):
+            turn_target(0, j, banks[j], (0, 1))
+        y_part = [target_part(0, j, banks[j], (2, 3)) for j in range(PACK)]
         for j in range(PACK):
             scores(0, j, banks[PACK + j])
-        turned = [banks[(j + 1) % PACK] for j in range(PACK)]
-        for j in range(PACK):
-            residual = part("a_part", j)
-            nc.vector.scalar_tensor_tensor(out=residual[:], in0=by_row(banks[PACK + j]),
-                                           scalar=ts_squared[:, 0, j:j + 1], in1=y_part[j][:], op0=MULT, op1=ADD)
-            for t in range(PACK):
-                nc.tensor.transpose(turned[j][:, t, :], residual[:, t, :], ident[:])
-        for j in range(PACK + 1):
+        for j in range(PACK + 2):
             if j < PACK:
-                nc.vector.tensor_tensor(out=h_grouped[0][:, block(j), :],
-                                        in0=turned[j][:].rearrange("p t i -> p i t"),
+                residual = part("a_part", j, "w_grouped1" if j == PACK - 1 else None)
+                nc.vector.scalar_tensor_tensor(out=residual[:], in0=by_row(banks[PACK + j]),
+                                               scalar=ts_squared[:, 0, j:j + 1], in1=y_part[j][:],
+                                               op0=MULT, op1=ADD)
+                for t in range(PACK):
+                    nc.tensor.transpose(banks[j][:, t, :], residual[:, t, :], ident[:])
+            if 1 <= j <= PACK:
+                nc.vector.tensor_tensor(out=h_grouped[0][:, block(j - 1), :],
+                                        in0=banks[j - 1][:].rearrange("p t i -> p i t"),
                                         in1=wt_rows[:, 0:1, :].to_broadcast([P, P, PACK]), op=MULT)
-            if j > 0:
-                quantise(h_op[0], E5M2, h_grouped[0], block(j - 1))
-        interleave(on_scalar, xm_grouped, xm_raw[0], HALVES[0])
-        quantise(xm_op[0], E4M3, xm_grouped, HALVES[0])
-        interleave(on_scalar, xm_grouped, xm_raw[0], HALVES[1])
-        for cols in HALVES:
-            interleave(on_scalar, x_grouped, x_raw[1], cols)
-        table_gradient(0, 0, banks[4])
-        quantise(x_op[1], E4M3, x_grouped, WHOLE)
-        quantise(xm_op[0], E4M3, xm_grouped, HALVES[1])
-        table_gradient(0, 1, banks[7])
-
-        a_part = []
-
-        def score_part(j, bank):
-            scores(1, j, bank)
-            a_part.append(part("a_part", j))
-            nc.scalar.activation(out=a_part[j][:], in_=by_row(bank), func=COPY, scale=ts_squared[:, 1, j:j + 1])
-
-        y_part = [target_part(1, 0, banks[3]), target_part(1, 1, banks[0])]
-        score_part(0, banks[5])
-        score_part(1, banks[6])
-        y_part.append(target_part(1, 2, banks[4]))
+            if j >= 2:
+                quantise(h_op[0], E5M2, h_grouped[0], block(j - 2))
+        stages = sbuf.tile([P, 3, N // 2, PACK], BF16, name="stages", tag="y_raw0", align_bytes=64)
+        xm_stage = [stages[:, half] for half in range(2)]
+        for half in range(2):
+            stage_half(on_scalar, xm_stage[half][:], xm_raw[0], half)
+            quantise_rows(0, half, xm_stage[half])
+        w_grouped.append(grouped_tile("w_grouped1"))
+        join_pairs(1)
+        quantise(w_op[1], E4M3, w_grouped[1], WHOLE)
+        x_stage = [stages[:, 2]]
+        stage_half(on_scalar, x_stage[0][:], x_raw[1], 0)
+        turn_pairs(0, 1, banks[6])
+        turn_pairs(1, 0, banks[7], early=True)
         for c in range(PACK):
-            interleave(on_scalar, x_grouped, xm_raw[1], block(c))
-            quantise(xm_op[1], E4M3, x_grouped, block(c))
-        y_part.append(target_part(1, 3, banks[5]))
-        table_gradient(0, 2, banks[1])
-        score_part(2, banks[3])
-        score_part(3, banks[0])
-        h_words = flat(h_grouped[0][:]).bitcast(F32)
-        for u, bank in enumerate((banks[6], banks[7])):
-            for s in range(PACK):
-                nc.tensor.transpose(bank[:, s, :], h_words[:, 2 * s + u:2 * N:2 * PACK], ident[:])
-            on_scalar(out=h_slots[0][:, HALVES[u], :].rearrange("p (e m) s -> p e m s", e=2),
-                      in_=flat(bank[:]).bitcast(BF16).rearrange("p (s m e) -> p e m s", s=PACK, e=2))
-        quantise(w_slot_op[0], E4M3, w_slots[0], WHOLE)
-        quantise(h_slot_op[0], E5M2, h_slots[0], WHOLE)
-        table_gradient(0, 3, banks[2])
-        for t, bank in enumerate((banks[4], banks[5], banks[3], banks[0])):
+            table_gradient(0, c, banks[PACK + c])
+        scatter(0, 0, banks[4])
+        x_stage.append(half_stage("xm00_codes"))
+        stage_half(on_scalar, x_stage[1][:], x_raw[1], 1)
+        for half in range(2):
+            quantise_half(x_op[1], x_stage[half][:], half)
+        for c in range(1, PACK):
+            scatter(0, c, banks[PACK + c])
+
+        y_part = [target_part(1, j, banks[PACK + j]) for j in range(PACK)]
+        a_part = [part("a_part", j) for j in range(PACK)]
+        for j in range(PACK):
+            scores(1, j, banks[PACK + j])
+            nc.scalar.activation(out=a_part[j][:], in_=by_row(banks[PACK + j]), func=COPY, scale=ts_squared[:, 1, j:j + 1])
+        xm_stage = [stages[:, 2], half_stage("xm00_codes")]
+        for half in range(2):
+            stage_half(on_scalar, xm_stage[half][:], xm_raw[1], half)
+            quantise_rows(1, half, xm_stage[half])
+        h_rows = sbuf.tile([P, PACK, N], BF16, name="h_rows", tag="ts_window", align_bytes=64)
+        for t in range(PACK):
+            bank = banks[t]
             for j in range(PACK):
                 nc.tensor.matmul(bank[:, j, :], lhsT=y_part[j][:, t, :], rhs=ident[:], start=True, stop=False,
                                  is_transpose=True)
                 nc.tensor.matmul(bank[:, j, :], lhsT=a_part[j][:, t, :], rhs=ident[:], start=False, stop=True,
                                  is_transpose=True)
-            nc.scalar.activation(out=h_rows[:, t, :], in_=flat(bank[:]), func=COPY, scale=wt_rows[:, 1, t:t + 1])
+            for cols in (HALVES if t == PACK - 1 else (WHOLE,)):
+                nc.scalar.activation(out=h_rows[:, t, cols], in_=flat(bank[:])[:, cols], func=COPY,
+                                     scale=wt_rows[:, 1, t:t + 1])
         interleave(on_scalar, h_grouped[1], h_rows, HALVES[0])
         interleave(on_vector, h_grouped[1], h_rows, HALVES[1])
         quantise(h_op[1], E5M2, h_grouped[1], WHOLE)
+        h_slots = [grouped_tile("h_slots%d" % b, tag="pairs%d" % b) for b in range(B)]
+        h_words = flat(h_grouped[0][:]).bitcast(F32)
 
-        late_codes = sbuf.tile([P, 2, N], U32, name="late_codes", tag="h_grouped1", align_bytes=64)
-        w_slot_op.append((late_codes[:, 0, :], scales_tile("w_i1")))
-        h_slot_op.append((late_codes[:, 1, :], scales_tile("h_i1")))
-        table_gradient(1, 0, banks[6])
-        turn_pairs(1, 1, banks[4])
-        for half, bank in enumerate((banks[5], banks[3])):
+        def turn_grouped(u, bank):
+            turn_words([h_words[:, 2 * s + u:2 * N:2 * PACK] for s in range(PACK)], bank)
+            on_scalar(out=h_slots[0][:, HALVES[u], :].rearrange("p (e m) s -> p e m s", e=2),
+                      in_=flat(bank[:]).bitcast(BF16).rearrange("p (s m e) -> p e m s", s=PACK, e=2))
+
+        def turn_rows(half, bank):
             for t in range(2):
                 words = h_rows[:, 2 * half + t, :].bitcast(F32)
                 for u in range(2):
@@ -300,12 +325,27 @@ def tile_attend_gsq_wx_ts_kernel(tc, xT, wT, y, wt, ts, xm, offs, out_0, out_1):
             out_words = flat(h_slots[1][:, HALVES[half], :]).bitcast(F32)
             on_scalar(out=out_words.rearrange("p (t m u) -> p t m u", t=2, u=2),
                       in_=bank[:].rearrange("p (t u) m -> p t m u", u=2))
-        quantise(w_slot_op[1], E4M3, w_slots[1], WHOLE)
+
+        def product_and_scatter(c):
+            table_gradient(1, c, banks[4])
+            scatter(1, c, banks[4])
+
+        late_codes = sbuf.tile([P, N], U32, name="w_i0_codes", tag="h_grouped1", align_bytes=64)
+        w_slot_op[0] = (late_codes, scales_tile("w_i0", N))
+        quantise(w_slot_op[0], E4M3, w_slots[0], WHOLE)
+        turn_grouped(0, banks[2])
+        turn_grouped(1, banks[3])
+        quantise(h_slot_op[0], E5M2, h_slots[0], WHOLE)
+        product_and_scatter(0)
+        turn_rows(0, banks[2])
+        turn_rows(1, banks[3])
+        turn_pairs(1, 1, banks[4])
         quantise(h_slot_op[1], E5M2, h_slots[1], WHOLE)
-        table_gradient(1, 1, banks[7])
+        quantise(w_slot_op[1], E4M3, w_slots[1], WHOLE)
+        product_and_scatter(1)
         row_gradient(0, 0, (banks[0], banks[1]))
-        row_gradient(0, 1, (banks[2], banks[6]))
-        table_gradient(1, 2, banks[4])
-        table_gradient(1, 3, banks[5])
-        row_gradient(1, 0, (banks[3], banks[7]))
-        row_gradient(1, 1, (banks[0], banks[1]))
+        row_gradient(0, 1, (banks[5], banks[6]))
+        product_and_scatter(2)
+        row_gradient(1, 0, (banks[7], banks[2]))
+        row_gradient(1, 1, (banks[3], banks[0]))
+        product_and_scatter(3)

@@ -97,9 +97,8 @@ def tile_attend_gsq_wx_ts_kernel(tc, xT, wT, y, wt, ts, xm, offs, out_0, out_1):
         wt_rows = sbuf.tile([P, B, PACK], F32, name="wt_rows")
         nc.sync.dma_start(out=wt_rows[:], in_=wt.rearrange("b (p t) o -> p b (t o)", t=PACK))
         y_raw = [sbuf.tile([P, PACK, N], F32, name="y_raw0", tag="y_raw0", align_bytes=64)]
-        for half in range(2):
-            rows = slice(2 * half, 2 * half + 2)
-            nc.sync.dma_start(out=y_raw[0][:, rows, :], in_=by_partition(y[0])[:, rows, :])
+        for cols in HALVES:
+            nc.sync.dma_start(out=y_raw[0][:, :, cols], in_=by_partition(y[0])[:, :, cols])
         xm_raw = [load(xm[0], "xm_raw0")]
         x_raw.append(load(xT[1], "x_raw1"))
         y_raw.append(load(y[1], "y_raw1"))
@@ -120,19 +119,19 @@ def tile_attend_gsq_wx_ts_kernel(tc, xT, wT, y, wt, ts, xm, offs, out_0, out_1):
             nc.vector.memset(window[:].bitcast(I32), 0)
 
         pairs = [sbuf.tile([P, T, 2], BF16, name="pairs%d" % u, tag="pairs%d" % u, align_bytes=64) for u in range(2)]
-        listed = sbuf.tile([P, 3, N], U32, name="listed", align_bytes=64)
-        listed_row = {(0, 0): 0, (0, 1): 1, (1, 0): 2, (1, 1): 1}
+        listed = sbuf.tile([P, 4, N], U32, name="listed", align_bytes=64)
+        listed_row = {(0, 0): 0, (0, 1): 1, (1, 0): 3, (1, 1): 1}
         ts_listed = sbuf.tile([P, B * N], F32, name="ts_listed")
         minus_ts = sbuf.tile([P, B, PACK], F32, name="minus_ts")
         ts_squared = sbuf.tile([P, B, PACK], F32, name="ts_squared")
         w_grouped = [grouped_tile("w_grouped0")]
         w_slots = [grouped_tile("w_slots%d" % b) for b in range(B)]
         h_grouped = [grouped_tile("h_grouped%d" % b) for b in range(B)]
-        x_op = [operand("x%d" % b) for b in range(B)]
+        x_op = [operand("x0")]
         w_op = [operand("w_d%d" % b) for b in range(B)]
         h_op = [operand("h_r%d" % b) for b in range(B)]
-        xm_op = [[operand("xm%d%d" % (b, half), N // 2) for half in range(2)] for b in range(B)]
-        w_slot_op = [None, operand("w_i1")]
+        xm_op = [[operand("xm00", N // 2)], [operand("xm1%d" % half, N // 2) for half in range(2)]]
+        w_slot_op = [operand("w_i%d" % b) for b in range(B)]
         h_slot_op = [operand("h_i%d" % b) for b in range(B)]
 
         def cast_pairs(copy, u, k, first, last):
@@ -147,7 +146,7 @@ def tile_attend_gsq_wx_ts_kernel(tc, xT, wT, y, wt, ts, xm, offs, out_0, out_1):
                                   flat(pairs[u][:]).bitcast(U32).indirect(offsets[:, b * LIST_COLS:(b + 1) * LIST_COLS]))
 
         def join_pairs(b):
-            rows = listed[:, 0:2, :] if b == 0 else listed[:, 2:0:-1, :]
+            rows = listed[:, 0:2, :] if b == 0 else listed[:, 3:0:-2, :]
             on_vector(out=flat(w_grouped[b][:]).bitcast(I32).rearrange("p (c u) -> p c u", u=2),
                       in_=rows.bitcast(I32).rearrange("p u c -> p c u"))
 
@@ -171,10 +170,6 @@ def tile_attend_gsq_wx_ts_kernel(tc, xT, wT, y, wt, ts, xm, offs, out_0, out_1):
         def stage_half(copy, stage, raw, half):
             copy(out=stage, in_=raw[:, :, HALVES[half]].rearrange("p t c -> p c t"))
 
-        def quantise_half(op, stage, half):
-            nc.vector.quantize_mx(out=op[0][:, HALVES[half]].bitcast(E4M3), scales=op[1][:, HALVES[half]],
-                                  in_=flat(stage))
-
         def quantise_rows(b, half, stage):
             quantise(xm_op[b][half], E4M3, stage, slice(0, N // 2))
 
@@ -187,12 +182,9 @@ def tile_attend_gsq_wx_ts_kernel(tc, xT, wT, y, wt, ts, xm, offs, out_0, out_1):
         def by_row(bank):
             return flat(bank[:]).rearrange("p (m t) -> p t m", t=PACK)
 
-        def turn_target(b, j, bank, rows):
-            for t in rows:
+        def target_part(b, j, bank):
+            for t in range(PACK):
                 nc.tensor.transpose(bank[:, t, :], y_raw[b][:, t, block(j)], ident[:])
-
-        def target_part(b, j, bank, rows=range(PACK)):
-            turn_target(b, j, bank, rows)
             out = part("y_part", j)
             nc.scalar.activation(out=out[:], in_=bank[:], func=COPY, scale=minus_ts[:, b, j:j + 1])
             return out
@@ -236,65 +228,54 @@ def tile_attend_gsq_wx_ts_kernel(tc, xT, wT, y, wt, ts, xm, offs, out_0, out_1):
               for b in range(B)]
         gx = [[sbuf.tile([P, 2, N], F32, name="gx%d" % b, tag="chunk1%d" % (2 * b + k)) for k in range(2)]
               for b in range(B)]
-        stage_a = half_stage("stage_a")
-        stage_half(on_scalar, stage_a[:], x_raw[0], 0)
-        stage_b = listed[:, 1, :].bitcast(BF16).rearrange("p (c t) -> p c t", t=PACK)
-        stage_half(on_vector, stage_b, x_raw[0], 1)
+        x_grouped = flat(listed[:, 1:3, :]).bitcast(BF16).rearrange("p (c t) -> p c t", t=PACK)
+        interleave(on_scalar, x_grouped, x_raw[0], HALVES[1])
+        interleave(on_vector, x_grouped, x_raw[0], HALVES[0])
         quantise(w_op[0], E4M3, w_grouped[0], WHOLE)
-        quantise_half(x_op[0], stage_a[:], 0)
-        quantise_half(x_op[0], stage_b, 1)
+        quantise(x_op[0], E4M3, x_grouped, WHOLE)
         gather(1, 1)
 
-        for j in range(PACK):
-            turn_target(0, j, banks[j], (0, 1))
-        y_part = [target_part(0, j, banks[j], (2, 3)) for j in range(PACK)]
+        y_part = [target_part(0, j, banks[j]) for j in range(PACK)]
         for j in range(PACK):
             scores(0, j, banks[PACK + j])
-        for j in range(PACK + 2):
-            if j < PACK:
-                residual = part("a_part", j, "w_grouped1" if j == PACK - 1 else None)
-                nc.vector.scalar_tensor_tensor(out=residual[:], in0=by_row(banks[PACK + j]),
-                                               scalar=ts_squared[:, 0, j:j + 1], in1=y_part[j][:],
-                                               op0=MULT, op1=ADD)
-                for t in range(PACK):
-                    nc.tensor.transpose(banks[j][:, t, :], residual[:, t, :], ident[:])
-            if 1 <= j <= PACK:
-                nc.vector.tensor_tensor(out=h_grouped[0][:, block(j - 1), :],
-                                        in0=banks[j - 1][:].rearrange("p t i -> p i t"),
-                                        in1=wt_rows[:, 0:1, :].to_broadcast([P, P, PACK]), op=MULT)
-            if j >= 2:
-                quantise(h_op[0], E5M2, h_grouped[0], block(j - 2))
-        stages = sbuf.tile([P, 3, N // 2, PACK], BF16, name="stages", tag="y_raw0", align_bytes=64)
-        xm_stage = [stages[:, half] for half in range(2)]
-        for half in range(2):
-            stage_half(on_scalar, xm_stage[half][:], xm_raw[0], half)
-            quantise_rows(0, half, xm_stage[half])
+        for j in range(PACK):
+            residual = part("a_part", j, {2: "late_codes", 3: "w_grouped1"}.get(j))
+            nc.vector.scalar_tensor_tensor(out=residual[:], in0=by_row(banks[PACK + j]),
+                                           scalar=ts_squared[:, 0, j:j + 1], in1=y_part[j][:], op0=MULT, op1=ADD)
+            for t in range(PACK):
+                nc.tensor.transpose(banks[j][:, t, :], residual[:, t, :], ident[:])
+        for j in range(PACK):
+            nc.vector.tensor_tensor(out=h_grouped[0][:, block(j), :],
+                                    in0=banks[j][:].rearrange("p t i -> p i t"),
+                                    in1=wt_rows[:, 0:1, :].to_broadcast([P, P, PACK]), op=MULT)
+        for cols in (HALVES[0], block(2), block(3)):
+            quantise(h_op[0], E5M2, h_grouped[0], cols)
         w_grouped.append(grouped_tile("w_grouped1"))
+        late = sbuf.tile([P, 3, N // 2], U32, name="late_codes", tag="late_codes", align_bytes=64)
+        xm_op[0].append((late[:, 0], scales_tile("xm01", N // 2)))
+        x_op.append((flat(late[:, 1:3]), scales_tile("x1", N)))
+        stages = sbuf.tile([P, 2, N, PACK], BF16, name="stages", tag="y_raw0", align_bytes=64)
+        for half in range(2):
+            interleave(on_scalar, stages[:, 0], xm_raw[0], HALVES[half])
+            quantise_rows(0, half, stages[:, 0, HALVES[half]])
         join_pairs(1)
         quantise(w_op[1], E4M3, w_grouped[1], WHOLE)
-        x_stage = [stages[:, 2]]
-        stage_half(on_scalar, x_stage[0][:], x_raw[1], 0)
-        turn_pairs(0, 1, banks[6])
-        turn_pairs(1, 0, banks[7], early=True)
-        for c in range(PACK):
+        for cols in HALVES:
+            interleave(on_scalar, stages[:, 1], x_raw[1], cols)
+        quantise(x_op[1], E4M3, stages[:, 1], WHOLE)
+        for c in range(PACK - 1):
             table_gradient(0, c, banks[PACK + c])
-        scatter(0, 0, banks[4])
-        x_stage.append(half_stage("xm00_codes"))
-        stage_half(on_scalar, x_stage[1][:], x_raw[1], 1)
-        for half in range(2):
-            quantise_half(x_op[1], x_stage[half][:], half)
-        for c in range(1, PACK):
+        for c in range(PACK - 1):
             scatter(0, c, banks[PACK + c])
 
         y_part = [target_part(1, j, banks[PACK + j]) for j in range(PACK)]
         a_part = [part("a_part", j) for j in range(PACK)]
         for j in range(PACK):
-            scores(1, j, banks[PACK + j])
-            nc.scalar.activation(out=a_part[j][:], in_=by_row(banks[PACK + j]), func=COPY, scale=ts_squared[:, 1, j:j + 1])
-        xm_stage = [stages[:, 2], half_stage("xm00_codes")]
-        for half in range(2):
-            stage_half(on_scalar, xm_stage[half][:], xm_raw[1], half)
-            quantise_rows(1, half, xm_stage[half])
+            bank = banks[PACK + (j - 1) % PACK]
+            scores(1, j, bank)
+            nc.scalar.activation(out=a_part[j][:], in_=by_row(bank), func=COPY, scale=ts_squared[:, 1, j:j + 1])
+        interleave(on_scalar, stages[:, 1], xm_raw[1], HALVES[0])
+        quantise_rows(1, 0, stages[:, 1, HALVES[0]])
         h_rows = sbuf.tile([P, PACK, N], BF16, name="h_rows", tag="ts_window", align_bytes=64)
         for t in range(PACK):
             bank = banks[t]
@@ -309,6 +290,8 @@ def tile_attend_gsq_wx_ts_kernel(tc, xT, wT, y, wt, ts, xm, offs, out_0, out_1):
         interleave(on_scalar, h_grouped[1], h_rows, HALVES[0])
         interleave(on_vector, h_grouped[1], h_rows, HALVES[1])
         quantise(h_op[1], E5M2, h_grouped[1], WHOLE)
+        table_gradient(0, 3, banks[0])
+        scatter(0, 3, banks[0])
         h_slots = [grouped_tile("h_slots%d" % b, tag="pairs%d" % b) for b in range(B)]
         h_words = flat(h_grouped[0][:]).bitcast(F32)
 
@@ -326,26 +309,29 @@ def tile_attend_gsq_wx_ts_kernel(tc, xT, wT, y, wt, ts, xm, offs, out_0, out_1):
             on_scalar(out=out_words.rearrange("p (t m u) -> p t m u", t=2, u=2),
                       in_=bank[:].rearrange("p (t u) m -> p t m u", u=2))
 
-        def product_and_scatter(c):
-            table_gradient(1, c, banks[4])
-            scatter(1, c, banks[4])
+        def product_and_scatter(c, bank):
+            table_gradient(1, c, bank)
+            scatter(1, c, bank)
 
-        late_codes = sbuf.tile([P, N], U32, name="w_i0_codes", tag="h_grouped1", align_bytes=64)
-        w_slot_op[0] = (late_codes, scales_tile("w_i0", N))
+        turn_pairs(0, 1, banks[1])
         quantise(w_slot_op[0], E4M3, w_slots[0], WHOLE)
         turn_grouped(0, banks[2])
         turn_grouped(1, banks[3])
         quantise(h_slot_op[0], E5M2, h_slots[0], WHOLE)
-        product_and_scatter(0)
-        turn_rows(0, banks[2])
-        turn_rows(1, banks[3])
-        turn_pairs(1, 1, banks[4])
+        product_and_scatter(0, banks[4])
+        turn_rows(0, banks[0])
+        turn_rows(1, banks[1])
         quantise(h_slot_op[1], E5M2, h_slots[1], WHOLE)
+        turn_pairs(1, 0, banks[2])
+        turn_pairs(1, 1, banks[3])
         quantise(w_slot_op[1], E4M3, w_slots[1], WHOLE)
-        product_and_scatter(1)
-        row_gradient(0, 0, (banks[0], banks[1]))
-        row_gradient(0, 1, (banks[5], banks[6]))
-        product_and_scatter(2)
-        row_gradient(1, 0, (banks[7], banks[2]))
-        row_gradient(1, 1, (banks[3], banks[0]))
-        product_and_scatter(3)
+        last_stage = half_stage("a_part3")
+        stage_half(on_scalar, last_stage[:], xm_raw[1], 1)
+        quantise_rows(1, 1, last_stage)
+        product_and_scatter(1, banks[4])
+        row_gradient(0, 0, (banks[5], banks[6]))
+        row_gradient(0, 1, (banks[7], banks[0]))
+        product_and_scatter(2, banks[4])
+        row_gradient(1, 0, (banks[1], banks[2]))
+        row_gradient(1, 1, (banks[3], banks[5]))
+        product_and_scatter(3, banks[4])

@@ -141,6 +141,9 @@ def tile_attend_gsq_wx_ts_kernel(tc, xT, wT, y, wt, ts, xm, offs, out_0, out_1):
         def activation_copy(out, in_):
             nc.scalar.activation(out=out, in_=in_, func=COPY)
 
+        def on_gpsimd(out, in_):
+            nc.gpsimd.tensor_scalar(out=out, in0=in_, scalar1=1.0, scalar2=0.0, op0=MULT, op1=ADD)
+
         def gather(b, u):
             nc.vector.tensor_copy(listed[:, listed_row[b, u], :],
                                   flat(pairs[u][:]).bitcast(U32).indirect(offsets[:, b * LIST_COLS:(b + 1) * LIST_COLS]))
@@ -163,12 +166,6 @@ def tile_attend_gsq_wx_ts_kernel(tc, xT, wT, y, wt, ts, xm, offs, out_0, out_1):
                 turn_words([words[:, 2 * s + u:2 * N:2 * PACK] for s in range(PACK)], bank)
             on_scalar(out=w_slots[b][:, HALVES[u], :].rearrange("p (m e) s -> p m e s", e=2),
                       in_=flat(bank[:]).bitcast(BF16).rearrange("p (s m e) -> p m e s", s=PACK, e=2))
-
-        def half_stage(tag):
-            return sbuf.tile([P, N // 2, PACK], BF16, name="stage", tag=tag, align_bytes=64)
-
-        def stage_half(copy, stage, raw, half):
-            copy(out=stage, in_=raw[:, :, HALVES[half]].rearrange("p t c -> p c t"))
 
         def quantise_rows(b, half, stage):
             quantise(xm_op[b][half], E4M3, stage, slice(0, N // 2))
@@ -274,8 +271,9 @@ def tile_attend_gsq_wx_ts_kernel(tc, xT, wT, y, wt, ts, xm, offs, out_0, out_1):
             bank = banks[PACK + (j - 1) % PACK]
             scores(1, j, bank)
             nc.scalar.activation(out=a_part[j][:], in_=by_row(bank), func=COPY, scale=ts_squared[:, 1, j:j + 1])
-        interleave(on_scalar, stages[:, 1], xm_raw[1], HALVES[0])
-        quantise_rows(1, 0, stages[:, 1, HALVES[0]])
+        for half in range(2):
+            interleave(on_gpsimd, stages[:, 1], xm_raw[1], HALVES[half])
+            quantise_rows(1, half, stages[:, 1, HALVES[half]])
         h_rows = sbuf.tile([P, PACK, N], BF16, name="h_rows", tag="ts_window", align_bytes=64)
         for t in range(PACK):
             bank = banks[t]
@@ -288,7 +286,7 @@ def tile_attend_gsq_wx_ts_kernel(tc, xT, wT, y, wt, ts, xm, offs, out_0, out_1):
                 nc.scalar.activation(out=h_rows[:, t, cols], in_=flat(bank[:])[:, cols], func=COPY,
                                      scale=wt_rows[:, 1, t:t + 1])
         interleave(on_scalar, h_grouped[1], h_rows, HALVES[0])
-        interleave(on_vector, h_grouped[1], h_rows, HALVES[1])
+        interleave(on_gpsimd, h_grouped[1], h_rows, HALVES[1])
         quantise(h_op[1], E5M2, h_grouped[1], WHOLE)
         table_gradient(0, 3, banks[0])
         scatter(0, 3, banks[0])
@@ -325,9 +323,6 @@ def tile_attend_gsq_wx_ts_kernel(tc, xT, wT, y, wt, ts, xm, offs, out_0, out_1):
         turn_pairs(1, 0, banks[2])
         turn_pairs(1, 1, banks[3])
         quantise(w_slot_op[1], E4M3, w_slots[1], WHOLE)
-        last_stage = half_stage("a_part3")
-        stage_half(on_scalar, last_stage[:], xm_raw[1], 1)
-        quantise_rows(1, 1, last_stage)
         product_and_scatter(1, banks[4])
         row_gradient(0, 0, (banks[5], banks[6]))
         row_gradient(0, 1, (banks[7], banks[0]))

@@ -1,7 +1,6 @@
 from contextlib import ExitStack
 
 import concourse.mybir as mybir
-from concourse.masks import make_identity
 
 F32 = mybir.dt.float32
 BF16 = mybir.dt.bfloat16
@@ -14,6 +13,7 @@ E5M2 = mybir.dt.float8_e5m2_x4
 COPY = mybir.ActivationFunctionType.Copy
 MULT = mybir.AluOpType.mult
 ADD = mybir.AluOpType.add
+NOT_EQUAL = mybir.AluOpType.not_equal
 
 P = 128
 PACK = 4
@@ -70,11 +70,14 @@ def tile_attend_gsq_wx_ts_kernel(tc, xT, wT, y, wt, ts, xm, offs, out_0, out_1):
         on_vector = nc.vector.tensor_copy
         on_scalar = nc.scalar.copy
 
-        ts_cols = sbuf.tile([P, TS_COLS + P], F32, name="ts_cols")
+        zeros = sbuf.tile([P, P], F32, name="zeros", tag="window2")
+        nc.gpsimd.memset(zeros[:], 0.0)
+        ts_cols = sbuf.tile([P, TS_COLS + P], F32, name="ts_cols", tag="window3")
         nc.gpsimd.memset(ts_cols[:, TS_COLS:], 0.0)
         nc.sync.dma_start(out=ts_cols[:, 0:TS_COLS], in_=ts[0:1, :].rearrange("o (p c) -> (o p) c", p=P))
         ident = sbuf.tile([P, P], F32, name="ident")
-        make_identity(nc, ident[:])
+        nc.gpsimd.affine_select(out=ident[:], in_=zeros[:], compare_op=NOT_EQUAL, fill=1.0, base=0,
+                                pattern=[[-1, P]], channel_multiplier=1)
 
         def load_chunk(u, k):
             tile = sbuf.tile([P, 2, CHUNK], F32, name="chunk%d%d" % (u, k), tag="chunk%d%d" % (u, k))
@@ -114,12 +117,12 @@ def tile_attend_gsq_wx_ts_kernel(tc, xT, wT, y, wt, ts, xm, offs, out_0, out_1):
                       in_=ts_bank[:].rearrange("m c p -> m p c"))
         banks = [psum.tile([P, PACK, P], F32, name="bank%d" % k, tag="bank%d" % k) for k in range(BANKS)]
 
-        windows = [sbuf.tile([P, T], F32, name="window%d" % c) for c in range(PACK)]
-        for window in windows:
-            nc.vector.memset(window[:].bitcast(I32), 0)
+        windows = [sbuf.tile([P, T], F32, name="window%d" % c, tag="window%d" % c) for c in range(PACK)]
+        for c in range(PACK):
+            (nc.vector if c < PACK // 2 else nc.gpsimd).memset(windows[c][:].bitcast(I32), 0)
 
         pairs = [sbuf.tile([P, T, 2], BF16, name="pairs%d" % u, tag="pairs%d" % u, align_bytes=64) for u in range(2)]
-        listed = sbuf.tile([P, 4, N], U32, name="listed", align_bytes=64)
+        listed = sbuf.tile([P, 4, N], U32, name="listed", tag="ts_window", align_bytes=64)
         listed_row = {(0, 0): 0, (0, 1): 1, (1, 0): 3, (1, 1): 1}
         ts_listed = sbuf.tile([P, B * N], F32, name="ts_listed")
         minus_ts = sbuf.tile([P, B, PACK], F32, name="minus_ts")
@@ -274,7 +277,7 @@ def tile_attend_gsq_wx_ts_kernel(tc, xT, wT, y, wt, ts, xm, offs, out_0, out_1):
         for half in range(2):
             interleave(on_gpsimd, stages[:, 1], xm_raw[1], HALVES[half])
             quantise_rows(1, half, stages[:, 1, HALVES[half]])
-        h_rows = sbuf.tile([P, PACK, N], BF16, name="h_rows", tag="ts_window", align_bytes=64)
+        h_rows = sbuf.tile([P, PACK, N], BF16, name="h_rows", align_bytes=64)
         for t in range(PACK):
             bank = banks[t]
             for j in range(PACK):

@@ -131,9 +131,9 @@ def tile_attend_gsq_wx_ts_kernel(tc, xT, wT, y, wt, ts, xm, offs, out_0, out_1):
         w_slots = [grouped_tile("w_slots%d" % b) for b in range(B)]
         h_grouped = [grouped_tile("h_grouped%d" % b) for b in range(B)]
         x_op = [operand("x0")]
-        w_op = [operand("w_d%d" % b) for b in range(B)]
+        w_op = [operand("w_d0")]
         h_op = [operand("h_r%d" % b) for b in range(B)]
-        xm_op = [[operand("xm00", N // 2)], [operand("xm1%d" % half, N // 2) for half in range(2)]]
+        xm_op = [[], [operand("xm1%d" % half, N // 2) for half in range(2)]]
         w_slot_op = [operand("w_i%d" % b) for b in range(B)]
         h_slot_op = [operand("h_i%d" % b) for b in range(B)]
 
@@ -151,10 +151,10 @@ def tile_attend_gsq_wx_ts_kernel(tc, xT, wT, y, wt, ts, xm, offs, out_0, out_1):
             nc.vector.tensor_copy(listed[:, listed_row[b, u], :],
                                   flat(pairs[u][:]).bitcast(U32).indirect(offsets[:, b * LIST_COLS:(b + 1) * LIST_COLS]))
 
-        def join_pairs(b):
+        def join_pairs(b, copy, word):
             rows = listed[:, 0:2, :] if b == 0 else listed[:, 3:0:-2, :]
-            on_vector(out=flat(w_grouped[b][:]).bitcast(I32).rearrange("p (c u) -> p c u", u=2),
-                      in_=rows.bitcast(I32).rearrange("p u c -> p c u"))
+            copy(out=flat(w_grouped[b][:]).bitcast(word).rearrange("p (c u) -> p c u", u=2),
+                 in_=rows.bitcast(word).rearrange("p u c -> p c u"))
 
         def turn_words(words, bank):
             for s in range(PACK):
@@ -223,7 +223,7 @@ def tile_attend_gsq_wx_ts_kernel(tc, xT, wT, y, wt, ts, xm, offs, out_0, out_1):
         nc.gpsimd.tensor_tensor(out=ts_squared[:], in0=minus_ts[:], in1=minus_ts[:], op=MULT)
         turn_pairs(0, 0, banks[6], early=True)
         gather(0, 1)
-        join_pairs(0)
+        join_pairs(0, on_vector, I32)
         dw = [[sbuf.tile([P, 2, N], F32, name="dw%d" % b, tag="chunk0%d" % (2 * b + k)) for k in range(2)]
               for b in range(B)]
         gx = [[sbuf.tile([P, 2, N], F32, name="gx%d" % b, tag="chunk1%d" % (2 * b + k)) for k in range(2)]
@@ -236,10 +236,13 @@ def tile_attend_gsq_wx_ts_kernel(tc, xT, wT, y, wt, ts, xm, offs, out_0, out_1):
         gather(1, 1)
 
         y_part = [target_part(0, j, banks[j]) for j in range(PACK)]
+        after_y = sbuf.tile([P, 3, N, PACK], BF16, name="after_y", tag="y_raw0", align_bytes=64)
+        w_grouped.append(after_y[:, 1])
+        join_pairs(1, on_scalar, U32)
         for j in range(PACK):
             scores(0, j, banks[PACK + j])
         for j in range(PACK):
-            residual = part("a_part", j, {2: "late_codes", 3: "w_grouped1"}.get(j))
+            residual = part("a_part", j, "late_codes" if j == PACK - 1 else None)
             nc.vector.scalar_tensor_tensor(out=residual[:], in0=by_row(banks[PACK + j]),
                                            scalar=ts_squared[:, 0, j:j + 1], in1=y_part[j][:], op0=MULT, op1=ADD)
             for t in range(PACK):
@@ -248,43 +251,45 @@ def tile_attend_gsq_wx_ts_kernel(tc, xT, wT, y, wt, ts, xm, offs, out_0, out_1):
             nc.vector.tensor_tensor(out=h_grouped[0][:, block(j), :],
                                     in0=banks[j][:].rearrange("p t i -> p i t"),
                                     in1=wt_rows[:, 0:1, :].to_broadcast([P, P, PACK]), op=MULT)
-        for cols in (HALVES[0], block(2), block(3)):
-            quantise(h_op[0], E5M2, h_grouped[0], cols)
-        w_grouped.append(grouped_tile("w_grouped1"))
-        late = sbuf.tile([P, 3, N // 2], U32, name="late_codes", tag="late_codes", align_bytes=64)
-        xm_op[0].append((late[:, 0], scales_tile("xm01", N // 2)))
+        late = sbuf.tile([P, 6, N // 2], U32, name="late_codes", tag="late_codes", align_bytes=64)
+        xm_op[0].extend([(late[:, 5], scales_tile("xm00", N // 2)), (late[:, 0], scales_tile("xm01", N // 2))])
         x_op.append((flat(late[:, 1:3]), scales_tile("x1", N)))
-        stages = sbuf.tile([P, 2, N, PACK], BF16, name="stages", tag="y_raw0", align_bytes=64)
-        for half in range(2):
-            interleave(on_scalar, stages[:, 0], xm_raw[0], HALVES[half])
-            quantise_rows(0, half, stages[:, 0, HALVES[half]])
-        join_pairs(1)
+        w_op.append((flat(late[:, 3:5]), scales_tile("w_d1", N)))
+        stages = [after_y[:, 0], after_y[:, 2]]
+        for cols in HALVES:
+            interleave(on_gpsimd, stages[0], xm_raw[0], cols)
+        quantise(h_op[0], E5M2, h_grouped[0], HALVES[0])
+        quantise_rows(0, 0, stages[0][:, HALVES[0]])
+        quantise(h_op[0], E5M2, h_grouped[0], HALVES[1])
+        quantise_rows(0, 1, stages[0][:, HALVES[1]])
         quantise(w_op[1], E4M3, w_grouped[1], WHOLE)
         for cols in HALVES:
-            interleave(on_scalar, stages[:, 1], x_raw[1], cols)
-        quantise(x_op[1], E4M3, stages[:, 1], WHOLE)
+            interleave(on_scalar, stages[1], x_raw[1], cols)
+        quantise(x_op[1], E4M3, stages[1], WHOLE)
+        y_part = [target_part(1, j, banks[j]) for j in range(2)]
         for c in range(PACK - 1):
             table_gradient(0, c, banks[PACK + c])
         for c in range(PACK - 1):
             scatter(0, c, banks[PACK + c])
 
-        y_part = [target_part(1, j, banks[PACK + j]) for j in range(PACK)]
+        y_part.extend(target_part(1, j, banks[2 + j]) for j in range(2, PACK))
         a_part = [part("a_part", j) for j in range(PACK)]
         for j in range(PACK):
-            bank = banks[PACK + (j - 1) % PACK]
+            bank = banks[(2, 3, 7, 6)[j]]
             scores(1, j, bank)
             nc.scalar.activation(out=a_part[j][:], in_=by_row(bank), func=COPY, scale=ts_squared[:, 1, j:j + 1])
         for half in range(2):
-            interleave(on_gpsimd, stages[:, 1], xm_raw[1], HALVES[half])
-            quantise_rows(1, half, stages[:, 1, HALVES[half]])
+            interleave(on_gpsimd, stages[1], xm_raw[1], HALVES[half])
+            quantise_rows(1, half, stages[1][:, HALVES[half]])
         h_rows = sbuf.tile([P, PACK, N], BF16, name="h_rows", align_bytes=64)
+        for j in range(PACK):
+            for t in range(PACK):
+                nc.tensor.matmul(banks[t][:, j, :], lhsT=a_part[j][:, t, :], rhs=ident[:], start=True, stop=False,
+                                 is_transpose=True)
+                nc.tensor.matmul(banks[t][:, j, :], lhsT=y_part[j][:, t, :], rhs=ident[:], start=False, stop=True,
+                                 is_transpose=True)
         for t in range(PACK):
             bank = banks[t]
-            for j in range(PACK):
-                nc.tensor.matmul(bank[:, j, :], lhsT=y_part[j][:, t, :], rhs=ident[:], start=True, stop=False,
-                                 is_transpose=True)
-                nc.tensor.matmul(bank[:, j, :], lhsT=a_part[j][:, t, :], rhs=ident[:], start=False, stop=True,
-                                 is_transpose=True)
             for cols in (HALVES if t == PACK - 1 else (WHOLE,)):
                 nc.scalar.activation(out=h_rows[:, t, cols], in_=flat(bank[:])[:, cols], func=COPY,
                                      scale=wt_rows[:, 1, t:t + 1])

@@ -70,9 +70,9 @@ def tile_attend_gsq_wx_ts_kernel(tc, xT, wT, y, wt, ts, xm, offs, out_0, out_1):
         on_vector = nc.vector.tensor_copy
         on_scalar = nc.scalar.copy
 
-        zeros = sbuf.tile([P, P], F32, name="zeros", tag="window2")
+        zeros = sbuf.tile([P, P], F32, name="zeros", tag="window0")
         nc.gpsimd.memset(zeros[:], 0.0)
-        ts_cols = sbuf.tile([P, TS_COLS + P], F32, name="ts_cols", tag="window3")
+        ts_cols = sbuf.tile([P, TS_COLS + P], F32, name="ts_cols", tag="window1")
         nc.gpsimd.memset(ts_cols[:, TS_COLS:], 0.0)
         nc.sync.dma_start(out=ts_cols[:, 0:TS_COLS], in_=ts[0:1, :].rearrange("o (p c) -> (o p) c", p=P))
         ident = sbuf.tile([P, P], F32, name="ident")
@@ -80,7 +80,8 @@ def tile_attend_gsq_wx_ts_kernel(tc, xT, wT, y, wt, ts, xm, offs, out_0, out_1):
                                 pattern=[[-1, P]], channel_multiplier=1)
 
         def load_chunk(u, k):
-            tile = sbuf.tile([P, 2, CHUNK], F32, name="chunk%d%d" % (u, k), tag="chunk%d%d" % (u, k))
+            tag = "window%d" % (2 + k) if u == 0 and k < 2 else "chunk%d%d" % (u, k)
+            tile = sbuf.tile([P, 2, CHUNK], F32, name="chunk%d%d" % (u, k), tag=tag)
             nc.sync.dma_start(out=tile[:], in_=by_partition(wT)[:, 2 * u:2 * u + 2, k * CHUNK:(k + 1) * CHUNK])
             return tile
 
@@ -97,11 +98,11 @@ def tile_attend_gsq_wx_ts_kernel(tc, xT, wT, y, wt, ts, xm, offs, out_0, out_1):
                 if (u, k) not in chunks:
                     chunks[u, k] = load_chunk(u, k)
         x_raw = [load(xT[0], "x_raw0")]
+        y_raw = [sbuf.tile([P, PACK, N], F32, name="y_raw0", tag="y_raw0", align_bytes=64)]
+        for rows in (slice(0, 2), slice(2, PACK)):
+            nc.sync.dma_start(out=y_raw[0][:, rows, :], in_=by_partition(y[0])[:, rows, :])
         wt_rows = sbuf.tile([P, B, PACK], F32, name="wt_rows")
         nc.sync.dma_start(out=wt_rows[:], in_=wt.rearrange("b (p t) o -> p b (t o)", t=PACK))
-        y_raw = [sbuf.tile([P, PACK, N], F32, name="y_raw0", tag="y_raw0", align_bytes=64)]
-        for cols in HALVES:
-            nc.sync.dma_start(out=y_raw[0][:, :, cols], in_=by_partition(y[0])[:, :, cols])
         xm_raw = [load(xm[0], "xm_raw0")]
         x_raw.append(load(xT[1], "x_raw1"))
         y_raw.append(load(y[1], "y_raw1"))
@@ -117,13 +118,8 @@ def tile_attend_gsq_wx_ts_kernel(tc, xT, wT, y, wt, ts, xm, offs, out_0, out_1):
                       in_=ts_bank[:].rearrange("m c p -> m p c"))
         banks = [psum.tile([P, PACK, P], F32, name="bank%d" % k, tag="bank%d" % k) for k in range(BANKS)]
 
-        windows = [sbuf.tile([P, T], F32, name="window%d" % c, tag="window%d" % c) for c in range(PACK)]
-        for c in range(PACK):
-            (nc.vector if c < PACK // 2 else nc.gpsimd).memset(windows[c][:].bitcast(I32), 0)
-
         pairs = [sbuf.tile([P, T, 2], BF16, name="pairs%d" % u, tag="pairs%d" % u, align_bytes=64) for u in range(2)]
-        listed = sbuf.tile([P, 4, N], U32, name="listed", tag="ts_window", align_bytes=64)
-        listed_row = {(0, 0): 0, (0, 1): 1, (1, 0): 3, (1, 1): 1}
+        listed = sbuf.tile([P, B, 2, N], U32, name="listed", tag="ts_window", align_bytes=64)
         ts_listed = sbuf.tile([P, B * N], F32, name="ts_listed")
         minus_ts = sbuf.tile([P, B, PACK], F32, name="minus_ts")
         ts_squared = sbuf.tile([P, B, PACK], F32, name="ts_squared")
@@ -131,10 +127,9 @@ def tile_attend_gsq_wx_ts_kernel(tc, xT, wT, y, wt, ts, xm, offs, out_0, out_1):
         w_slots = [grouped_tile("w_slots%d" % b) for b in range(B)]
         h_grouped = [grouped_tile("h_grouped%d" % b) for b in range(B)]
         x_op = [operand("x0")]
-        w_op = [operand("w_d0")]
+        w_op = [operand("w_d%d" % b) for b in range(B)]
         h_op = [operand("h_r%d" % b) for b in range(B)]
         xm_op = [[], [operand("xm1%d" % half, N // 2) for half in range(2)]]
-        w_slot_op = [operand("w_i%d" % b) for b in range(B)]
         h_slot_op = [operand("h_i%d" % b) for b in range(B)]
 
         def cast_pairs(copy, u, k, first, last):
@@ -148,27 +143,22 @@ def tile_attend_gsq_wx_ts_kernel(tc, xT, wT, y, wt, ts, xm, offs, out_0, out_1):
             nc.gpsimd.tensor_scalar(out=out, in0=in_, scalar1=1.0, scalar2=0.0, op0=MULT, op1=ADD)
 
         def gather(b, u):
-            nc.vector.tensor_copy(listed[:, listed_row[b, u], :],
+            nc.vector.tensor_copy(listed[:, b, u, :],
                                   flat(pairs[u][:]).bitcast(U32).indirect(offsets[:, b * LIST_COLS:(b + 1) * LIST_COLS]))
 
         def join_pairs(b, copy, word):
-            rows = listed[:, 0:2, :] if b == 0 else listed[:, 3:0:-2, :]
             copy(out=flat(w_grouped[b][:]).bitcast(word).rearrange("p (c u) -> p c u", u=2),
-                 in_=rows.bitcast(word).rearrange("p u c -> p c u"))
+                 in_=listed[:, b].bitcast(word).rearrange("p u c -> p c u"))
 
         def turn_words(words, bank):
             for s in range(PACK):
                 nc.tensor.transpose(bank[:, s, :], words[s], ident[:])
 
-        def turn_pairs(b, u, bank, early=False):
-            if early:
-                words = listed[:, listed_row[b, u], :].bitcast(F32)
-                turn_words([words[:, s:N:PACK] for s in range(PACK)], bank)
-            else:
-                words = flat(w_grouped[b][:]).bitcast(F32)
-                turn_words([words[:, 2 * s + u:2 * N:2 * PACK] for s in range(PACK)], bank)
-            on_scalar(out=w_slots[b][:, HALVES[u], :].rearrange("p (m e) s -> p m e s", e=2),
-                      in_=flat(bank[:]).bitcast(BF16).rearrange("p (s m e) -> p m e s", s=PACK, e=2))
+        def turn_pairs(b, u, bank, copy):
+            words = listed[:, b, u, :].bitcast(F32)
+            turn_words([words[:, s:N:PACK] for s in range(PACK)], bank)
+            copy(out=w_slots[b][:, HALVES[u], :].rearrange("p (m e) s -> p m e s", e=2),
+                 in_=flat(bank[:]).bitcast(BF16).rearrange("p (s m e) -> p m e s", s=PACK, e=2))
 
         def quantise_rows(b, half, stage):
             quantise(xm_op[b][half], E4M3, stage, slice(0, N // 2))
@@ -182,23 +172,35 @@ def tile_attend_gsq_wx_ts_kernel(tc, xT, wT, y, wt, ts, xm, offs, out_0, out_1):
         def by_row(bank):
             return flat(bank[:]).rearrange("p (m t) -> p t m", t=PACK)
 
-        def target_part(b, j, bank):
-            for t in range(PACK):
+        def turn_targets(b, j, bank, rows):
+            for t in rows:
                 nc.tensor.transpose(bank[:, t, :], y_raw[b][:, t, block(j)], ident[:])
+
+        def scale_targets(b, j, bank):
             out = part("y_part", j)
             nc.scalar.activation(out=out[:], in_=bank[:], func=COPY, scale=minus_ts[:, b, j:j + 1])
             return out
 
+        def target_part(b, j, bank):
+            turn_targets(b, j, bank, range(PACK))
+            return scale_targets(b, j, bank)
+
         def scores(b, j, bank):
             product(bank, w_op[b], E4M3, j, x_op[b], E4M3)
 
-        def scatter(b, c, bank):
+        def stage(b, c, bank):
             staged = dw[b][c // 2][:, c % 2, :]
             on_scalar(out=staged, in_=flat(bank[:]))
+            return staged
+
+        def place(b, c, staged):
             nc.vector.tensor_copy(windows[c][:].indirect(offsets[:, b * LIST_COLS:(b + 1) * LIST_COLS]),
                                   staged)
             if b == B - 1:
                 nc.sync.dma_start(out=out_0[block(c), :], in_=windows[c][:])
+
+        def scatter(b, c, bank):
+            place(b, c, stage(b, c, bank))
 
         def row_gradient(b, half, bank_pair):
             rows = slice(2 * half, 2 * half + 2)
@@ -213,32 +215,38 @@ def tile_attend_gsq_wx_ts_kernel(tc, xT, wT, y, wt, ts, xm, offs, out_0, out_1):
             cast_pairs(activation_copy, 0, k, 0, CHUNK)
         for b in range(B):
             gather(b, 0)
+        windows = [sbuf.tile([P, T], F32, name="window%d" % c, tag="window%d" % c) for c in range(PACK)]
+        for c in range(PACK):
+            nc.gpsimd.memset(windows[c][:].bitcast(I32), 0)
         for k in range(T // CHUNK):
             cast_pairs(activation_copy, 1, k, 0, CHUNK)
+        turn_pairs(0, 0, banks[6], on_vector)
+        turn_pairs(1, 0, banks[7], on_scalar)
         for k in range(PACK):
             for j in range(2):
                 nc.tensor.transpose(banks[k][:, j, :], ts_listed[:, block(2 * k + j)], ident[:])
             nc.scalar.activation(out=flat(minus_ts[:])[:, 2 * k:2 * k + 2], in_=banks[k][:, 0:2, 0], func=COPY,
                                  scale=-1.0)
         nc.gpsimd.tensor_tensor(out=ts_squared[:], in0=minus_ts[:], in1=minus_ts[:], op=MULT)
-        turn_pairs(0, 0, banks[6], early=True)
-        gather(0, 1)
+        for b in range(B):
+            gather(b, 1)
         join_pairs(0, on_vector, I32)
+        quantise(w_op[0], E4M3, w_grouped[0], WHOLE)
+        x_grouped = grouped_tile("x_grouped0")
+        interleave(on_scalar, x_grouped, x_raw[0], WHOLE)
+        quantise(x_op[0], E4M3, x_grouped, WHOLE)
+        w_grouped.append(grouped_tile("w_grouped1", tag="x_grouped0"))
+        join_pairs(1, on_vector, I32)
+        quantise(w_op[1], E4M3, w_grouped[1], WHOLE)
         dw = [[sbuf.tile([P, 2, N], F32, name="dw%d" % b, tag="chunk0%d" % (2 * b + k)) for k in range(2)]
               for b in range(B)]
         gx = [[sbuf.tile([P, 2, N], F32, name="gx%d" % b, tag="chunk1%d" % (2 * b + k)) for k in range(2)]
               for b in range(B)]
-        x_grouped = flat(listed[:, 1:3, :]).bitcast(BF16).rearrange("p (c t) -> p c t", t=PACK)
-        interleave(on_scalar, x_grouped, x_raw[0], HALVES[1])
-        interleave(on_vector, x_grouped, x_raw[0], HALVES[0])
-        quantise(w_op[0], E4M3, w_grouped[0], WHOLE)
-        quantise(x_op[0], E4M3, x_grouped, WHOLE)
-        gather(1, 1)
 
-        y_part = [target_part(0, j, banks[j]) for j in range(PACK)]
-        after_y = sbuf.tile([P, 3, N, PACK], BF16, name="after_y", tag="y_raw0", align_bytes=64)
-        w_grouped.append(after_y[:, 1])
-        join_pairs(1, on_scalar, U32)
+        for rows in (range(0, 2), range(2, PACK)):
+            for j in range(PACK):
+                turn_targets(0, j, banks[j], rows)
+        y_part = [scale_targets(0, j, banks[j]) for j in range(PACK)]
         for j in range(PACK):
             scores(0, j, banks[PACK + j])
         for j in range(PACK):
@@ -251,54 +259,62 @@ def tile_attend_gsq_wx_ts_kernel(tc, xT, wT, y, wt, ts, xm, offs, out_0, out_1):
             nc.vector.tensor_tensor(out=h_grouped[0][:, block(j), :],
                                     in0=banks[j][:].rearrange("p t i -> p i t"),
                                     in1=wt_rows[:, 0:1, :].to_broadcast([P, P, PACK]), op=MULT)
-        late = sbuf.tile([P, 6, N // 2], U32, name="late_codes", tag="late_codes", align_bytes=64)
-        xm_op[0].extend([(late[:, 5], scales_tile("xm00", N // 2)), (late[:, 0], scales_tile("xm01", N // 2))])
-        x_op.append((flat(late[:, 1:3]), scales_tile("x1", N)))
-        w_op.append((flat(late[:, 3:5]), scales_tile("w_d1", N)))
-        stages = [after_y[:, 0], after_y[:, 2]]
-        for cols in HALVES:
-            interleave(on_gpsimd, stages[0], xm_raw[0], cols)
-        quantise(h_op[0], E5M2, h_grouped[0], HALVES[0])
-        quantise_rows(0, 0, stages[0][:, HALVES[0]])
-        quantise(h_op[0], E5M2, h_grouped[0], HALVES[1])
-        quantise_rows(0, 1, stages[0][:, HALVES[1]])
-        quantise(w_op[1], E4M3, w_grouped[1], WHOLE)
-        for cols in HALVES:
-            interleave(on_scalar, stages[1], x_raw[1], cols)
-        quantise(x_op[1], E4M3, stages[1], WHOLE)
-        y_part = [target_part(1, j, banks[j]) for j in range(2)]
+        late = sbuf.tile([P, 8, N // 2], U32, name="late_codes", tag="late_codes", align_bytes=64)
+        xm_op[0].extend([(late[:, 0], scales_tile("xm00", N // 2)), (late[:, 1], scales_tile("xm01", N // 2))])
+        x_op.append((flat(late[:, 2:4]), scales_tile("x1", N)))
+        w_slot_op = [(flat(late[:, 4 + 2 * b:6 + 2 * b]), scales_tile("w_i%d" % b, N)) for b in range(B)]
+        after_y = sbuf.tile([P, 3, N // 2, PACK], BF16, name="after_y", tag="y_raw0", align_bytes=64)
+        x_stage = [after_y[:, 2], sbuf.tile([P, N // 2, PACK], BF16, name="x_stage", tag="y_part0", align_bytes=64)]
+        for half in range(2):
+            interleave(on_gpsimd, after_y[:, half], xm_raw[0][:, :, HALVES[half]], HALVES[0])
+        quantise_rows(0, 0, after_y[:, 0])
+        quantise(h_op[0], E5M2, h_grouped[0], WHOLE)
+        quantise_rows(0, 1, after_y[:, 1])
+        for half, copy in enumerate((on_gpsimd, on_scalar)):
+            interleave(copy, x_stage[half], x_raw[1][:, :, HALVES[half]], HALVES[0])
+            quantise((x_op[1][0][:, HALVES[half]], x_op[1][1][:, HALVES[half]]), E4M3, x_stage[half], HALVES[0])
+        for b in range(B):
+            turn_pairs(b, 1, banks[b], on_scalar)
+            quantise(w_slot_op[b], E4M3, w_slots[b], WHOLE)
         for c in range(PACK - 1):
             table_gradient(0, c, banks[PACK + c])
         for c in range(PACK - 1):
             scatter(0, c, banks[PACK + c])
 
-        y_part.extend(target_part(1, j, banks[2 + j]) for j in range(2, PACK))
-        a_part = [part("a_part", j) for j in range(PACK)]
-        for j in range(PACK):
-            bank = banks[(2, 3, 7, 6)[j]]
-            scores(1, j, bank)
-            nc.scalar.activation(out=a_part[j][:], in_=by_row(bank), func=COPY, scale=ts_squared[:, 1, j:j + 1])
+        xm_stage = grouped_tile("xm_stage", tag="w_slots1")
         for half in range(2):
-            interleave(on_gpsimd, stages[1], xm_raw[1], HALVES[half])
-            quantise_rows(1, half, stages[1][:, HALVES[half]])
+            interleave(on_gpsimd, xm_stage, xm_raw[1], HALVES[half])
+            quantise_rows(1, half, xm_stage[:, HALVES[half]])
         h_rows = sbuf.tile([P, PACK, N], BF16, name="h_rows", align_bytes=64)
-        for j in range(PACK):
+        sums = [banks[k] for k in (2, 1, 4, 5)]
+
+        def parts(j):
+            y_part = target_part(1, j, sums[j])
+            bank = banks[(7, 3, 0, 7)[j]]
+            scores(1, j, bank)
+            a_part = part("a_part", j)
+            nc.scalar.activation(out=a_part[:], in_=by_row(bank), func=COPY, scale=ts_squared[:, 1, j:j + 1])
+            return y_part, a_part
+
+        def weigh(j, y_part, a_part):
+            for k, term in enumerate((y_part, a_part)):
+                for t in range(PACK):
+                    nc.tensor.matmul(sums[j][:, t, :], lhsT=term[:, t, :], rhs=ident[:], start=k == 0 and t == 0,
+                                     stop=k == 1 and t == PACK - 1, is_transpose=True)
             for t in range(PACK):
-                nc.tensor.matmul(banks[t][:, j, :], lhsT=a_part[j][:, t, :], rhs=ident[:], start=True, stop=False,
-                                 is_transpose=True)
-                nc.tensor.matmul(banks[t][:, j, :], lhsT=y_part[j][:, t, :], rhs=ident[:], start=False, stop=True,
-                                 is_transpose=True)
-        for t in range(PACK):
-            bank = banks[t]
-            for cols in (HALVES if t == PACK - 1 else (WHOLE,)):
-                nc.scalar.activation(out=h_rows[:, t, cols], in_=flat(bank[:])[:, cols], func=COPY,
+                nc.scalar.activation(out=h_rows[:, t, block(j)], in_=sums[j][:, t, :], func=COPY,
                                      scale=wt_rows[:, 1, t:t + 1])
-        interleave(on_scalar, h_grouped[1], h_rows, HALVES[0])
-        interleave(on_gpsimd, h_grouped[1], h_rows, HALVES[1])
+            interleave(on_scalar if j == PACK - 1 else on_gpsimd, h_grouped[1], h_rows, block(j))
+
+        made = [parts(0)]
+        for j in range(PACK):
+            if j + 1 < PACK:
+                made.append(parts(j + 1))
+            weigh(j, *made[j])
         quantise(h_op[1], E5M2, h_grouped[1], WHOLE)
-        table_gradient(0, 3, banks[0])
-        scatter(0, 3, banks[0])
-        h_slots = [grouped_tile("h_slots%d" % b, tag="pairs%d" % b) for b in range(B)]
+        table_gradient(0, 3, sums[3])
+        scatter(0, 3, sums[3])
+        h_slots = [grouped_tile("h_slots0", tag="h_grouped1"), grouped_tile("h_slots1", tag="pairs1")]
         h_words = flat(h_grouped[0][:]).bitcast(F32)
 
         def turn_grouped(u, bank):
@@ -319,22 +335,19 @@ def tile_attend_gsq_wx_ts_kernel(tc, xT, wT, y, wt, ts, xm, offs, out_0, out_1):
             table_gradient(1, c, bank)
             scatter(1, c, bank)
 
-        turn_pairs(0, 1, banks[1])
-        quantise(w_slot_op[0], E4M3, w_slots[0], WHOLE)
-        turn_grouped(0, banks[2])
-        turn_grouped(1, banks[3])
+        turn_grouped(0, banks[1])
+        turn_grouped(1, sums[3])
         quantise(h_slot_op[0], E5M2, h_slots[0], WHOLE)
-        product_and_scatter(0, banks[4])
-        turn_rows(0, banks[0])
-        turn_rows(1, banks[1])
+        table_gradient(1, 0, banks[4])
+        staged_first = stage(1, 0, banks[4])
+        turn_rows(0, banks[1])
+        turn_rows(1, sums[3])
         quantise(h_slot_op[1], E5M2, h_slots[1], WHOLE)
-        turn_pairs(1, 0, banks[2])
-        turn_pairs(1, 1, banks[3])
-        quantise(w_slot_op[1], E4M3, w_slots[1], WHOLE)
+        place(1, 0, staged_first)
         product_and_scatter(1, banks[4])
         row_gradient(0, 0, (banks[5], banks[6]))
         row_gradient(0, 1, (banks[7], banks[0]))
-        product_and_scatter(2, banks[4])
         row_gradient(1, 0, (banks[1], banks[2]))
+        product_and_scatter(2, banks[4])
         row_gradient(1, 1, (banks[3], banks[5]))
         product_and_scatter(3, banks[4])

@@ -25,6 +25,7 @@ OFFSET_ROWS = 16
 LIST_COLS = N // OFFSET_ROWS
 TS_COLS = T // P
 CHUNK = T // 4
+ON_VECTOR = 4
 WHOLE = slice(0, N)
 HALVES = (slice(0, N // 2), slice(N // 2, N))
 
@@ -70,9 +71,9 @@ def tile_attend_gsq_wx_ts_kernel(tc, xT, wT, y, wt, ts, xm, offs, out_0, out_1):
         on_vector = nc.vector.tensor_copy
         on_scalar = nc.scalar.copy
 
-        zeros = sbuf.tile([P, P], F32, name="zeros", tag="window0")
+        zeros = sbuf.tile([P, P], F32, name="zeros", tag="window1", align_bytes=64)
         nc.gpsimd.memset(zeros[:], 0.0)
-        ts_cols = sbuf.tile([P, TS_COLS + P], F32, name="ts_cols", tag="window1")
+        ts_cols = sbuf.tile([P, TS_COLS + P], F32, name="ts_cols")
         nc.gpsimd.memset(ts_cols[:, TS_COLS:], 0.0)
         nc.sync.dma_start(out=ts_cols[:, 0:TS_COLS], in_=ts[0:1, :].rearrange("o (p c) -> (o p) c", p=P))
         ident = sbuf.tile([P, P], F32, name="ident")
@@ -80,8 +81,7 @@ def tile_attend_gsq_wx_ts_kernel(tc, xT, wT, y, wt, ts, xm, offs, out_0, out_1):
                                 pattern=[[-1, P]], channel_multiplier=1)
 
         def load_chunk(u, k):
-            tag = "window%d" % (2 + k) if u == 0 and k < 2 else "chunk%d%d" % (u, k)
-            tile = sbuf.tile([P, 2, CHUNK], F32, name="chunk%d%d" % (u, k), tag=tag)
+            tile = sbuf.tile([P, 2, CHUNK], F32, name="chunk%d%d" % (u, k), tag="chunk%d%d" % (u, k))
             nc.sync.dma_start(out=tile[:], in_=by_partition(wT)[:, 2 * u:2 * u + 2, k * CHUNK:(k + 1) * CHUNK])
             return tile
 
@@ -118,6 +118,15 @@ def tile_attend_gsq_wx_ts_kernel(tc, xT, wT, y, wt, ts, xm, offs, out_0, out_1):
                       in_=ts_bank[:].rearrange("m c p -> m p c"))
         banks = [psum.tile([P, PACK, P], F32, name="bank%d" % k, tag="bank%d" % k) for k in range(BANKS)]
 
+        windows = []
+
+        def zero_window(engine, tag):
+            windows.append(sbuf.tile([P, T], F32, name="window%d" % len(windows), tag=tag, align_bytes=64))
+            engine.memset(windows[-1][:].bitcast(I32), 0)
+
+        zero_window(nc.vector, "window0")
+        zero_window(nc.gpsimd, "window1")
+
         pairs = [sbuf.tile([P, T, 2], BF16, name="pairs%d" % u, tag="pairs%d" % u, align_bytes=64) for u in range(2)]
         listed = sbuf.tile([P, B, 2, N], U32, name="listed", tag="ts_window", align_bytes=64)
         ts_listed = sbuf.tile([P, B * N], F32, name="ts_listed")
@@ -128,7 +137,6 @@ def tile_attend_gsq_wx_ts_kernel(tc, xT, wT, y, wt, ts, xm, offs, out_0, out_1):
         h_grouped = [grouped_tile("h_grouped%d" % b) for b in range(B)]
         x_op = [operand("x0")]
         w_op = [operand("w_d%d" % b) for b in range(B)]
-        h_op = [operand("h_r%d" % b) for b in range(B)]
         xm_op = [[], [operand("xm1%d" % half, N // 2) for half in range(2)]]
         h_slot_op = [operand("h_i%d" % b) for b in range(B)]
 
@@ -185,6 +193,12 @@ def tile_attend_gsq_wx_ts_kernel(tc, xT, wT, y, wt, ts, xm, offs, out_0, out_1):
             turn_targets(b, j, bank, range(PACK))
             return scale_targets(b, j, bank)
 
+        def turn_sum(bank, terms):
+            for k, term in enumerate(terms):
+                for t in range(PACK):
+                    nc.tensor.matmul(bank[:, t, :], lhsT=term[:, t, :], rhs=ident[:], start=k == 0 and t == 0,
+                                     stop=k == len(terms) - 1 and t == PACK - 1, is_transpose=True)
+
         def scores(b, j, bank):
             product(bank, w_op[b], E4M3, j, x_op[b], E4M3)
 
@@ -215,19 +229,16 @@ def tile_attend_gsq_wx_ts_kernel(tc, xT, wT, y, wt, ts, xm, offs, out_0, out_1):
             cast_pairs(activation_copy, 0, k, 0, CHUNK)
         for b in range(B):
             gather(b, 0)
-        windows = [sbuf.tile([P, T], F32, name="window%d" % c, tag="window%d" % c) for c in range(PACK)]
-        for c in range(PACK):
-            nc.gpsimd.memset(windows[c][:].bitcast(I32), 0)
+        zero_window(nc.gpsimd, "pairs0")
         for k in range(T // CHUNK):
             cast_pairs(activation_copy, 1, k, 0, CHUNK)
         turn_pairs(0, 0, banks[6], on_vector)
         turn_pairs(1, 0, banks[7], on_scalar)
-        for k in range(PACK):
-            for j in range(2):
-                nc.tensor.transpose(banks[k][:, j, :], ts_listed[:, block(2 * k + j)], ident[:])
-            nc.scalar.activation(out=flat(minus_ts[:])[:, 2 * k:2 * k + 2], in_=banks[k][:, 0:2, 0], func=COPY,
-                                 scale=-1.0)
-        nc.gpsimd.tensor_tensor(out=ts_squared[:], in0=minus_ts[:], in1=minus_ts[:], op=MULT)
+        for b in range(B):
+            for j in range(PACK):
+                nc.tensor.transpose(banks[b][:, j, :], ts_listed[:, block(PACK * b + j)], ident[:])
+            nc.vector.tensor_scalar(out=minus_ts[:, b, :], in0=banks[b][:, :, 0], scalar1=-1.0, scalar2=None, op0=MULT)
+        nc.vector.tensor_tensor(out=ts_squared[:], in0=minus_ts[:], in1=minus_ts[:], op=MULT)
         for b in range(B):
             gather(b, 1)
         join_pairs(0, on_vector, I32)
@@ -249,29 +260,37 @@ def tile_attend_gsq_wx_ts_kernel(tc, xT, wT, y, wt, ts, xm, offs, out_0, out_1):
         y_part = [scale_targets(0, j, banks[j]) for j in range(PACK)]
         for j in range(PACK):
             scores(0, j, banks[PACK + j])
+        early = sbuf.tile([P, PACK - 1, PACK, P], F32, name="residuals", tag="x_grouped0", align_bytes=64)
         for j in range(PACK):
-            residual = part("a_part", j, "late_codes" if j == PACK - 1 else None)
-            nc.vector.scalar_tensor_tensor(out=residual[:], in0=by_row(banks[PACK + j]),
-                                           scalar=ts_squared[:, 0, j:j + 1], in1=y_part[j][:], op0=MULT, op1=ADD)
-            for t in range(PACK):
-                nc.tensor.transpose(banks[j][:, t, :], residual[:, t, :], ident[:])
+            residual = early[:, j] if j < PACK - 1 else part("residual", j, "late_codes")
+            if j < ON_VECTOR:
+                nc.vector.scalar_tensor_tensor(out=residual[:], in0=by_row(banks[PACK + j]),
+                                               scalar=ts_squared[:, 0, j:j + 1], in1=y_part[j][:], op0=MULT, op1=ADD)
+                turn_sum(banks[j], [residual])
+            else:
+                nc.scalar.activation(out=residual[:], in_=by_row(banks[PACK + j]), func=COPY,
+                                     scale=ts_squared[:, 0, j:j + 1])
+                turn_sum(banks[j], [y_part[j], residual])
         for j in range(PACK):
             nc.vector.tensor_tensor(out=h_grouped[0][:, block(j), :],
                                     in0=banks[j][:].rearrange("p t i -> p i t"),
                                     in1=wt_rows[:, 0:1, :].to_broadcast([P, P, PACK]), op=MULT)
-        late = sbuf.tile([P, 8, N // 2], U32, name="late_codes", tag="late_codes", align_bytes=64)
+        late = sbuf.tile([P, 10, N // 2], U32, name="late_codes", tag="late_codes", align_bytes=64)
         xm_op[0].extend([(late[:, 0], scales_tile("xm00", N // 2)), (late[:, 1], scales_tile("xm01", N // 2))])
         x_op.append((flat(late[:, 2:4]), scales_tile("x1", N)))
         w_slot_op = [(flat(late[:, 4 + 2 * b:6 + 2 * b]), scales_tile("w_i%d" % b, N)) for b in range(B)]
-        after_y = sbuf.tile([P, 3, N // 2, PACK], BF16, name="after_y", tag="y_raw0", align_bytes=64)
-        x_stage = [after_y[:, 2], sbuf.tile([P, N // 2, PACK], BF16, name="x_stage", tag="y_part0", align_bytes=64)]
+        h_op = [(flat(late[:, 8:10]), scales_tile("h_r0", N)), operand("h_r1")]
+        halves = [sbuf.tile([P, N // 2, PACK], BF16, name="stage%d" % j, tag="y_part%d" % j, align_bytes=64)
+                 for j in range(PACK)]
+        x_stage = halves[2:]
         for half in range(2):
-            interleave(on_gpsimd, after_y[:, half], xm_raw[0][:, :, HALVES[half]], HALVES[0])
-        quantise_rows(0, 0, after_y[:, 0])
-        quantise(h_op[0], E5M2, h_grouped[0], WHOLE)
-        quantise_rows(0, 1, after_y[:, 1])
-        for half, copy in enumerate((on_gpsimd, on_scalar)):
-            interleave(copy, x_stage[half], x_raw[1][:, :, HALVES[half]], HALVES[0])
+            interleave(on_gpsimd, halves[half], xm_raw[0][:, :, HALVES[half]], HALVES[0])
+        quantise_rows(0, 0, halves[0])
+        for cols in HALVES:
+            quantise(h_op[0], E5M2, h_grouped[0], cols)
+        quantise_rows(0, 1, halves[1])
+        for half in range(2):
+            interleave(on_scalar, x_stage[half], x_raw[1][:, :, HALVES[half]], HALVES[0])
             quantise((x_op[1][0][:, HALVES[half]], x_op[1][1][:, HALVES[half]]), E4M3, x_stage[half], HALVES[0])
         for b in range(B):
             turn_pairs(b, 1, banks[b], on_scalar)
@@ -285,6 +304,7 @@ def tile_attend_gsq_wx_ts_kernel(tc, xT, wT, y, wt, ts, xm, offs, out_0, out_1):
         for half in range(2):
             interleave(on_gpsimd, xm_stage, xm_raw[1], HALVES[half])
             quantise_rows(1, half, xm_stage[:, HALVES[half]])
+        zero_window(nc.gpsimd, "xm_raw1")
         h_rows = sbuf.tile([P, PACK, N], BF16, name="h_rows", align_bytes=64)
         sums = [banks[k] for k in (2, 1, 4, 5)]
 
@@ -297,10 +317,7 @@ def tile_attend_gsq_wx_ts_kernel(tc, xT, wT, y, wt, ts, xm, offs, out_0, out_1):
             return y_part, a_part
 
         def weigh(j, y_part, a_part):
-            for k, term in enumerate((y_part, a_part)):
-                for t in range(PACK):
-                    nc.tensor.matmul(sums[j][:, t, :], lhsT=term[:, t, :], rhs=ident[:], start=k == 0 and t == 0,
-                                     stop=k == 1 and t == PACK - 1, is_transpose=True)
+            turn_sum(sums[j], [y_part, a_part])
             for t in range(PACK):
                 nc.scalar.activation(out=h_rows[:, t, block(j)], in_=sums[j][:, t, :], func=COPY,
                                      scale=wt_rows[:, 1, t:t + 1])

@@ -25,7 +25,7 @@ OFFSET_ROWS = 16
 LIST_COLS = N // OFFSET_ROWS
 TS_COLS = T // P
 CHUNK = T // 4
-ON_VECTOR = 4
+ADDED_ON_GPSIMD = (0, 1, 2, 3)
 WHOLE = slice(0, N)
 HALVES = (slice(0, N // 2), slice(N // 2, N))
 
@@ -73,7 +73,7 @@ def tile_attend_gsq_wx_ts_kernel(tc, xT, wT, y, wt, ts, xm, offs, out_0, out_1):
 
         zeros = sbuf.tile([P, P], F32, name="zeros", tag="window1", align_bytes=64)
         nc.gpsimd.memset(zeros[:], 0.0)
-        ts_cols = sbuf.tile([P, TS_COLS + P], F32, name="ts_cols")
+        ts_cols = sbuf.tile([P, TS_COLS + P], F32, name="ts_cols", tag="window0", align_bytes=64)
         nc.gpsimd.memset(ts_cols[:, TS_COLS:], 0.0)
         nc.sync.dma_start(out=ts_cols[:, 0:TS_COLS], in_=ts[0:1, :].rearrange("o (p c) -> (o p) c", p=P))
         ident = sbuf.tile([P, P], F32, name="ident")
@@ -81,7 +81,8 @@ def tile_attend_gsq_wx_ts_kernel(tc, xT, wT, y, wt, ts, xm, offs, out_0, out_1):
                                 pattern=[[-1, P]], channel_multiplier=1)
 
         def load_chunk(u, k):
-            tile = sbuf.tile([P, 2, CHUNK], F32, name="chunk%d%d" % (u, k), tag="chunk%d%d" % (u, k))
+            tag = "window%d" % (2 + k) if u == 0 and k < 2 else "chunk%d%d" % (u, k)
+            tile = sbuf.tile([P, 2, CHUNK], F32, name="chunk%d%d" % (u, k), tag=tag, align_bytes=64)
             nc.sync.dma_start(out=tile[:], in_=by_partition(wT)[:, 2 * u:2 * u + 2, k * CHUNK:(k + 1) * CHUNK])
             return tile
 
@@ -118,15 +119,6 @@ def tile_attend_gsq_wx_ts_kernel(tc, xT, wT, y, wt, ts, xm, offs, out_0, out_1):
                       in_=ts_bank[:].rearrange("m c p -> m p c"))
         banks = [psum.tile([P, PACK, P], F32, name="bank%d" % k, tag="bank%d" % k) for k in range(BANKS)]
 
-        windows = []
-
-        def zero_window(engine, tag):
-            windows.append(sbuf.tile([P, T], F32, name="window%d" % len(windows), tag=tag, align_bytes=64))
-            engine.memset(windows[-1][:].bitcast(I32), 0)
-
-        zero_window(nc.vector, "window0")
-        zero_window(nc.gpsimd, "window1")
-
         pairs = [sbuf.tile([P, T, 2], BF16, name="pairs%d" % u, tag="pairs%d" % u, align_bytes=64) for u in range(2)]
         listed = sbuf.tile([P, B, 2, N], U32, name="listed", tag="ts_window", align_bytes=64)
         ts_listed = sbuf.tile([P, B * N], F32, name="ts_listed")
@@ -137,8 +129,7 @@ def tile_attend_gsq_wx_ts_kernel(tc, xT, wT, y, wt, ts, xm, offs, out_0, out_1):
         h_grouped = [grouped_tile("h_grouped%d" % b) for b in range(B)]
         x_op = [operand("x0")]
         w_op = [operand("w_d%d" % b) for b in range(B)]
-        xm_op = [[], [operand("xm1%d" % half, N // 2) for half in range(2)]]
-        h_slot_op = [operand("h_i%d" % b) for b in range(B)]
+        xm_op = [[], []]
 
         def cast_pairs(copy, u, k, first, last):
             copy(out=pairs[u][:, k * CHUNK + first:k * CHUNK + last, :],
@@ -193,11 +184,16 @@ def tile_attend_gsq_wx_ts_kernel(tc, xT, wT, y, wt, ts, xm, offs, out_0, out_1):
             turn_targets(b, j, bank, range(PACK))
             return scale_targets(b, j, bank)
 
-        def turn_sum(bank, terms):
-            for k, term in enumerate(terms):
-                for t in range(PACK):
-                    nc.tensor.matmul(bank[:, t, :], lhsT=term[:, t, :], rhs=ident[:], start=k == 0 and t == 0,
-                                     stop=k == len(terms) - 1 and t == PACK - 1, is_transpose=True)
+        def turn_part(bank, term):
+            for t in range(PACK):
+                nc.tensor.transpose(bank[:, t, :], term[:, t, :], ident[:])
+
+        def turn_sum(bank, first, second):
+            for t in range(PACK):
+                nc.tensor.matmul(bank[:, t, :], lhsT=first[:, t, :], rhs=ident[:], start=True, stop=False,
+                                 is_transpose=True)
+                nc.tensor.matmul(bank[:, t, :], lhsT=second[:, t, :], rhs=ident[:], start=False, stop=True,
+                                 is_transpose=True)
 
         def scores(b, j, bank):
             product(bank, w_op[b], E4M3, j, x_op[b], E4M3)
@@ -229,7 +225,9 @@ def tile_attend_gsq_wx_ts_kernel(tc, xT, wT, y, wt, ts, xm, offs, out_0, out_1):
             cast_pairs(activation_copy, 0, k, 0, CHUNK)
         for b in range(B):
             gather(b, 0)
-        zero_window(nc.gpsimd, "pairs0")
+        windows = [sbuf.tile([P, T], F32, name="window%d" % c, tag="window%d" % c, align_bytes=64) for c in range(PACK)]
+        for c in (1, 2, 0, 3):
+            nc.gpsimd.memset(windows[c][:].bitcast(I32), 0)
         for k in range(T // CHUNK):
             cast_pairs(activation_copy, 1, k, 0, CHUNK)
         turn_pairs(0, 0, banks[6], on_vector)
@@ -249,9 +247,11 @@ def tile_attend_gsq_wx_ts_kernel(tc, xT, wT, y, wt, ts, xm, offs, out_0, out_1):
         w_grouped.append(grouped_tile("w_grouped1", tag="x_grouped0"))
         join_pairs(1, on_vector, I32)
         quantise(w_op[1], E4M3, w_grouped[1], WHOLE)
-        dw = [[sbuf.tile([P, 2, N], F32, name="dw%d" % b, tag="chunk0%d" % (2 * b + k)) for k in range(2)]
+        dw = [[sbuf.tile([P, 2, N], F32, name="dw%d" % b, tag="chunk0%d" % (2 * b + k), align_bytes=64)
+               for k in range(2)]
               for b in range(B)]
-        gx = [[sbuf.tile([P, 2, N], F32, name="gx%d" % b, tag="chunk1%d" % (2 * b + k)) for k in range(2)]
+        gx = [[sbuf.tile([P, 2, N], F32, name="gx%d" % b, tag="chunk1%d" % (2 * b + k), align_bytes=64)
+               for k in range(2)]
               for b in range(B)]
 
         for rows in (range(0, 2), range(2, PACK)):
@@ -263,28 +263,23 @@ def tile_attend_gsq_wx_ts_kernel(tc, xT, wT, y, wt, ts, xm, offs, out_0, out_1):
         early = sbuf.tile([P, PACK - 1, PACK, P], F32, name="residuals", tag="x_grouped0", align_bytes=64)
         for j in range(PACK):
             residual = early[:, j] if j < PACK - 1 else part("residual", j, "late_codes")
-            if j < ON_VECTOR:
-                nc.vector.scalar_tensor_tensor(out=residual[:], in0=by_row(banks[PACK + j]),
-                                               scalar=ts_squared[:, 0, j:j + 1], in1=y_part[j][:], op0=MULT, op1=ADD)
-                turn_sum(banks[j], [residual])
-            else:
-                nc.scalar.activation(out=residual[:], in_=by_row(banks[PACK + j]), func=COPY,
-                                     scale=ts_squared[:, 0, j:j + 1])
-                turn_sum(banks[j], [y_part[j], residual])
+            nc.vector.scalar_tensor_tensor(out=residual[:], in0=by_row(banks[PACK + j]),
+                                           scalar=ts_squared[:, 0, j:j + 1], in1=y_part[j][:], op0=MULT, op1=ADD)
+            turn_part(banks[j], residual)
         for j in range(PACK):
             nc.vector.tensor_tensor(out=h_grouped[0][:, block(j), :],
                                     in0=banks[j][:].rearrange("p t i -> p i t"),
                                     in1=wt_rows[:, 0:1, :].to_broadcast([P, P, PACK]), op=MULT)
-        late = sbuf.tile([P, 10, N // 2], U32, name="late_codes", tag="late_codes", align_bytes=64)
+        late = sbuf.tile([P, 8, N // 2], U32, name="late_codes", tag="late_codes", align_bytes=64)
         xm_op[0].extend([(late[:, 0], scales_tile("xm00", N // 2)), (late[:, 1], scales_tile("xm01", N // 2))])
         x_op.append((flat(late[:, 2:4]), scales_tile("x1", N)))
-        w_slot_op = [(flat(late[:, 4 + 2 * b:6 + 2 * b]), scales_tile("w_i%d" % b, N)) for b in range(B)]
-        h_op = [(flat(late[:, 8:10]), scales_tile("h_r0", N)), operand("h_r1")]
-        halves = [sbuf.tile([P, N // 2, PACK], BF16, name="stage%d" % j, tag="y_part%d" % j, align_bytes=64)
-                 for j in range(PACK)]
+        w_slot_op = [(flat(late[:, 4:6]), scales_tile("w_i0", N))]
+        h_op = [(flat(late[:, 6:8]), scales_tile("h_r0", N)), operand("h_r1")]
+        halves = [sbuf.tile([P, N // 2, PACK], BF16, name="stage%d" % j, tag="y_raw0" if j == 1 else "y_part%d" % j,
+                            align_bytes=64) for j in range(PACK)]
         x_stage = halves[2:]
-        for half in range(2):
-            interleave(on_gpsimd, halves[half], xm_raw[0][:, :, HALVES[half]], HALVES[0])
+        for half, copy in enumerate((on_gpsimd, on_scalar)):
+            interleave(copy, halves[half], xm_raw[0][:, :, HALVES[half]], HALVES[0])
         quantise_rows(0, 0, halves[0])
         for cols in HALVES:
             quantise(h_op[0], E5M2, h_grouped[0], cols)
@@ -292,19 +287,16 @@ def tile_attend_gsq_wx_ts_kernel(tc, xT, wT, y, wt, ts, xm, offs, out_0, out_1):
         for half in range(2):
             interleave(on_scalar, x_stage[half], x_raw[1][:, :, HALVES[half]], HALVES[0])
             quantise((x_op[1][0][:, HALVES[half]], x_op[1][1][:, HALVES[half]]), E4M3, x_stage[half], HALVES[0])
-        for b in range(B):
-            turn_pairs(b, 1, banks[b], on_scalar)
-            quantise(w_slot_op[b], E4M3, w_slots[b], WHOLE)
+        turn_pairs(0, 1, banks[0], on_scalar)
+        quantise(w_slot_op[0], E4M3, w_slots[0], WHOLE)
         for c in range(PACK - 1):
             table_gradient(0, c, banks[PACK + c])
         for c in range(PACK - 1):
             scatter(0, c, banks[PACK + c])
 
-        xm_stage = grouped_tile("xm_stage", tag="w_slots1")
+        xm_stage = grouped_tile("xm_stage", tag="w_slots0")
         for half in range(2):
             interleave(on_gpsimd, xm_stage, xm_raw[1], HALVES[half])
-            quantise_rows(1, half, xm_stage[:, HALVES[half]])
-        zero_window(nc.gpsimd, "xm_raw1")
         h_rows = sbuf.tile([P, PACK, N], BF16, name="h_rows", align_bytes=64)
         sums = [banks[k] for k in (2, 1, 4, 5)]
 
@@ -317,21 +309,27 @@ def tile_attend_gsq_wx_ts_kernel(tc, xT, wT, y, wt, ts, xm, offs, out_0, out_1):
             return y_part, a_part
 
         def weigh(j, y_part, a_part):
-            turn_sum(sums[j], [y_part, a_part])
+            if j in ADDED_ON_GPSIMD:
+                nc.gpsimd.tensor_tensor(out=a_part[:], in0=a_part[:], in1=y_part[:], op=ADD)
+                turn_part(sums[j], a_part)
+            else:
+                turn_sum(sums[j], y_part, a_part)
             for t in range(PACK):
                 nc.scalar.activation(out=h_rows[:, t, block(j)], in_=sums[j][:, t, :], func=COPY,
                                      scale=wt_rows[:, 1, t:t + 1])
-            interleave(on_scalar if j == PACK - 1 else on_gpsimd, h_grouped[1], h_rows, block(j))
+            interleave(on_gpsimd, h_grouped[1], h_rows, block(j))
 
-        made = [parts(0)]
+        made = [parts(j) for j in range(PACK)]
+        turn_pairs(1, 1, banks[6], on_scalar)
+        table_gradient(0, 3, banks[6])
+        scatter(0, 3, banks[6])
+        xm_op[1].append((sbuf.tile([P, N // 2], U32, name="xm10_codes", tag="chunk01", align_bytes=64),
+                         scales_tile("xm10", N // 2)))
+        quantise_rows(1, 0, xm_stage[:, HALVES[0]])
         for j in range(PACK):
-            if j + 1 < PACK:
-                made.append(parts(j + 1))
             weigh(j, *made[j])
         quantise(h_op[1], E5M2, h_grouped[1], WHOLE)
-        table_gradient(0, 3, sums[3])
-        scatter(0, 3, sums[3])
-        h_slots = [grouped_tile("h_slots0", tag="h_grouped1"), grouped_tile("h_slots1", tag="pairs1")]
+        h_slots = [grouped_tile("h_slots0", tag="pairs0"), grouped_tile("h_slots1", tag="pairs1")]
         h_words = flat(h_grouped[0][:]).bitcast(F32)
 
         def turn_grouped(u, bank):
@@ -352,19 +350,25 @@ def tile_attend_gsq_wx_ts_kernel(tc, xT, wT, y, wt, ts, xm, offs, out_0, out_1):
             table_gradient(1, c, bank)
             scatter(1, c, bank)
 
-        turn_grouped(0, banks[1])
-        turn_grouped(1, sums[3])
-        quantise(h_slot_op[0], E5M2, h_slots[0], WHOLE)
         table_gradient(1, 0, banks[4])
         staged_first = stage(1, 0, banks[4])
-        turn_rows(0, banks[1])
-        turn_rows(1, sums[3])
+        last = sbuf.tile([P, 7, N // 2], U32, name="last_codes", tag="h_grouped1", align_bytes=64)
+        xm_op[1].append((last[:, 0], scales_tile("xm11", N // 2)))
+        h_slot_op = [(flat(last[:, 1 + 2 * b:3 + 2 * b]), scales_tile("h_i%d" % b, N)) for b in range(B)]
+        w_slot_op.append((flat(last[:, 5:7]), scales_tile("w_i1", N)))
+        turn_grouped(0, banks[3])
+        turn_grouped(1, banks[0])
+        quantise(h_slot_op[0], E5M2, h_slots[0], WHOLE)
+        quantise_rows(1, 1, xm_stage[:, HALVES[1]])
+        quantise(w_slot_op[1], E4M3, w_slots[1], WHOLE)
+        turn_rows(0, banks[7])
+        turn_rows(1, banks[6])
         quantise(h_slot_op[1], E5M2, h_slots[1], WHOLE)
         place(1, 0, staged_first)
-        product_and_scatter(1, banks[4])
-        row_gradient(0, 0, (banks[5], banks[6]))
-        row_gradient(0, 1, (banks[7], banks[0]))
-        row_gradient(1, 0, (banks[1], banks[2]))
+        product_and_scatter(1, banks[5])
+        row_gradient(0, 0, (banks[2], banks[1]))
+        row_gradient(0, 1, (banks[5], banks[3]))
+        row_gradient(1, 0, (banks[0], banks[7]))
         product_and_scatter(2, banks[4])
-        row_gradient(1, 1, (banks[3], banks[5]))
+        row_gradient(1, 1, (banks[6], banks[2]))
         product_and_scatter(3, banks[4])

@@ -25,7 +25,7 @@ OFFSET_ROWS = 16
 LIST_COLS = N // OFFSET_ROWS
 TS_COLS = T // P
 CHUNK = T // 4
-ADDED_ON_GPSIMD = (0, 1, 2, 3)
+ADDED_ON_GPSIMD = (1, 2, 3)
 WHOLE = slice(0, N)
 HALVES = (slice(0, N // 2), slice(N // 2, N))
 
@@ -56,7 +56,12 @@ def tile_attend_gsq_wx_ts_kernel(tc, xT, wT, y, wt, ts, xm, offs, out_0, out_1):
             return codes, scales_tile(name, width)
 
         def interleave(copy, grouped, rows, cols):
-            copy(out=grouped[:, cols, :], in_=rows[:, :, cols].rearrange("p t c -> p c t"))
+            copy(out=grouped[:, cols, :].rearrange("p (c i) t -> p c t i", i=PACK),
+                 in_=rows[:, :, cols].rearrange("p t (c i) -> p c t i", i=PACK))
+
+        def interleave_on_gpsimd(grouped, rows, cols):
+            nc.gpsimd.tensor_scalar(out=grouped[:, cols, :], in0=rows[:, :, cols].rearrange("p t c -> p c t"),
+                                    scalar1=1.0, scalar2=0.0, op0=MULT, op1=ADD)
 
         def quantise(op, fmt, grouped, cols):
             nc.vector.quantize_mx(out=op[0][:, cols].bitcast(fmt), scales=op[1][:, cols],
@@ -71,18 +76,20 @@ def tile_attend_gsq_wx_ts_kernel(tc, xT, wT, y, wt, ts, xm, offs, out_0, out_1):
         on_vector = nc.vector.tensor_copy
         on_scalar = nc.scalar.copy
 
-        zeros = sbuf.tile([P, P], F32, name="zeros", tag="window1", align_bytes=64)
-        nc.gpsimd.memset(zeros[:], 0.0)
-        ts_cols = sbuf.tile([P, TS_COLS + P], F32, name="ts_cols", tag="window0", align_bytes=64)
+        zeros = [sbuf.tile([P, P // 2], F32, name="zeros", tag="window%d" % c, align_bytes=64) for c in (1, 3)]
+        for half in range(2):
+            nc.gpsimd.memset(zeros[half][:], 0.0)
+        ts_cols = sbuf.tile([P, TS_COLS + P], F32, name="ts_cols")
         nc.gpsimd.memset(ts_cols[:, TS_COLS:], 0.0)
         nc.sync.dma_start(out=ts_cols[:, 0:TS_COLS], in_=ts[0:1, :].rearrange("o (p c) -> (o p) c", p=P))
         ident = sbuf.tile([P, P], F32, name="ident")
-        nc.gpsimd.affine_select(out=ident[:], in_=zeros[:], compare_op=NOT_EQUAL, fill=1.0, base=0,
-                                pattern=[[-1, P]], channel_multiplier=1)
+        for half in range(2):
+            nc.gpsimd.affine_select(out=ident[:, half * P // 2:(half + 1) * P // 2], in_=zeros[half][:],
+                                    pattern=[[-1, P // 2]], compare_op=NOT_EQUAL, fill=1.0,
+                                    base=-half * (P // 2), channel_multiplier=1)
 
         def load_chunk(u, k):
-            tag = "window%d" % (2 + k) if u == 0 and k < 2 else "chunk%d%d" % (u, k)
-            tile = sbuf.tile([P, 2, CHUNK], F32, name="chunk%d%d" % (u, k), tag=tag, align_bytes=64)
+            tile = sbuf.tile([P, 2, CHUNK], F32, name="chunk%d%d" % (u, k), tag="chunk%d%d" % (u, k), align_bytes=64)
             nc.sync.dma_start(out=tile[:], in_=by_partition(wT)[:, 2 * u:2 * u + 2, k * CHUNK:(k + 1) * CHUNK])
             return tile
 
@@ -138,9 +145,6 @@ def tile_attend_gsq_wx_ts_kernel(tc, xT, wT, y, wt, ts, xm, offs, out_0, out_1):
         def activation_copy(out, in_):
             nc.scalar.activation(out=out, in_=in_, func=COPY)
 
-        def on_gpsimd(out, in_):
-            nc.gpsimd.tensor_scalar(out=out, in0=in_, scalar1=1.0, scalar2=0.0, op0=MULT, op1=ADD)
-
         def gather(b, u):
             nc.vector.tensor_copy(listed[:, b, u, :],
                                   flat(pairs[u][:]).bitcast(U32).indirect(offsets[:, b * LIST_COLS:(b + 1) * LIST_COLS]))
@@ -156,8 +160,8 @@ def tile_attend_gsq_wx_ts_kernel(tc, xT, wT, y, wt, ts, xm, offs, out_0, out_1):
         def turn_pairs(b, u, bank, copy):
             words = listed[:, b, u, :].bitcast(F32)
             turn_words([words[:, s:N:PACK] for s in range(PACK)], bank)
-            copy(out=w_slots[b][:, HALVES[u], :].rearrange("p (m e) s -> p m e s", e=2),
-                 in_=flat(bank[:]).bitcast(BF16).rearrange("p (s m e) -> p m e s", s=PACK, e=2))
+            copy(out=w_slots[b][:, HALVES[u], :].rearrange("p (a k) s -> p a s k", k=PACK),
+                 in_=flat(bank[:]).bitcast(BF16).rearrange("p (s a k) -> p a s k", s=PACK, k=PACK))
 
         def quantise_rows(b, half, stage):
             quantise(xm_op[b][half], E4M3, stage, slice(0, N // 2))
@@ -225,9 +229,10 @@ def tile_attend_gsq_wx_ts_kernel(tc, xT, wT, y, wt, ts, xm, offs, out_0, out_1):
             cast_pairs(activation_copy, 0, k, 0, CHUNK)
         for b in range(B):
             gather(b, 0)
-        windows = [sbuf.tile([P, T], F32, name="window%d" % c, tag="window%d" % c, align_bytes=64) for c in range(PACK)]
-        for c in (1, 2, 0, 3):
-            nc.gpsimd.memset(windows[c][:].bitcast(I32), 0)
+        windows = [sbuf.tile([P, T], F32, name="window%d" % c, tag="pairs0" if c == 2 else "window%d" % c,
+                             align_bytes=64) for c in range(PACK)]
+        for c in range(PACK):
+            (nc.vector if c == 0 else nc.gpsimd).memset(windows[c][:].bitcast(I32), 0)
         for k in range(T // CHUNK):
             cast_pairs(activation_copy, 1, k, 0, CHUNK)
         turn_pairs(0, 0, banks[6], on_vector)
@@ -278,8 +283,8 @@ def tile_attend_gsq_wx_ts_kernel(tc, xT, wT, y, wt, ts, xm, offs, out_0, out_1):
         halves = [sbuf.tile([P, N // 2, PACK], BF16, name="stage%d" % j, tag="y_raw0" if j == 1 else "y_part%d" % j,
                             align_bytes=64) for j in range(PACK)]
         x_stage = halves[2:]
-        for half, copy in enumerate((on_gpsimd, on_scalar)):
-            interleave(copy, halves[half], xm_raw[0][:, :, HALVES[half]], HALVES[0])
+        interleave_on_gpsimd(halves[0], xm_raw[0][:, :, HALVES[0]], HALVES[0])
+        interleave(on_scalar, halves[1], xm_raw[0][:, :, HALVES[1]], HALVES[0])
         quantise_rows(0, 0, halves[0])
         for cols in HALVES:
             quantise(h_op[0], E5M2, h_grouped[0], cols)
@@ -296,7 +301,7 @@ def tile_attend_gsq_wx_ts_kernel(tc, xT, wT, y, wt, ts, xm, offs, out_0, out_1):
 
         xm_stage = grouped_tile("xm_stage", tag="w_slots0")
         for half in range(2):
-            interleave(on_gpsimd, xm_stage, xm_raw[1], HALVES[half])
+            interleave_on_gpsimd(xm_stage, xm_raw[1], HALVES[half])
         h_rows = sbuf.tile([P, PACK, N], BF16, name="h_rows", align_bytes=64)
         sums = [banks[k] for k in (2, 1, 4, 5)]
 
@@ -317,7 +322,7 @@ def tile_attend_gsq_wx_ts_kernel(tc, xT, wT, y, wt, ts, xm, offs, out_0, out_1):
             for t in range(PACK):
                 nc.scalar.activation(out=h_rows[:, t, block(j)], in_=sums[j][:, t, :], func=COPY,
                                      scale=wt_rows[:, 1, t:t + 1])
-            interleave(on_gpsimd, h_grouped[1], h_rows, block(j))
+            interleave_on_gpsimd(h_grouped[1], h_rows, block(j))
 
         made = [parts(j) for j in range(PACK)]
         turn_pairs(1, 1, banks[6], on_scalar)
@@ -329,13 +334,13 @@ def tile_attend_gsq_wx_ts_kernel(tc, xT, wT, y, wt, ts, xm, offs, out_0, out_1):
         for j in range(PACK):
             weigh(j, *made[j])
         quantise(h_op[1], E5M2, h_grouped[1], WHOLE)
-        h_slots = [grouped_tile("h_slots0", tag="pairs0"), grouped_tile("h_slots1", tag="pairs1")]
+        h_slots = [grouped_tile("h_slots0"), grouped_tile("h_slots1", tag="pairs1")]
         h_words = flat(h_grouped[0][:]).bitcast(F32)
 
         def turn_grouped(u, bank):
             turn_words([h_words[:, 2 * s + u:2 * N:2 * PACK] for s in range(PACK)], bank)
-            on_scalar(out=h_slots[0][:, HALVES[u], :].rearrange("p (e m) s -> p e m s", e=2),
-                      in_=flat(bank[:]).bitcast(BF16).rearrange("p (s m e) -> p e m s", s=PACK, e=2))
+            on_scalar(out=h_slots[0][:, HALVES[u], :].rearrange("p (e a b) s -> p a s b e", e=2, b=2),
+                      in_=flat(bank[:]).bitcast(BF16).rearrange("p (s a b e) -> p a s b e", s=PACK, b=2, e=2))
 
         def turn_rows(half, bank):
             for t in range(2):

@@ -22,10 +22,8 @@ N = 512
 T = 2048
 BANKS = 8
 OFFSET_ROWS = 16
-LIST_COLS = N // OFFSET_ROWS
-TS_COLS = T // P
-CHUNK = T // 4
-ADDED_ON_GPSIMD = (1, 2, 3)
+WORDS = N // 2
+WHOLE_PACK = slice(0, PACK)
 WHOLE = slice(0, N)
 HALVES = (slice(0, N // 2), slice(N // 2, N))
 
@@ -36,344 +34,316 @@ def tile_attend_gsq_wx_ts_kernel(tc, xT, wT, y, wt, ts, xm, offs, out_0, out_1):
         sbuf = ctx.enter_context(tc.tile_pool(name="sbuf", bufs=1))
         psum = ctx.enter_context(tc.psum_pool(name="psum", bufs=1))
 
+        def tile(shape, dtype, name, tag=None):
+            return sbuf.tile(shape, dtype, name=name, tag=tag or name, align_bytes=64)
+
         def flat(ap):
             return ap.rearrange("p a c -> p (a c)")
 
-        def block(k):
-            return slice(k * P, (k + 1) * P)
+        def block(k, width=P):
+            return slice(k * width, (k + 1) * width)
 
         def by_partition(rows):
             return rows.rearrange("(p t) c -> p t c", t=PACK)
 
-        def grouped_tile(name, tag=None):
-            return sbuf.tile([P, N, PACK], BF16, name=name, tag=tag or name, align_bytes=64)
+        def values(name, tag=None):
+            return tile([P, PACK * N], BF16, name, tag)
 
-        def scales_tile(name, width):
-            return sbuf.tile([P, width], U8, name=name + "_scales", align_bytes=64)
+        def half_values(name, tag=None):
+            return tile([P, PACK * N // 2], BF16, name, tag)
 
-        def operand(name, width=N):
-            codes = sbuf.tile([P, width], U32, name=name + "_codes", tag=name + "_codes", align_bytes=64)
-            return codes, scales_tile(name, width)
+        def half_of(op, half):
+            return op[0][:, HALVES[half]], op[1][:, HALVES[half]]
 
-        def interleave(copy, grouped, rows, cols):
-            copy(out=grouped[:, cols, :].rearrange("p (c i) t -> p c t i", i=PACK),
-                 in_=rows[:, :, cols].rearrange("p t (c i) -> p c t i", i=PACK))
+        def operand(name, width=N, codes=None):
+            codes = tile([P, width], U32, name + "_codes")[:] if codes is None else codes
+            return codes, tile([P, width], U8, name + "_scales")[:]
 
-        def interleave_on_gpsimd(grouped, rows, cols):
-            nc.gpsimd.tensor_scalar(out=grouped[:, cols, :], in0=rows[:, :, cols].rearrange("p t c -> p c t"),
-                                    scalar1=1.0, scalar2=0.0, op0=MULT, op1=ADD)
+        def entries(b, cols):
+            return offsets[:, (b * N + cols.start) // OFFSET_ROWS:(b * N + cols.stop) // OFFSET_ROWS]
 
-        def quantise(op, fmt, grouped, cols):
-            nc.vector.quantize_mx(out=op[0][:, cols].bitcast(fmt), scales=op[1][:, cols],
-                                  in_=flat(grouped[:, cols, :]))
-
-        def product(bank, still, still_fmt, k, moving, moving_fmt):
-            nc.tensor.matmul_mx(out=flat(bank[:]),
-                                lhsT=still[0][:, block(k)].bitcast(still_fmt), lhsT_scale=still[1][:, block(k)],
-                                rhs=moving[0][:].bitcast(moving_fmt), rhs_scale=moving[1][:],
-                                start=True, stop=True)
-
-        on_vector = nc.vector.tensor_copy
-        on_scalar = nc.scalar.copy
-
-        zeros = [sbuf.tile([P, P // 2], F32, name="zeros", tag="window%d" % c, align_bytes=64) for c in (1, 3)]
-        for half in range(2):
-            nc.gpsimd.memset(zeros[half][:], 0.0)
-        ts_cols = sbuf.tile([P, TS_COLS + P], F32, name="ts_cols")
-        nc.gpsimd.memset(ts_cols[:, TS_COLS:], 0.0)
-        nc.sync.dma_start(out=ts_cols[:, 0:TS_COLS], in_=ts[0:1, :].rearrange("o (p c) -> (o p) c", p=P))
-        ident = sbuf.tile([P, P], F32, name="ident")
-        for half in range(2):
-            nc.gpsimd.affine_select(out=ident[:, half * P // 2:(half + 1) * P // 2], in_=zeros[half][:],
-                                    pattern=[[-1, P // 2]], compare_op=NOT_EQUAL, fill=1.0,
-                                    base=-half * (P // 2), channel_multiplier=1)
-
-        def load_chunk(u, k):
-            tile = sbuf.tile([P, 2, CHUNK], F32, name="chunk%d%d" % (u, k), tag="chunk%d%d" % (u, k), align_bytes=64)
-            nc.sync.dma_start(out=tile[:], in_=by_partition(wT)[:, 2 * u:2 * u + 2, k * CHUNK:(k + 1) * CHUNK])
-            return tile
-
-        def load(src, name):
-            raw = sbuf.tile([P, PACK, N], F32, name=name, tag=name, align_bytes=64)
-            nc.sync.dma_start(out=raw[:], in_=by_partition(src))
-            return raw
-
-        chunks = {(0, 0): load_chunk(0, 0)}
-        offsets = sbuf.tile([P, B * LIST_COLS], U16, name="offsets")
-        nc.sync.dma_start(offsets[:], offs)
-        for u in range(2):
-            for k in range(T // CHUNK):
-                if (u, k) not in chunks:
-                    chunks[u, k] = load_chunk(u, k)
-        x_raw = [load(xT[0], "x_raw0")]
-        y_raw = [sbuf.tile([P, PACK, N], F32, name="y_raw0", tag="y_raw0", align_bytes=64)]
-        for rows in (slice(0, 2), slice(2, PACK)):
-            nc.sync.dma_start(out=y_raw[0][:, rows, :], in_=by_partition(y[0])[:, rows, :])
-        wt_rows = sbuf.tile([P, B, PACK], F32, name="wt_rows")
-        nc.sync.dma_start(out=wt_rows[:], in_=wt.rearrange("b (p t) o -> p b (t o)", t=PACK))
-        xm_raw = [load(xm[0], "xm_raw0")]
-        x_raw.append(load(xT[1], "x_raw1"))
-        y_raw.append(load(y[1], "y_raw1"))
-        xm_raw.append(load(xm[1], "xm_raw1"))
-
-        ts_window = sbuf.tile([P, T], F32, name="ts_window", tag="ts_window", align_bytes=64)
-        for k in range(PACK):
-            ts_bank = psum.tile([P, PACK, P], F32, name="ts_bank", tag="bank%d" % k)
-            for c in range(PACK):
-                col = PACK * k + c
-                nc.tensor.transpose(ts_bank[:, c, :], ts_cols[:, col:col + P], ident[:])
-            on_vector(out=ts_window[:].rearrange("m (p c) -> m p c", p=P)[:, :, PACK * k:PACK * (k + 1)],
-                      in_=ts_bank[:].rearrange("m c p -> m p c"))
-        banks = [psum.tile([P, PACK, P], F32, name="bank%d" % k, tag="bank%d" % k) for k in range(BANKS)]
-
-        pairs = [sbuf.tile([P, T, 2], BF16, name="pairs%d" % u, tag="pairs%d" % u, align_bytes=64) for u in range(2)]
-        listed = sbuf.tile([P, B, 2, N], U32, name="listed", tag="ts_window", align_bytes=64)
-        ts_listed = sbuf.tile([P, B * N], F32, name="ts_listed")
-        minus_ts = sbuf.tile([P, B, PACK], F32, name="minus_ts")
-        ts_squared = sbuf.tile([P, B, PACK], F32, name="ts_squared")
-        w_grouped = [grouped_tile("w_grouped0")]
-        w_slots = [grouped_tile("w_slots%d" % b) for b in range(B)]
-        h_grouped = [grouped_tile("h_grouped%d" % b) for b in range(B)]
-        x_op = [operand("x0")]
-        w_op = [operand("w_d%d" % b) for b in range(B)]
-        xm_op = [[], []]
-
-        def cast_pairs(copy, u, k, first, last):
-            copy(out=pairs[u][:, k * CHUNK + first:k * CHUNK + last, :],
-                 in_=chunks[u, k][:, :, first:last].rearrange("p e c -> p c e"))
+        def copy_on_gpsimd(out, in_):
+            nc.gpsimd.tensor_scalar(out=out, in0=in_, scalar1=1.0, scalar2=0.0, op0=MULT, op1=ADD)
 
         def activation_copy(out, in_):
             nc.scalar.activation(out=out, in_=in_, func=COPY)
 
-        def gather(b, u):
-            nc.vector.tensor_copy(listed[:, b, u, :],
-                                  flat(pairs[u][:]).bitcast(U32).indirect(offsets[:, b * LIST_COLS:(b + 1) * LIST_COLS]))
+        on_vector = nc.vector.tensor_copy
+        on_scalar = nc.scalar.copy
 
-        def join_pairs(b, copy, word):
-            copy(out=flat(w_grouped[b][:]).bitcast(word).rearrange("p (c u) -> p c u", u=2),
-                 in_=listed[:, b].bitcast(word).rearrange("p u c -> p c u"))
+        def interleave(copy, grouped, rows, cols):
+            copy(out=grouped.rearrange("p (c t) -> p c t", t=PACK)[:, cols, :],
+                 in_=rows.rearrange("p t c -> p c t"))
 
-        def turn_words(words, bank):
+        def quantise(op, fmt, grouped, cols):
+            nc.vector.quantize_mx(out=op[0][:, cols].bitcast(fmt), scales=op[1][:, cols],
+                                  in_=grouped[:, PACK * cols.start:PACK * cols.stop])
+
+        def product(bank, still, still_fmt, k, moving, moving_fmt):
+            nc.tensor.matmul_mx(out=flat(bank[:]),
+                                lhsT=still[0][:, block(k)].bitcast(still_fmt), lhsT_scale=still[1][:, block(k)],
+                                rhs=moving[0].bitcast(moving_fmt), rhs_scale=moving[1],
+                                start=True, stop=True)
+
+        zeros = tile([P, P], F32, "zeros", "window0")
+        nc.vector.memset(zeros[:], 0.0)
+        ts_window = tile([P, T], F32, "ts_window")
+        nc.scalar.dma_start(out=ts_window[P - 1:P, :], in_=ts[0:1, :])
+        wt_rows = tile([P, B, PACK], F32, "wt_rows")
+        nc.scalar.dma_start(out=wt_rows[:], in_=wt.rearrange("b (p t) o -> p b (t o)", t=PACK))
+        ident = tile([P, P], F32, "ident")
+        nc.gpsimd.affine_select(out=ident[:], in_=zeros[:], pattern=[[-1, P]], compare_op=NOT_EQUAL, fill=1.0,
+                                base=0, channel_multiplier=1)
+        nc.gpsimd.memset(ts_window[0:P - 1, :].bitcast(I32), 0)
+
+        def load_plane(t):
+            plane = tile([P, T], F32, "plane%d" % t)
+            nc.sync.dma_start(out=plane[:], in_=by_partition(wT)[:, t, :])
+            return plane
+
+        def load(src, name, rows=WHOLE_PACK, cols=WHOLE):
+            raw = tile([P, rows.stop - rows.start, cols.stop - cols.start], F32, name)
+            nc.sync.dma_start(out=raw[:], in_=by_partition(src)[:, rows, cols])
+            return raw
+
+        def load_targets(b):
+            return [load(y[b], "y_raw%d%d" % (b, k), rows=block(k, 2)) for k in range(2)]
+
+        offsets = sbuf.tile([P, B * N // OFFSET_ROWS], U16, name="offsets")
+        nc.sync.dma_start(offsets[:], offs)
+        planes = [load_plane(t) for t in range(PACK)]
+        x_first = [load(xT[0], "x_raw0%d" % k, cols=HALVES[k]) for k in range(2)]
+        y_raw = [load_targets(0)]
+        x_second = load(xT[1], "x_raw1")
+        xm_raw = [[load(xm[0], "xm_raw00", cols=HALVES[0])]]
+        y_raw.append(load_targets(1))
+        xm_raw[0].append(load(xm[0], "xm_raw01", cols=HALVES[1]))
+        xm_raw.append([load(xm[1], "xm_raw1%d" % k, cols=HALVES[k]) for k in range(2)])
+
+        windows = [tile([P, T], F32, "window%d" % c) for c in range(PACK)]
+        for c in range(PACK):
+            nc.gpsimd.memset(windows[c][:].bitcast(I32), 0)
+        banks = [psum.tile([P, PACK, P], F32, name="bank%d" % k, tag="bank%d" % k) for k in range(BANKS)]
+
+        listed = [values("listed%d" % b) for b in range(B)]
+        h_rows = [values("h_rows%d" % b) for b in range(B)]
+        ts_listed = tile([P, B * N], F32, "ts_listed")
+        minus_ts = tile([P, B, PACK], F32, "minus_ts")
+        ts_squared = tile([P, B, PACK], F32, "ts_squared")
+        wt_spread = tile([P, B, N], F32, "wt_spread")
+
+        def gather(copy, b, t, cols):
+            copy(out=listed[b][:, t * N + cols.start:t * N + cols.stop], in_=planes[t][:].indirect(entries(b, cols)))
+
+        def deal_listed(copy, b, grouped, half):
+            copy(out=grouped.rearrange("p (s m t) -> p s m t", s=PACK, t=PACK)[:, block(half, 2)],
+                 in_=listed[b][:].rearrange("p (t m s) -> p s m t", t=PACK, s=PACK)[:, block(half, 2)])
+
+        def turn_words(copy, rows, half, grouped, bank):
+            words = rows[:].bitcast(F32)
+            for e in range(2):
+                first = (2 * half + e) * WORDS
+                for u in range(2):
+                    nc.tensor.transpose(bank[:, 2 * e + u, :], words[:, first + u:first + WORDS:2], ident[:])
+            copy(out=grouped.bitcast(F32).rearrange("p (e m u) -> p e m u", e=2, u=2),
+                 in_=bank[:].rearrange("p (e u) m -> p e m u", u=2))
+
+        def weigh_targets(b, t, weighted, on_gpsimd):
+            out = weighted[:, t, :].rearrange("p (s a k) -> p a s k", s=PACK, k=PACK)
+            in_ = y_raw[b][t // 2][:, t % 2, :].rearrange("p (a k s) -> p a s k", s=PACK, k=PACK)
+            if on_gpsimd:
+                nc.gpsimd.tensor_scalar(out=out, in0=in_, scalar1=wt_rows[:, b, t:t + 1], scalar2=0.0,
+                                        op0=MULT, op1=ADD)
+            else:
+                nc.scalar.activation(out=out, in_=in_, func=COPY, scale=wt_rows[:, b, t:t + 1])
+
+        def turn_targets(weighted, t, target_banks):
             for s in range(PACK):
-                nc.tensor.transpose(bank[:, s, :], words[s], ident[:])
+                nc.tensor.transpose(target_banks[s][:, t, :], weighted[:, t, block(s)], ident[:])
 
-        def turn_pairs(b, u, bank, copy):
-            words = listed[:, b, u, :].bitcast(F32)
-            turn_words([words[:, s:N:PACK] for s in range(PACK)], bank)
-            copy(out=w_slots[b][:, HALVES[u], :].rearrange("p (a k) s -> p a s k", k=PACK),
-                 in_=flat(bank[:]).bitcast(BF16).rearrange("p (s a k) -> p a s k", s=PACK, k=PACK))
+        def weigh_scores(b, s, bank, scored):
+            nc.vector.scalar_tensor_tensor(out=scored[:, s, :], in0=flat(bank[:]), scalar=ts_squared[:, b, s:s + 1],
+                                           in1=wt_spread[:, b, :], op0=MULT, op1=MULT)
 
-        def quantise_rows(b, half, stage):
-            quantise(xm_op[b][half], E4M3, stage, slice(0, N // 2))
+        def residual(b, s, bank, scored):
+            nc.vector.scalar_tensor_tensor(out=h_rows[b][:, block(s, N)].rearrange("p (q t) -> p q t", t=PACK),
+                                           in0=bank[:].rearrange("p t q -> p q t"), scalar=minus_ts[:, b, s:s + 1],
+                                           in1=scored[:, s, :].rearrange("p (q t) -> p q t", t=PACK),
+                                           op0=MULT, op1=ADD)
 
-        def table_gradient(b, c, bank):
+        def in_order(copy, staged, bank):
+            copy(out=staged.rearrange("p (m a) -> p m a", a=PACK), in_=bank[:].rearrange("p a m -> p m a"))
+
+        def table_gradient(copy, b, c, bank, staged):
             product(bank, xm_op[b][c // 2], E4M3, c % 2, h_op[b], E5M2)
-
-        def part(name, j, tag=None):
-            return sbuf.tile([P, PACK, P], F32, name=name, tag=tag or "%s%d" % (name, j), align_bytes=64)
-
-        def by_row(bank):
-            return flat(bank[:]).rearrange("p (m t) -> p t m", t=PACK)
-
-        def turn_targets(b, j, bank, rows):
-            for t in rows:
-                nc.tensor.transpose(bank[:, t, :], y_raw[b][:, t, block(j)], ident[:])
-
-        def scale_targets(b, j, bank):
-            out = part("y_part", j)
-            nc.scalar.activation(out=out[:], in_=bank[:], func=COPY, scale=minus_ts[:, b, j:j + 1])
-            return out
-
-        def target_part(b, j, bank):
-            turn_targets(b, j, bank, range(PACK))
-            return scale_targets(b, j, bank)
-
-        def turn_part(bank, term):
-            for t in range(PACK):
-                nc.tensor.transpose(bank[:, t, :], term[:, t, :], ident[:])
-
-        def turn_sum(bank, first, second):
-            for t in range(PACK):
-                nc.tensor.matmul(bank[:, t, :], lhsT=first[:, t, :], rhs=ident[:], start=True, stop=False,
-                                 is_transpose=True)
-                nc.tensor.matmul(bank[:, t, :], lhsT=second[:, t, :], rhs=ident[:], start=False, stop=True,
-                                 is_transpose=True)
-
-        def scores(b, j, bank):
-            product(bank, w_op[b], E4M3, j, x_op[b], E4M3)
-
-        def stage(b, c, bank):
-            staged = dw[b][c // 2][:, c % 2, :]
-            on_scalar(out=staged, in_=flat(bank[:]))
-            return staged
+            in_order(copy, staged, bank)
 
         def place(b, c, staged):
-            nc.vector.tensor_copy(windows[c][:].indirect(offsets[:, b * LIST_COLS:(b + 1) * LIST_COLS]),
-                                  staged)
-            if b == B - 1:
-                nc.sync.dma_start(out=out_0[block(c), :], in_=windows[c][:])
-
-        def scatter(b, c, bank):
-            place(b, c, stage(b, c, bank))
-
-        def row_gradient(b, half, bank_pair):
-            rows = slice(2 * half, 2 * half + 2)
-            for t, bank in zip(range(rows.start, rows.stop), bank_pair):
-                product(bank, h_slot_op[b], E5M2, t, w_slot_op[b], E4M3)
-                on_scalar(out=gx[b][half][:, t % 2, :].rearrange("p (m u e) -> p m u e", u=2, e=2),
-                          in_=flat(bank[:]).rearrange("p (u m e) -> p m u e", u=2, e=2))
-            nc.scalar.dma_start(out=by_partition(out_1[b])[:, rows, :], in_=gx[b][half][:])
-
-        nc.vector.tensor_copy(ts_listed[:], ts_window[:].indirect(offsets[:]))
-        for k in range(T // CHUNK):
-            cast_pairs(activation_copy, 0, k, 0, CHUNK)
-        for b in range(B):
-            gather(b, 0)
-        windows = [sbuf.tile([P, T], F32, name="window%d" % c, tag="pairs0" if c == 2 else "window%d" % c,
-                             align_bytes=64) for c in range(PACK)]
-        for c in range(PACK):
-            (nc.vector if c == 0 else nc.gpsimd).memset(windows[c][:].bitcast(I32), 0)
-        for k in range(T // CHUNK):
-            cast_pairs(activation_copy, 1, k, 0, CHUNK)
-        turn_pairs(0, 0, banks[6], on_vector)
-        turn_pairs(1, 0, banks[7], on_scalar)
-        for b in range(B):
-            for j in range(PACK):
-                nc.tensor.transpose(banks[b][:, j, :], ts_listed[:, block(PACK * b + j)], ident[:])
-            nc.vector.tensor_scalar(out=minus_ts[:, b, :], in0=banks[b][:, :, 0], scalar1=-1.0, scalar2=None, op0=MULT)
-        nc.vector.tensor_tensor(out=ts_squared[:], in0=minus_ts[:], in1=minus_ts[:], op=MULT)
-        for b in range(B):
-            gather(b, 1)
-        join_pairs(0, on_vector, I32)
-        quantise(w_op[0], E4M3, w_grouped[0], WHOLE)
-        x_grouped = grouped_tile("x_grouped0")
-        interleave(on_scalar, x_grouped, x_raw[0], WHOLE)
-        quantise(x_op[0], E4M3, x_grouped, WHOLE)
-        w_grouped.append(grouped_tile("w_grouped1", tag="x_grouped0"))
-        join_pairs(1, on_vector, I32)
-        quantise(w_op[1], E4M3, w_grouped[1], WHOLE)
-        dw = [[sbuf.tile([P, 2, N], F32, name="dw%d" % b, tag="chunk0%d" % (2 * b + k), align_bytes=64)
-               for k in range(2)]
-              for b in range(B)]
-        gx = [[sbuf.tile([P, 2, N], F32, name="gx%d" % b, tag="chunk1%d" % (2 * b + k), align_bytes=64)
-               for k in range(2)]
-              for b in range(B)]
-
-        for rows in (range(0, 2), range(2, PACK)):
-            for j in range(PACK):
-                turn_targets(0, j, banks[j], rows)
-        y_part = [scale_targets(0, j, banks[j]) for j in range(PACK)]
-        for j in range(PACK):
-            scores(0, j, banks[PACK + j])
-        early = sbuf.tile([P, PACK - 1, PACK, P], F32, name="residuals", tag="x_grouped0", align_bytes=64)
-        for j in range(PACK):
-            residual = early[:, j] if j < PACK - 1 else part("residual", j, "late_codes")
-            nc.vector.scalar_tensor_tensor(out=residual[:], in0=by_row(banks[PACK + j]),
-                                           scalar=ts_squared[:, 0, j:j + 1], in1=y_part[j][:], op0=MULT, op1=ADD)
-            turn_part(banks[j], residual)
-        for j in range(PACK):
-            nc.vector.tensor_tensor(out=h_grouped[0][:, block(j), :],
-                                    in0=banks[j][:].rearrange("p t i -> p i t"),
-                                    in1=wt_rows[:, 0:1, :].to_broadcast([P, P, PACK]), op=MULT)
-        late = sbuf.tile([P, 8, N // 2], U32, name="late_codes", tag="late_codes", align_bytes=64)
-        xm_op[0].extend([(late[:, 0], scales_tile("xm00", N // 2)), (late[:, 1], scales_tile("xm01", N // 2))])
-        x_op.append((flat(late[:, 2:4]), scales_tile("x1", N)))
-        w_slot_op = [(flat(late[:, 4:6]), scales_tile("w_i0", N))]
-        h_op = [(flat(late[:, 6:8]), scales_tile("h_r0", N)), operand("h_r1")]
-        halves = [sbuf.tile([P, N // 2, PACK], BF16, name="stage%d" % j, tag="y_raw0" if j == 1 else "y_part%d" % j,
-                            align_bytes=64) for j in range(PACK)]
-        x_stage = halves[2:]
-        interleave_on_gpsimd(halves[0], xm_raw[0][:, :, HALVES[0]], HALVES[0])
-        interleave(on_scalar, halves[1], xm_raw[0][:, :, HALVES[1]], HALVES[0])
-        quantise_rows(0, 0, halves[0])
-        for cols in HALVES:
-            quantise(h_op[0], E5M2, h_grouped[0], cols)
-        quantise_rows(0, 1, halves[1])
-        for half in range(2):
-            interleave(on_scalar, x_stage[half], x_raw[1][:, :, HALVES[half]], HALVES[0])
-            quantise((x_op[1][0][:, HALVES[half]], x_op[1][1][:, HALVES[half]]), E4M3, x_stage[half], HALVES[0])
-        turn_pairs(0, 1, banks[0], on_scalar)
-        quantise(w_slot_op[0], E4M3, w_slots[0], WHOLE)
-        for c in range(PACK - 1):
-            table_gradient(0, c, banks[PACK + c])
-        for c in range(PACK - 1):
-            scatter(0, c, banks[PACK + c])
-
-        xm_stage = grouped_tile("xm_stage", tag="w_slots0")
-        for half in range(2):
-            interleave_on_gpsimd(xm_stage, xm_raw[1], HALVES[half])
-        h_rows = sbuf.tile([P, PACK, N], BF16, name="h_rows", align_bytes=64)
-        sums = [banks[k] for k in (2, 1, 4, 5)]
-
-        def parts(j):
-            y_part = target_part(1, j, sums[j])
-            bank = banks[(7, 3, 0, 7)[j]]
-            scores(1, j, bank)
-            a_part = part("a_part", j)
-            nc.scalar.activation(out=a_part[:], in_=by_row(bank), func=COPY, scale=ts_squared[:, 1, j:j + 1])
-            return y_part, a_part
-
-        def weigh(j, y_part, a_part):
-            if j in ADDED_ON_GPSIMD:
-                nc.gpsimd.tensor_tensor(out=a_part[:], in0=a_part[:], in1=y_part[:], op=ADD)
-                turn_part(sums[j], a_part)
+            if c < 2:
+                for cols in HALVES:
+                    activation_copy(windows[c][:].indirect(entries(b, cols)), staged[:, cols])
             else:
-                turn_sum(sums[j], y_part, a_part)
+                on_vector(windows[c][:].indirect(entries(b, WHOLE)), staged)
+            if b == B - 1:
+                (nc.scalar if c < 2 else nc.sync).dma_start(out=out_0[block(c), :], in_=windows[c][:])
+
+        def row_gradient(b, j, bank, staged):
+            product(bank, h_slot_op[b], E5M2, j, w_slot_op[b], E4M3)
+            in_order(on_scalar, staged, bank)
+            nc.scalar.dma_start(out=out_1[b][block(j), :], in_=staged)
+
+        on_vector(ts_listed[:], ts_window[:].indirect(offsets[:]))
+        for b in range(B):
             for t in range(PACK):
-                nc.scalar.activation(out=h_rows[:, t, block(j)], in_=sums[j][:, t, :], func=COPY,
-                                     scale=wt_rows[:, 1, t:t + 1])
-            interleave_on_gpsimd(h_grouped[1], h_rows, block(j))
+                nc.tensor.transpose(banks[b][:, t, :], wt_rows[:, b, t:t + 1].to_broadcast([P, P]), ident[:])
+        for b in range(B):
+            for s in range(PACK):
+                nc.tensor.transpose(banks[2 + b][:, s, :], ts_listed[:, b * N + s:(b + 1) * N:PACK], ident[:])
+        gather(activation_copy, 0, 0, WHOLE)
+        gather(on_vector, 1, 0, WHOLE)
+        for b in range(B):
+            in_order(on_scalar, wt_spread[:, b, :], banks[b])
+        gather(activation_copy, 0, 1, WHOLE)
+        gather(on_vector, 1, 1, WHOLE)
+        for b in range(B):
+            nc.vector.tensor_scalar(out=minus_ts[:, b, :], in0=banks[2 + b][:, :, P - 1], scalar1=-1.0, scalar2=None,
+                                    op0=MULT)
+        nc.vector.tensor_tensor(out=ts_squared[:], in0=minus_ts[:], in1=minus_ts[:], op=MULT)
+        gather(activation_copy, 0, 2, WHOLE)
+        gather(on_vector, 1, 2, WHOLE)
+        w_slots = [[half_values("w_slots%d" % b)[:]] for b in range(B)]
+        turn_words(on_scalar, listed[0], 0, w_slots[0][0], banks[4])
+        turn_words(on_vector, listed[1], 0, w_slots[1][0], banks[5])
+        gather(activation_copy, 0, 3, HALVES[0])
+        gather(on_vector, 0, 3, HALVES[1])
+        gather(activation_copy, 1, 3, WHOLE)
+        w_grouped = values("w_grouped0")
+        x_grouped = values("x_grouped0")
+        w_op = [operand("w_d0")]
+        x_op = [operand("x0")]
+        for half in range(2):
+            deal_listed(on_vector, 0, w_grouped[:], half)
+        interleave(on_scalar, x_grouped[:], x_first[0][:], HALVES[0])
+        quantise(w_op[0], E4M3, w_grouped, WHOLE)
+        interleave(on_vector, x_grouped[:], x_first[1][:], HALVES[1])
+        quantise(x_op[0], E4M3, x_grouped, WHOLE)
+        laid = tile([P, 2 * PACK * N], BF16, "laid_beside_group0", "x_grouped0")
+        w_grouped = laid[:, 0:PACK * N]
+        for b in range(B):
+            w_slots[b].append(laid[:, block(2 + b, PACK * N // 2)])
+            turn_words(on_vector, listed[b], 1, w_slots[b][1], banks[6 + b])
 
-        made = [parts(j) for j in range(PACK)]
-        turn_pairs(1, 1, banks[6], on_scalar)
-        table_gradient(0, 3, banks[6])
-        scatter(0, 3, banks[6])
-        xm_op[1].append((sbuf.tile([P, N // 2], U32, name="xm10_codes", tag="chunk01", align_bytes=64),
-                         scales_tile("xm10", N // 2)))
-        quantise_rows(1, 0, xm_stage[:, HALVES[0]])
+        weighted = tile([P, PACK, N], F32, "weighted0", "weighted")
+        scored = tile([P, PACK, N], F32, "scored0")
+        weigh_targets(0, 0, weighted, False)
+        turn_targets(weighted, 0, banks[0:4])
+        for s in range(PACK):
+            product(banks[4 + s], w_op[0], E4M3, s, x_op[0], E4M3)
+        for t in range(1, PACK):
+            weigh_targets(0, t, weighted, False)
+            turn_targets(weighted, t, banks[0:4])
+        for s in range(PACK):
+            weigh_scores(0, s, banks[4 + s], scored)
+        for s in range(PACK):
+            residual(0, s, banks[s], scored)
+        x_grouped = values("x_grouped1", "w_grouped0")
+        for half in range(2):
+            deal_listed(copy_on_gpsimd, 1, w_grouped, half)
+        for cols in HALVES:
+            interleave(copy_on_gpsimd, x_grouped[:], x_second[:, :, cols], cols)
+        xm_stage = half_values("xm_stage")
+        interleave(on_scalar, xm_stage[:], xm_raw[0][0][:], HALVES[0])
+        weighted = tile([P, PACK, N], F32, "weighted1", "weighted")
+        for t in range(2):
+            weigh_targets(1, t, weighted, False)
+        h_grouped = values("h_grouped0")
+        for half in range(2):
+            turn_words(on_scalar, h_rows[0], half, h_grouped[:, block(half, PACK * N // 2)], banks[4 + half])
+        codes = tile([P, 5, N // 2], U32, "codes_after_group0", "scored0")
+        w_op.append(operand("w_d1", N, flat(codes[:, 0:2])))
+        x_op.append(operand("x1", N, flat(codes[:, 2:4])))
+        xm_op = [[operand("xm00", N // 2, codes[:, 4])]]
+        h_op = [operand("h_r0")]
+        quantise(w_op[1], E4M3, w_grouped, WHOLE)
+        quantise(x_op[1], E4M3, x_grouped, WHOLE)
+        quantise(xm_op[0][0], E4M3, xm_stage, HALVES[0])
+        quantise(h_op[0], E5M2, h_grouped, WHOLE)
+
+        scored = tile([P, PACK, N], F32, "scored1")
+        target_banks = [banks[k] for k in (6, 7, 0, 1)]
+        score_banks = [banks[k] for k in (2, 3, 4, 2)]
+        for t in range(2):
+            turn_targets(weighted, t, target_banks)
+        for s in range(2):
+            product(score_banks[s], w_op[1], E4M3, s, x_op[1], E4M3)
+        for t in range(2, PACK):
+            weigh_targets(1, t, weighted, False)
+        first_stage = tile([P, N], F32, "first_stage", "plane0")
+        table_gradient(on_scalar, 0, 0, banks[5], first_stage[:])
+        place(0, 0, first_stage[:])
+        product(score_banks[2], w_op[1], E4M3, 2, x_op[1], E4M3)
+        weigh_scores(1, 0, score_banks[0], scored)
+        product(score_banks[3], w_op[1], E4M3, 3, x_op[1], E4M3)
+        for t in range(2, PACK):
+            turn_targets(weighted, t, target_banks)
+        for s in range(1, PACK):
+            weigh_scores(1, s, score_banks[s], scored)
+        for s in range(PACK):
+            residual(1, s, target_banks[s], scored)
+        h_by_slot = [h_rows[b][:].rearrange("p (s r) -> p s r", s=PACK) for b in range(B)]
+        laid = tile([P, 3 * PACK * N // 2], BF16, "laid_beside_group1", "h_grouped0")
+        h_slots, xm_stage = laid[:, 0:PACK * N], laid[:, PACK * N:]
+        interleave(copy_on_gpsimd, xm_stage, xm_raw[0][1][:], HALVES[0])
+        for cols in HALVES:
+            interleave(copy_on_gpsimd, h_slots, h_by_slot[0][:, :, cols], cols)
+        h_grouped = values("h_grouped1")
+        for half in range(2):
+            turn_words(on_scalar, h_rows[1], half, h_grouped[:, block(half, PACK * N // 2)], banks[3 + half])
+        codes = tile([P, 5, N // 2], U32, "codes_after_group1", "scored1")
+        xm_op[0].append(operand("xm01", N // 2, codes[:, 0]))
+        h_slot_op = [operand("h_i0", N, flat(codes[:, 1:3])), operand("h_i1")]
+        w_slot_op = [operand("w_i0", N, flat(codes[:, 3:5]))]
+        h_op.append(operand("h_r1"))
+        quantise(xm_op[0][1], E4M3, xm_stage, HALVES[0])
+        quantise(h_slot_op[0], E5M2, h_slots, WHOLE)
+        for half in range(2):
+            quantise(half_of(w_slot_op[0], half), E4M3, w_slots[0][half], HALVES[0])
+        quantise(h_op[1], E5M2, h_grouped, WHOLE)
+
+        laid = tile([P, 3 * N], F32, "laid_beside_scatter", "h_grouped1")
+        xm_grouped = laid[:, N:].bitcast(BF16)
+        vector_stage = tile([P, 2, N], F32, "vector_stage", "plane1")
+        scalar_stage = tile([P, PACK - 1, N], F32, "scalar_stage", "plane2")
+        rows_stage = tile([P, PACK, N], F32, "rows_stage0", "plane3")
+        table_gradient(on_vector, 0, 2, banks[6], laid[:, 0:N])
+        table_gradient(on_scalar, 0, 1, banks[4], scalar_stage[:, 0, :])
+        place(0, 2, laid[:, 0:N])
+        place(0, 1, scalar_stage[:, 0, :])
+        xm_whole = operand("xm1")
+        xm_op.append([half_of(xm_whole, half) for half in range(2)])
+        for half in range(2):
+            interleave(copy_on_gpsimd, xm_grouped, xm_raw[1][half][:], HALVES[half])
+        quantise(xm_whole, E4M3, xm_grouped, WHOLE)
         for j in range(PACK):
-            weigh(j, *made[j])
-        quantise(h_op[1], E5M2, h_grouped[1], WHOLE)
-        h_slots = [grouped_tile("h_slots0"), grouped_tile("h_slots1", tag="pairs1")]
-        h_words = flat(h_grouped[0][:]).bitcast(F32)
-
-        def turn_grouped(u, bank):
-            turn_words([h_words[:, 2 * s + u:2 * N:2 * PACK] for s in range(PACK)], bank)
-            on_scalar(out=h_slots[0][:, HALVES[u], :].rearrange("p (e a b) s -> p a s b e", e=2, b=2),
-                      in_=flat(bank[:]).bitcast(BF16).rearrange("p (s a b e) -> p a s b e", s=PACK, b=2, e=2))
-
-        def turn_rows(half, bank):
-            for t in range(2):
-                words = h_rows[:, 2 * half + t, :].bitcast(F32)
-                for u in range(2):
-                    nc.tensor.transpose(bank[:, 2 * t + u, :], words[:, u:N // 2:2], ident[:])
-            out_words = flat(h_slots[1][:, HALVES[half], :]).bitcast(F32)
-            on_scalar(out=out_words.rearrange("p (t m u) -> p t m u", t=2, u=2),
-                      in_=bank[:].rearrange("p (t u) m -> p t m u", u=2))
-
-        def product_and_scatter(c, bank):
-            table_gradient(1, c, bank)
-            scatter(1, c, bank)
-
-        table_gradient(1, 0, banks[4])
-        staged_first = stage(1, 0, banks[4])
-        last = sbuf.tile([P, 7, N // 2], U32, name="last_codes", tag="h_grouped1", align_bytes=64)
-        xm_op[1].append((last[:, 0], scales_tile("xm11", N // 2)))
-        h_slot_op = [(flat(last[:, 1 + 2 * b:3 + 2 * b]), scales_tile("h_i%d" % b, N)) for b in range(B)]
-        w_slot_op.append((flat(last[:, 5:7]), scales_tile("w_i1", N)))
-        turn_grouped(0, banks[3])
-        turn_grouped(1, banks[0])
-        quantise(h_slot_op[0], E5M2, h_slots[0], WHOLE)
-        quantise_rows(1, 1, xm_stage[:, HALVES[1]])
-        quantise(w_slot_op[1], E4M3, w_slots[1], WHOLE)
-        turn_rows(0, banks[7])
-        turn_rows(1, banks[6])
-        quantise(h_slot_op[1], E5M2, h_slots[1], WHOLE)
-        place(1, 0, staged_first)
-        product_and_scatter(1, banks[5])
-        row_gradient(0, 0, (banks[2], banks[1]))
-        row_gradient(0, 1, (banks[5], banks[3]))
-        row_gradient(1, 0, (banks[0], banks[7]))
-        product_and_scatter(2, banks[4])
-        row_gradient(1, 1, (banks[6], banks[2]))
-        product_and_scatter(3, banks[4])
+            row_gradient(0, j, banks[(7, 0, 1, 2)[j]], rows_stage[:, j, :])
+        w_slot_op.append(operand("w_i1", N, tile([P, N], U32, "w_i1_codes", "h_grouped1")[:]))
+        for half in range(2):
+            quantise(half_of(w_slot_op[1], half), E4M3, w_slots[1][half], HALVES[0])
+        table_gradient(on_vector, 1, 2, banks[6], vector_stage[:, 0, :])
+        place(1, 2, vector_stage[:, 0, :])
+        table_gradient(on_scalar, 1, 0, banks[4], scalar_stage[:, 1, :])
+        place(1, 0, scalar_stage[:, 1, :])
+        h_slots = values("h_slots1", "x_grouped0")
+        for cols in HALVES:
+            interleave(copy_on_gpsimd, h_slots[:], h_by_slot[1][:, :, cols], cols)
+        quantise(h_slot_op[1], E5M2, h_slots, WHOLE)
+        late_stage = tile([P, N], F32, "late_stage", "x_grouped0")
+        table_gradient(on_vector, 0, 3, banks[5], late_stage[:])
+        place(0, 3, late_stage[:])
+        table_gradient(on_scalar, 1, 1, banks[4], scalar_stage[:, 2, :])
+        table_gradient(on_scalar, 1, 3, banks[4], vector_stage[:, 1, :])
+        place(1, 3, vector_stage[:, 1, :])
+        place(1, 1, scalar_stage[:, 2, :])
+        rows_stage = tile([P, PACK, N], F32, "rows_stage1", "plane2")
+        for j in range(PACK):
+            row_gradient(1, j, banks[j], rows_stage[:, j, :])

@@ -23,6 +23,9 @@ T = 2048
 BANKS = 8
 OFFSET_ROWS = 16
 WORDS = N // 2
+LAST_SPLIT = 192
+VALUES = PACK * N
+CHAIN = 2 * VALUES
 WHOLE_PACK = slice(0, PACK)
 WHOLE = slice(0, N)
 HALVES = (slice(0, N // 2), slice(N // 2, N))
@@ -32,10 +35,14 @@ def tile_attend_gsq_wx_ts_kernel(tc, xT, wT, y, wt, ts, xm, offs, out_0, out_1):
     nc = tc.nc
     with ExitStack() as ctx:
         sbuf = ctx.enter_context(tc.tile_pool(name="sbuf", bufs=1))
+        shared = ctx.enter_context(tc.tile_pool(name="shared", bufs=1))
         psum = ctx.enter_context(tc.psum_pool(name="psum", bufs=1))
 
         def tile(shape, dtype, name, tag=None):
             return sbuf.tile(shape, dtype, name=name, tag=tag or name, align_bytes=64)
+
+        def placed(columns, dtype, name, offset):
+            return shared.tile([P, columns], dtype, name=name, align_bytes=64, offset=offset)[:]
 
         def flat(ap):
             return ap.rearrange("p a c -> p (a c)")
@@ -88,7 +95,7 @@ def tile_attend_gsq_wx_ts_kernel(tc, xT, wT, y, wt, ts, xm, offs, out_0, out_1):
         zeros = tile([P, P], F32, "zeros", "window0")
         nc.vector.memset(zeros[:], 0.0)
         ts_window = tile([P, T], F32, "ts_window")
-        nc.scalar.dma_start(out=ts_window[P - 1:P, :], in_=ts[0:1, :])
+        nc.sync.dma_start(out=ts_window[P - 1:P, :], in_=ts[0:1, :])
         wt_rows = tile([P, B, PACK], F32, "wt_rows")
         nc.scalar.dma_start(out=wt_rows[:], in_=wt.rearrange("b (p t) o -> p b (t o)", t=PACK))
         ident = tile([P, P], F32, "ident")
@@ -106,17 +113,14 @@ def tile_attend_gsq_wx_ts_kernel(tc, xT, wT, y, wt, ts, xm, offs, out_0, out_1):
             nc.sync.dma_start(out=raw[:], in_=by_partition(src)[:, rows, cols])
             return raw
 
-        def load_targets(b):
-            return [load(y[b], "y_raw%d%d" % (b, k), rows=block(k, 2)) for k in range(2)]
-
         offsets = sbuf.tile([P, B * N // OFFSET_ROWS], U16, name="offsets")
         nc.sync.dma_start(offsets[:], offs)
         planes = [load_plane(t) for t in range(PACK)]
         x_first = [load(xT[0], "x_raw0%d" % k, cols=HALVES[k]) for k in range(2)]
-        y_raw = [load_targets(0)]
+        y_raw = [[load(y[0], "y_raw0%d" % k, rows=block(k, 2)) for k in range(2)]]
         x_second = load(xT[1], "x_raw1")
         xm_raw = [[load(xm[0], "xm_raw00", cols=HALVES[0])]]
-        y_raw.append(load_targets(1))
+        y_raw.append([load(y[1], "y_raw1%d" % k, rows=block(k, 2)) for k in range(2)])
         xm_raw[0].append(load(xm[0], "xm_raw01", cols=HALVES[1]))
         xm_raw.append([load(xm[1], "xm_raw1%d" % k, cols=HALVES[k]) for k in range(2)])
 
@@ -128,8 +132,6 @@ def tile_attend_gsq_wx_ts_kernel(tc, xT, wT, y, wt, ts, xm, offs, out_0, out_1):
         listed = [values("listed%d" % b) for b in range(B)]
         h_rows = [values("h_rows%d" % b) for b in range(B)]
         ts_listed = tile([P, B * N], F32, "ts_listed")
-        minus_ts = tile([P, B, PACK], F32, "minus_ts")
-        ts_squared = tile([P, B, PACK], F32, "ts_squared")
         wt_spread = tile([P, B, N], F32, "wt_spread")
 
         def gather(copy, b, t, cols):
@@ -149,7 +151,7 @@ def tile_attend_gsq_wx_ts_kernel(tc, xT, wT, y, wt, ts, xm, offs, out_0, out_1):
                  in_=bank[:].rearrange("p (e u) m -> p e m u", u=2))
 
         def weigh_targets(b, t, weighted, on_gpsimd):
-            out = weighted[:, t, :].rearrange("p (s a k) -> p a s k", s=PACK, k=PACK)
+            out = weighted[t].rearrange("p (s a k) -> p a s k", s=PACK, k=PACK)
             in_ = y_raw[b][t // 2][:, t % 2, :].rearrange("p (a k s) -> p a s k", s=PACK, k=PACK)
             if on_gpsimd:
                 nc.gpsimd.tensor_scalar(out=out, in0=in_, scalar1=wt_rows[:, b, t:t + 1], scalar2=0.0,
@@ -159,38 +161,41 @@ def tile_attend_gsq_wx_ts_kernel(tc, xT, wT, y, wt, ts, xm, offs, out_0, out_1):
 
         def turn_targets(weighted, t, target_banks):
             for s in range(PACK):
-                nc.tensor.transpose(target_banks[s][:, t, :], weighted[:, t, block(s)], ident[:])
+                nc.tensor.transpose(target_banks[s][:, t, :], weighted[t][:, block(s)], ident[:])
+
+        def scored_rows(b):
+            first = tile([P, PACK - 1, N], F32, "scored%d" % b)
+            return [first[:, s, :] for s in range(PACK - 1)] + [tile([P, N], F32, "scored_last%d" % b, "last_row")[:]]
 
         def weigh_scores(b, s, bank, scored):
-            nc.vector.scalar_tensor_tensor(out=scored[:, s, :], in0=flat(bank[:]), scalar=ts_squared[:, b, s:s + 1],
+            nc.vector.scalar_tensor_tensor(out=scored[s], in0=flat(bank[:]), scalar=ts_squared[:, b, s:s + 1],
                                            in1=wt_spread[:, b, :], op0=MULT, op1=MULT)
 
         def residual(b, s, bank, scored):
             nc.vector.scalar_tensor_tensor(out=h_rows[b][:, block(s, N)].rearrange("p (q t) -> p q t", t=PACK),
                                            in0=bank[:].rearrange("p t q -> p q t"), scalar=minus_ts[:, b, s:s + 1],
-                                           in1=scored[:, s, :].rearrange("p (q t) -> p q t", t=PACK),
+                                           in1=scored[s].rearrange("p (q t) -> p q t", t=PACK),
                                            op0=MULT, op1=ADD)
 
         def in_order(copy, staged, bank):
             copy(out=staged.rearrange("p (m a) -> p m a", a=PACK), in_=bank[:].rearrange("p a m -> p m a"))
 
-        def table_gradient(copy, b, c, bank, staged):
+        def table_gradient(copy, b, c, bank):
             product(bank, xm_op[b][c // 2], E4M3, c % 2, h_op[b], E5M2)
-            in_order(copy, staged, bank)
+            in_order(copy, staged[b][c], bank)
 
-        def place(b, c, staged):
-            if c < 2:
-                for cols in HALVES:
-                    activation_copy(windows[c][:].indirect(entries(b, cols)), staged[:, cols])
-            else:
-                on_vector(windows[c][:].indirect(entries(b, WHOLE)), staged)
-            if b == B - 1:
+        def place(scatter, b, c, cols):
+            scatter(windows[c][:].indirect(entries(b, cols)), staged[b][c][:, cols])
+            if b == B - 1 and cols.stop == N:
                 (nc.scalar if c < 2 else nc.sync).dma_start(out=out_0[block(c), :], in_=windows[c][:])
 
-        def row_gradient(b, j, bank, staged):
+        def row_gradient(b, j, bank):
             product(bank, h_slot_op[b], E5M2, j, w_slot_op[b], E4M3)
-            in_order(on_scalar, staged, bank)
-            nc.scalar.dma_start(out=out_1[b][block(j), :], in_=staged)
+            in_order(on_scalar, rows_stage[b][:, j, :], bank)
+
+        def store_rows(queue, b, blocks):
+            queue.dma_start(out=out_1[b].rearrange("(j q) d -> q j d", q=P)[:, blocks, :],
+                            in_=rows_stage[b][:, blocks, :])
 
         on_vector(ts_listed[:], ts_window[:].indirect(offsets[:]))
         for b in range(B):
@@ -202,44 +207,49 @@ def tile_attend_gsq_wx_ts_kernel(tc, xT, wT, y, wt, ts, xm, offs, out_0, out_1):
         gather(activation_copy, 0, 0, WHOLE)
         gather(on_vector, 1, 0, WHOLE)
         for b in range(B):
-            in_order(on_scalar, wt_spread[:, b, :], banks[b])
+            in_order(activation_copy, wt_spread[:, b, :], banks[b])
         gather(activation_copy, 0, 1, WHOLE)
         gather(on_vector, 1, 1, WHOLE)
+        ts_columns = tile([P, 2, B, PACK], F32, "ts_columns", "plane1")
+        minus_ts, ts_squared = ts_columns[:, 0], ts_columns[:, 1]
         for b in range(B):
             nc.vector.tensor_scalar(out=minus_ts[:, b, :], in0=banks[2 + b][:, :, P - 1], scalar1=-1.0, scalar2=None,
                                     op0=MULT)
-        nc.vector.tensor_tensor(out=ts_squared[:], in0=minus_ts[:], in1=minus_ts[:], op=MULT)
-        gather(activation_copy, 0, 2, WHOLE)
+        nc.vector.tensor_tensor(out=ts_squared, in0=minus_ts, in1=minus_ts, op=MULT)
+        gather(activation_copy, 0, 2, HALVES[0])
         gather(on_vector, 1, 2, WHOLE)
-        w_slots = [[half_values("w_slots%d" % b)[:]] for b in range(B)]
+        gather(on_vector, 0, 2, HALVES[1])
+        early_slots = values("early_slots", "plane0")
+        w_slots = [[early_slots[:, block(b, PACK * N // 2)]] for b in range(B)]
         turn_words(on_scalar, listed[0], 0, w_slots[0][0], banks[4])
-        turn_words(on_vector, listed[1], 0, w_slots[1][0], banks[5])
-        gather(activation_copy, 0, 3, HALVES[0])
-        gather(on_vector, 0, 3, HALVES[1])
-        gather(activation_copy, 1, 3, WHOLE)
+        turn_words(on_scalar, listed[1], 0, w_slots[1][0], banks[5])
+        gather(activation_copy, 0, 3, slice(0, LAST_SPLIT))
+        gather(on_vector, 0, 3, slice(LAST_SPLIT, N))
+        gather(activation_copy, 1, 3, HALVES[0])
+        gather(on_vector, 1, 3, HALVES[1])
         w_grouped = values("w_grouped0")
-        x_grouped = values("x_grouped0")
+        x_grouped = placed(VALUES, BF16, "x_grouped0", CHAIN // 2)
         w_op = [operand("w_d0")]
         x_op = [operand("x0")]
         for half in range(2):
             deal_listed(on_vector, 0, w_grouped[:], half)
-        interleave(on_scalar, x_grouped[:], x_first[0][:], HALVES[0])
+        interleave(on_vector, x_grouped, x_first[0][:], HALVES[0])
+        interleave(on_scalar, x_grouped, x_first[1][:], HALVES[1])
         quantise(w_op[0], E4M3, w_grouped, WHOLE)
-        interleave(on_vector, x_grouped[:], x_first[1][:], HALVES[1])
         quantise(x_op[0], E4M3, x_grouped, WHOLE)
-        laid = tile([P, 2 * PACK * N], BF16, "laid_beside_group0", "x_grouped0")
+        laid = placed(2 * VALUES, BF16, "laid_beside_group0", CHAIN)
         w_grouped = laid[:, 0:PACK * N]
+        late_slots = placed(VALUES, BF16, "late_slots", 0)
         for b in range(B):
-            w_slots[b].append(laid[:, block(2 + b, PACK * N // 2)])
+            w_slots[b].append(late_slots[:, block(b, PACK * N // 2)])
             turn_words(on_vector, listed[b], 1, w_slots[b][1], banks[6 + b])
 
         weighted = tile([P, PACK, N], F32, "weighted0", "weighted")
-        scored = tile([P, PACK, N], F32, "scored0")
-        weigh_targets(0, 0, weighted, False)
-        turn_targets(weighted, 0, banks[0:4])
+        weighted = [weighted[:, t, :] for t in range(PACK)]
+        scored = scored_rows(0)
         for s in range(PACK):
             product(banks[4 + s], w_op[0], E4M3, s, x_op[0], E4M3)
-        for t in range(1, PACK):
+        for t in range(PACK):
             weigh_targets(0, t, weighted, False)
             turn_targets(weighted, t, banks[0:4])
         for s in range(PACK):
@@ -253,10 +263,11 @@ def tile_attend_gsq_wx_ts_kernel(tc, xT, wT, y, wt, ts, xm, offs, out_0, out_1):
             interleave(copy_on_gpsimd, x_grouped[:], x_second[:, :, cols], cols)
         xm_stage = half_values("xm_stage")
         interleave(on_scalar, xm_stage[:], xm_raw[0][0][:], HALVES[0])
-        weighted = tile([P, PACK, N], F32, "weighted1", "weighted")
+        weighted = tile([P, PACK, N], F32, "weighted1", "y_raw00")
+        weighted = [weighted[:, t, :] for t in range(PACK)]
         for t in range(2):
             weigh_targets(1, t, weighted, False)
-        h_grouped = values("h_grouped0")
+        h_grouped = laid[:, PACK * N:]
         for half in range(2):
             turn_words(on_scalar, h_rows[0], half, h_grouped[:, block(half, PACK * N // 2)], banks[4 + half])
         codes = tile([P, 5, N // 2], U32, "codes_after_group0", "scored0")
@@ -269,81 +280,82 @@ def tile_attend_gsq_wx_ts_kernel(tc, xT, wT, y, wt, ts, xm, offs, out_0, out_1):
         quantise(xm_op[0][0], E4M3, xm_stage, HALVES[0])
         quantise(h_op[0], E5M2, h_grouped, WHOLE)
 
-        scored = tile([P, PACK, N], F32, "scored1")
-        target_banks = [banks[k] for k in (6, 7, 0, 1)]
-        score_banks = [banks[k] for k in (2, 3, 4, 2)]
-        for t in range(2):
-            turn_targets(weighted, t, target_banks)
-        for s in range(2):
-            product(score_banks[s], w_op[1], E4M3, s, x_op[1], E4M3)
+        scored = scored_rows(1)
+        target_banks = [banks[k] for k in (3, 2, 1, 0)]
         for t in range(2, PACK):
             weigh_targets(1, t, weighted, False)
-        first_stage = tile([P, N], F32, "first_stage", "plane0")
-        table_gradient(on_scalar, 0, 0, banks[5], first_stage[:])
-        place(0, 0, first_stage[:])
-        product(score_banks[2], w_op[1], E4M3, 2, x_op[1], E4M3)
-        weigh_scores(1, 0, score_banks[0], scored)
-        product(score_banks[3], w_op[1], E4M3, 3, x_op[1], E4M3)
-        for t in range(2, PACK):
+        for s in range(2):
+            product(banks[6 + s], w_op[1], E4M3, s, x_op[1], E4M3)
+        stages = [tile([P, PACK, N], F32, "staged%d" % b, "plane%d" % (2 + b)) for b in range(B)]
+        staged = [[stages[b][:, c, :] for c in range(PACK)] for b in range(B)]
+        xm_grouped = values("xm_grouped1", "w_grouped0")
+        for c in range(2):
+            table_gradient(on_scalar, 0, c, banks[5 - c])
+        for half in range(2):
+            interleave(on_scalar, xm_grouped[:], xm_raw[1][half][:], HALVES[half])
+        for cols in HALVES:
+            for c in range(2):
+                place(activation_copy, 0, c, cols)
+        for s in range(2):
+            weigh_scores(1, s, banks[6 + s], scored)
+            product(banks[6 + s], w_op[1], E4M3, 2 + s, x_op[1], E4M3)
+        for t in range(PACK):
             turn_targets(weighted, t, target_banks)
-        for s in range(1, PACK):
-            weigh_scores(1, s, score_banks[s], scored)
+        for s in range(2, PACK):
+            weigh_scores(1, s, banks[4 + s], scored)
         for s in range(PACK):
             residual(1, s, target_banks[s], scored)
         h_by_slot = [h_rows[b][:].rearrange("p (s r) -> p s r", s=PACK) for b in range(B)]
-        laid = tile([P, 3 * PACK * N // 2], BF16, "laid_beside_group1", "h_grouped0")
-        h_slots, xm_stage = laid[:, 0:PACK * N], laid[:, PACK * N:]
+        laid = placed(5 * VALUES // 2, BF16, "laid_beside_group1", CHAIN)
+        h_slots, h_grouped, xm_stage = laid[:, 0:VALUES], laid[:, VALUES:2 * VALUES], laid[:, 2 * VALUES:]
         interleave(copy_on_gpsimd, xm_stage, xm_raw[0][1][:], HALVES[0])
         for cols in HALVES:
             interleave(copy_on_gpsimd, h_slots, h_by_slot[0][:, :, cols], cols)
-        h_grouped = values("h_grouped1")
-        for half in range(2):
-            turn_words(on_scalar, h_rows[1], half, h_grouped[:, block(half, PACK * N // 2)], banks[3 + half])
-        codes = tile([P, 5, N // 2], U32, "codes_after_group1", "scored1")
+        codes = tile([P, 7, N // 2], U32, "codes_after_group1", "scored1")
         xm_op[0].append(operand("xm01", N // 2, codes[:, 0]))
-        h_slot_op = [operand("h_i0", N, flat(codes[:, 1:3])), operand("h_i1")]
+        xm_whole = operand("xm1", N, flat(codes[:, 1:3]))
+        xm_op.append([half_of(xm_whole, half) for half in range(2)])
         w_slot_op = [operand("w_i0", N, flat(codes[:, 3:5]))]
+        h_slot_op = [operand("h_i0", N, flat(codes[:, 5:7])), operand("h_i1")]
         h_op.append(operand("h_r1"))
+        turn_words(on_vector, h_rows[1], 0, h_grouped[:, block(0, VALUES // 2)], banks[4])
         quantise(xm_op[0][1], E4M3, xm_stage, HALVES[0])
-        quantise(h_slot_op[0], E5M2, h_slots, WHOLE)
+        quantise(xm_whole, E4M3, xm_grouped, WHOLE)
+        turn_words(on_vector, h_rows[1], 1, h_grouped[:, block(1, VALUES // 2)], banks[5])
         for half in range(2):
             quantise(half_of(w_slot_op[0], half), E4M3, w_slots[0][half], HALVES[0])
+        quantise(h_slot_op[0], E5M2, h_slots, WHOLE)
+        staged[0][2] = tile([P, N], F32, "first_placed")[:]
+        table_gradient(on_vector, 0, 2, banks[6])
         quantise(h_op[1], E5M2, h_grouped, WHOLE)
 
-        laid = tile([P, 3 * N], F32, "laid_beside_scatter", "h_grouped1")
-        xm_grouped = laid[:, N:].bitcast(BF16)
-        vector_stage = tile([P, 2, N], F32, "vector_stage", "plane1")
-        scalar_stage = tile([P, PACK - 1, N], F32, "scalar_stage", "plane2")
-        rows_stage = tile([P, PACK, N], F32, "rows_stage0", "plane3")
-        table_gradient(on_vector, 0, 2, banks[6], laid[:, 0:N])
-        table_gradient(on_scalar, 0, 1, banks[4], scalar_stage[:, 0, :])
-        place(0, 2, laid[:, 0:N])
-        place(0, 1, scalar_stage[:, 0, :])
-        xm_whole = operand("xm1")
-        xm_op.append([half_of(xm_whole, half) for half in range(2)])
-        for half in range(2):
-            interleave(copy_on_gpsimd, xm_grouped, xm_raw[1][half][:], HALVES[half])
-        quantise(xm_whole, E4M3, xm_grouped, WHOLE)
+        rows_stage = [tile([P, PACK, N], F32, "rows_stage%d" % b, ("plane1", "weighted")[b]) for b in range(B)]
+        place(on_vector, 0, 2, WHOLE)
+        h_slots = placed(VALUES, BF16, "h_slots1", CHAIN)
+        for cols in HALVES:
+            interleave(copy_on_gpsimd, h_slots, h_by_slot[1][:, :, cols], cols)
         for j in range(PACK):
-            row_gradient(0, j, banks[(7, 0, 1, 2)[j]], rows_stage[:, j, :])
-        w_slot_op.append(operand("w_i1", N, tile([P, N], U32, "w_i1_codes", "h_grouped1")[:]))
+            row_gradient(0, j, banks[j])
+            store_rows(nc.sync, 0, block(j, 1))
+            if j == 1:
+                table_gradient(on_scalar, 1, 2, banks[7])
+        w_slot_op.append(operand("w_i1", N, tile([P, N], U32, "w_i1_codes", "first_placed")[:]))
         for half in range(2):
             quantise(half_of(w_slot_op[1], half), E4M3, w_slots[1][half], HALVES[0])
-        table_gradient(on_vector, 1, 2, banks[6], vector_stage[:, 0, :])
-        place(1, 2, vector_stage[:, 0, :])
-        table_gradient(on_scalar, 1, 0, banks[4], scalar_stage[:, 1, :])
-        place(1, 0, scalar_stage[:, 1, :])
-        h_slots = values("h_slots1", "x_grouped0")
-        for cols in HALVES:
-            interleave(copy_on_gpsimd, h_slots[:], h_by_slot[1][:, :, cols], cols)
+        place(on_vector, 1, 2, WHOLE)
         quantise(h_slot_op[1], E5M2, h_slots, WHOLE)
-        late_stage = tile([P, N], F32, "late_stage", "x_grouped0")
-        table_gradient(on_vector, 0, 3, banks[5], late_stage[:])
-        place(0, 3, late_stage[:])
-        table_gradient(on_scalar, 1, 1, banks[4], scalar_stage[:, 2, :])
-        table_gradient(on_scalar, 1, 3, banks[4], vector_stage[:, 1, :])
-        place(1, 3, vector_stage[:, 1, :])
-        place(1, 1, scalar_stage[:, 2, :])
-        rows_stage = tile([P, PACK, N], F32, "rows_stage1", "plane2")
+        table_gradient(on_scalar, 1, 0, banks[4])
+        table_gradient(on_scalar, 1, 3, banks[5])
+        place(activation_copy, 1, 0, HALVES[0])
+        table_gradient(on_scalar, 0, 3, banks[3])
+        for b in range(B):
+            place(on_vector, b, 3, WHOLE)
+        place(activation_copy, 1, 0, HALVES[1])
         for j in range(PACK):
-            row_gradient(1, j, banks[j], rows_stage[:, j, :])
+            row_gradient(1, j, banks[j])
+            if j == 2:
+                store_rows(nc.scalar, 1, block(0, 2))
+        table_gradient(on_scalar, 1, 1, banks[1])
+        store_rows(nc.scalar, 1, block(1, 2))
+        for cols in HALVES:
+            place(activation_copy, 1, 1, cols)

@@ -25,7 +25,8 @@ OFFSET_ROWS = 16
 WORDS = N // 2
 LAST_SPLIT = 192
 VALUES = PACK * N
-CHAIN = 2 * VALUES
+X_SPLIT = 320
+KIB = 1024
 WHOLE_PACK = slice(0, PACK)
 WHOLE = slice(0, N)
 HALVES = (slice(0, N // 2), slice(N // 2, N))
@@ -116,13 +117,11 @@ def tile_attend_gsq_wx_ts_kernel(tc, xT, wT, y, wt, ts, xm, offs, out_0, out_1):
         offsets = sbuf.tile([P, B * N // OFFSET_ROWS], U16, name="offsets")
         nc.sync.dma_start(offsets[:], offs)
         planes = [load_plane(t) for t in range(PACK)]
-        x_first = [load(xT[0], "x_raw0%d" % k, cols=HALVES[k]) for k in range(2)]
-        y_raw = [[load(y[0], "y_raw0%d" % k, rows=block(k, 2)) for k in range(2)]]
+        x_first = load(xT[0], "x_raw0")
+        y_raw = [[load(y[b], "y_raw%d%d" % (b, k), rows=block(k, 2)) for k in range(2)] for b in range(B)]
         x_second = load(xT[1], "x_raw1")
-        xm_raw = [[load(xm[0], "xm_raw00", cols=HALVES[0])]]
-        y_raw.append([load(y[1], "y_raw1%d" % k, rows=block(k, 2)) for k in range(2)])
-        xm_raw[0].append(load(xm[0], "xm_raw01", cols=HALVES[1]))
-        xm_raw.append([load(xm[1], "xm_raw1%d" % k, cols=HALVES[k]) for k in range(2)])
+        xm_first = [load(xm[0], "xm_raw0%d" % k, cols=HALVES[k]) for k in range(2)]
+        xm_second = load(xm[1], "xm_raw1")
 
         windows = [tile([P, T], F32, "window%d" % c) for c in range(PACK)]
         for c in range(PACK):
@@ -163,9 +162,8 @@ def tile_attend_gsq_wx_ts_kernel(tc, xT, wT, y, wt, ts, xm, offs, out_0, out_1):
             for s in range(PACK):
                 nc.tensor.transpose(target_banks[s][:, t, :], weighted[t][:, block(s)], ident[:])
 
-        def scored_rows(b):
-            first = tile([P, PACK - 1, N], F32, "scored%d" % b)
-            return [first[:, s, :] for s in range(PACK - 1)] + [tile([P, N], F32, "scored_last%d" % b, "last_row")[:]]
+        def scored_rows(b, first):
+            return [first[:, block(s, N)] for s in range(PACK - 1)] + [tile([P, N], F32, "scored_last%d" % b)[:]]
 
         def weigh_scores(b, s, bank, scored):
             nc.vector.scalar_tensor_tensor(out=scored[s], in0=flat(bank[:]), scalar=ts_squared[:, b, s:s + 1],
@@ -187,7 +185,7 @@ def tile_attend_gsq_wx_ts_kernel(tc, xT, wT, y, wt, ts, xm, offs, out_0, out_1):
         def place(scatter, b, c, cols):
             scatter(windows[c][:].indirect(entries(b, cols)), staged[b][c][:, cols])
             if b == B - 1 and cols.stop == N:
-                (nc.scalar if c < 2 else nc.sync).dma_start(out=out_0[block(c), :], in_=windows[c][:])
+                (nc.scalar if c == 0 else nc.sync).dma_start(out=out_0[block(c), :], in_=windows[c][:])
 
         def row_gradient(b, j, bank):
             product(bank, h_slot_op[b], E5M2, j, w_slot_op[b], E4M3)
@@ -225,28 +223,30 @@ def tile_attend_gsq_wx_ts_kernel(tc, xT, wT, y, wt, ts, xm, offs, out_0, out_1):
         turn_words(on_scalar, listed[1], 0, w_slots[1][0], banks[5])
         gather(activation_copy, 0, 3, slice(0, LAST_SPLIT))
         gather(on_vector, 0, 3, slice(LAST_SPLIT, N))
-        gather(activation_copy, 1, 3, HALVES[0])
-        gather(on_vector, 1, 3, HALVES[1])
+        gather(activation_copy, 1, 3, slice(LAST_SPLIT, N))
+        gather(on_vector, 1, 3, slice(0, LAST_SPLIT))
         w_grouped = values("w_grouped0")
-        x_grouped = placed(VALUES, BF16, "x_grouped0", CHAIN // 2)
+        x_grouped = placed(VALUES, BF16, "x_grouped0", 2 * KIB)
         w_op = [operand("w_d0")]
         x_op = [operand("x0")]
         for half in range(2):
             deal_listed(on_vector, 0, w_grouped[:], half)
-        interleave(on_vector, x_grouped, x_first[0][:], HALVES[0])
-        interleave(on_scalar, x_grouped, x_first[1][:], HALVES[1])
-        quantise(w_op[0], E4M3, w_grouped, WHOLE)
-        quantise(x_op[0], E4M3, x_grouped, WHOLE)
-        laid = placed(2 * VALUES, BF16, "laid_beside_group0", CHAIN)
-        w_grouped = laid[:, 0:PACK * N]
-        late_slots = placed(VALUES, BF16, "late_slots", 0)
+        for cols in HALVES:
+            quantise(w_op[0], E4M3, w_grouped, cols)
+        interleave(on_vector, x_grouped, x_first[:, :, HALVES[0]], HALVES[0])
+        interleave(on_scalar, x_grouped, x_first[:, :, HALVES[1]], HALVES[1])
+        for half in (1, 0):
+            quantise(x_op[0], E4M3, x_grouped, HALVES[half])
+        laid = placed(5 * VALUES // 2, BF16, "laid_beside_group0", 4 * KIB)
+        w_grouped = laid[:, 0:VALUES]
+        late_slots = [laid[:, 2 * VALUES:], placed(VALUES // 2, BF16, "late_slots", 2 * KIB)]
         for b in range(B):
-            w_slots[b].append(late_slots[:, block(b, PACK * N // 2)])
+            w_slots[b].append(late_slots[b])
             turn_words(on_vector, listed[b], 1, w_slots[b][1], banks[6 + b])
 
         weighted = tile([P, PACK, N], F32, "weighted0", "weighted")
         weighted = [weighted[:, t, :] for t in range(PACK)]
-        scored = scored_rows(0)
+        scored = scored_rows(0, tile([P, (PACK - 1) * N], F32, "scored0")[:])
         for s in range(PACK):
             product(banks[4 + s], w_op[0], E4M3, s, x_op[0], E4M3)
         for t in range(PACK):
@@ -259,17 +259,20 @@ def tile_attend_gsq_wx_ts_kernel(tc, xT, wT, y, wt, ts, xm, offs, out_0, out_1):
         x_grouped = values("x_grouped1", "w_grouped0")
         for half in range(2):
             deal_listed(copy_on_gpsimd, 1, w_grouped, half)
-        for cols in HALVES:
+        for cols in (slice(P, X_SPLIT), slice(X_SPLIT, N)):
             interleave(copy_on_gpsimd, x_grouped[:], x_second[:, :, cols], cols)
-        xm_stage = half_values("xm_stage")
-        interleave(on_scalar, xm_stage[:], xm_raw[0][0][:], HALVES[0])
-        weighted = tile([P, PACK, N], F32, "weighted1", "y_raw00")
+        weighted = tile([P, PACK, N], F32, "weighted1", "plane2")
         weighted = [weighted[:, t, :] for t in range(PACK)]
-        for t in range(2):
+        target_banks = banks[4:8]
+        for t in range(PACK):
             weigh_targets(1, t, weighted, False)
-        h_grouped = laid[:, PACK * N:]
+            turn_targets(weighted, t, target_banks)
+        interleave(on_scalar, x_grouped[:], x_second[:, :, block(0)], block(0))
+        xm_stage = half_values("xm_stage")
+        interleave(on_scalar, xm_stage[:], xm_first[0][:], HALVES[0])
+        h_grouped = laid[:, VALUES:2 * VALUES]
         for half in range(2):
-            turn_words(on_scalar, h_rows[0], half, h_grouped[:, block(half, PACK * N // 2)], banks[4 + half])
+            turn_words(on_scalar, h_rows[0], half, h_grouped[:, block(half, VALUES // 2)], banks[half])
         codes = tile([P, 5, N // 2], U32, "codes_after_group0", "scored0")
         w_op.append(operand("w_d1", N, flat(codes[:, 0:2])))
         x_op.append(operand("x1", N, flat(codes[:, 2:4])))
@@ -279,51 +282,48 @@ def tile_attend_gsq_wx_ts_kernel(tc, xT, wT, y, wt, ts, xm, offs, out_0, out_1):
         quantise(x_op[1], E4M3, x_grouped, WHOLE)
         quantise(xm_op[0][0], E4M3, xm_stage, HALVES[0])
         quantise(h_op[0], E5M2, h_grouped, WHOLE)
-
-        scored = scored_rows(1)
-        target_banks = [banks[k] for k in (3, 2, 1, 0)]
-        for t in range(2, PACK):
-            weigh_targets(1, t, weighted, False)
-        for s in range(2):
-            product(banks[6 + s], w_op[1], E4M3, s, x_op[1], E4M3)
-        stages = [tile([P, PACK, N], F32, "staged%d" % b, "plane%d" % (2 + b)) for b in range(B)]
-        staged = [[stages[b][:, c, :] for c in range(PACK)] for b in range(B)]
-        xm_grouped = values("xm_grouped1", "w_grouped0")
-        for c in range(2):
-            table_gradient(on_scalar, 0, c, banks[5 - c])
+        w_slot_op = [operand("w_i0", N, tile([P, N], U32, "w_i0_codes", "scored_last0")[:])]
         for half in range(2):
-            interleave(on_scalar, xm_grouped[:], xm_raw[1][half][:], HALVES[half])
+            quantise(half_of(w_slot_op[0], half), E4M3, w_slots[0][half], HALVES[0])
+
+        scored = scored_rows(1, placed((PACK - 1) * N, F32, "scored1", 4 * KIB))
+        for s in range(2):
+            product(banks[2 + s], w_op[1], E4M3, s, x_op[1], E4M3)
+        stages = [tile([P, PACK, N], F32, "staged%d" % b, ("x_raw0", "plane3")[b]) for b in range(B)]
+        staged = [[stages[b][:, c, :] for c in range(PACK)] for b in range(B)]
+        laid = placed(7 * VALUES // 2, BF16, "laid_beside_group1", 11 * KIB)
+        h_slots, h_grouped, xm_grouped = (laid[:, block(k, VALUES)] for k in range(3))
+        xm_stage = laid[:, 3 * VALUES:]
+        for c in range(2):
+            table_gradient(on_scalar, 0, c, banks[1 - c])
+        interleave(on_scalar, xm_stage, xm_first[1][:], HALVES[0])
         for cols in HALVES:
             for c in range(2):
                 place(activation_copy, 0, c, cols)
         for s in range(2):
-            weigh_scores(1, s, banks[6 + s], scored)
-            product(banks[6 + s], w_op[1], E4M3, 2 + s, x_op[1], E4M3)
-        for t in range(PACK):
-            turn_targets(weighted, t, target_banks)
+            weigh_scores(1, s, banks[2 + s], scored)
+            product(banks[2 + s], w_op[1], E4M3, 2 + s, x_op[1], E4M3)
+        for s in range(2):
+            residual(1, s, target_banks[s], scored)
         for s in range(2, PACK):
-            weigh_scores(1, s, banks[4 + s], scored)
-        for s in range(PACK):
+            weigh_scores(1, s, banks[s], scored)
+        for s in range(2, PACK):
             residual(1, s, target_banks[s], scored)
         h_by_slot = [h_rows[b][:].rearrange("p (s r) -> p s r", s=PACK) for b in range(B)]
-        laid = placed(5 * VALUES // 2, BF16, "laid_beside_group1", CHAIN)
-        h_slots, h_grouped, xm_stage = laid[:, 0:VALUES], laid[:, VALUES:2 * VALUES], laid[:, 2 * VALUES:]
-        interleave(copy_on_gpsimd, xm_stage, xm_raw[0][1][:], HALVES[0])
+        for cols in HALVES:
+            interleave(copy_on_gpsimd, xm_grouped, xm_second[:, :, cols], cols)
         for cols in HALVES:
             interleave(copy_on_gpsimd, h_slots, h_by_slot[0][:, :, cols], cols)
-        codes = tile([P, 7, N // 2], U32, "codes_after_group1", "scored1")
+        codes = placed(5 * N // 2, U32, "codes_after_group1", 4 * KIB).rearrange("p (a c) -> p a c", a=5)
         xm_op[0].append(operand("xm01", N // 2, codes[:, 0]))
         xm_whole = operand("xm1", N, flat(codes[:, 1:3]))
         xm_op.append([half_of(xm_whole, half) for half in range(2)])
-        w_slot_op = [operand("w_i0", N, flat(codes[:, 3:5]))]
-        h_slot_op = [operand("h_i0", N, flat(codes[:, 5:7])), operand("h_i1")]
+        h_slot_op = [operand("h_i0", N, flat(codes[:, 3:5])), operand("h_i1")]
         h_op.append(operand("h_r1"))
         turn_words(on_vector, h_rows[1], 0, h_grouped[:, block(0, VALUES // 2)], banks[4])
         quantise(xm_op[0][1], E4M3, xm_stage, HALVES[0])
         quantise(xm_whole, E4M3, xm_grouped, WHOLE)
         turn_words(on_vector, h_rows[1], 1, h_grouped[:, block(1, VALUES // 2)], banks[5])
-        for half in range(2):
-            quantise(half_of(w_slot_op[0], half), E4M3, w_slots[0][half], HALVES[0])
         quantise(h_slot_op[0], E5M2, h_slots, WHOLE)
         staged[0][2] = tile([P, N], F32, "first_placed")[:]
         table_gradient(on_vector, 0, 2, banks[6])
@@ -331,7 +331,7 @@ def tile_attend_gsq_wx_ts_kernel(tc, xT, wT, y, wt, ts, xm, offs, out_0, out_1):
 
         rows_stage = [tile([P, PACK, N], F32, "rows_stage%d" % b, ("plane1", "weighted")[b]) for b in range(B)]
         place(on_vector, 0, 2, WHOLE)
-        h_slots = placed(VALUES, BF16, "h_slots1", CHAIN)
+        h_slots = placed(VALUES, BF16, "h_slots1", 11 * KIB)
         for cols in HALVES:
             interleave(copy_on_gpsimd, h_slots, h_by_slot[1][:, :, cols], cols)
         for j in range(PACK):
@@ -351,11 +351,11 @@ def tile_attend_gsq_wx_ts_kernel(tc, xT, wT, y, wt, ts, xm, offs, out_0, out_1):
         for b in range(B):
             place(on_vector, b, 3, WHOLE)
         place(activation_copy, 1, 0, HALVES[1])
-        for j in range(PACK):
+        for j in range(PACK - 1):
             row_gradient(1, j, banks[j])
-            if j == 2:
-                store_rows(nc.scalar, 1, block(0, 2))
-        table_gradient(on_scalar, 1, 1, banks[1])
-        store_rows(nc.scalar, 1, block(1, 2))
-        for cols in HALVES:
-            place(activation_copy, 1, 1, cols)
+        table_gradient(on_scalar, 1, 1, banks[0])
+        store_rows(nc.scalar, 1, slice(0, PACK - 1))
+        row_gradient(1, PACK - 1, banks[PACK - 1])
+        place(activation_copy, 1, 1, HALVES[0])
+        store_rows(nc.scalar, 1, slice(PACK - 1, PACK))
+        place(on_vector, 1, 1, HALVES[1])

@@ -233,6 +233,8 @@ def tile_attend_gsq_wx_ts_kernel(tc, xT, wT, y, wt, ts, xm, offs, out_0, out_1):
             deal_listed(on_vector, 0, w_grouped[:], half)
         for cols in HALVES:
             quantise(w_op[0], E4M3, w_grouped, cols)
+        for k in range(2):
+            product(banks[4 + k], w_op[0], E4M3, k, w_op[0], E4M3)
         interleave(on_vector, x_grouped, x_first[:, :, HALVES[0]], HALVES[0])
         interleave(on_scalar, x_grouped, x_first[:, :, HALVES[1]], HALVES[1])
         for half in (1, 0):

@@ -184,8 +184,9 @@ def tile_attend_gsq_wx_ts_kernel(tc, xT, wT, y, wt, ts, xm, offs, out_0, out_1):
 
         def place(scatter, b, c, cols):
             scatter(windows[c][:].indirect(entries(b, cols)), staged[b][c][:, cols])
-            if b == B - 1 and cols.stop == N:
-                (nc.scalar if c == 0 else nc.sync).dma_start(out=out_0[block(c), :], in_=windows[c][:])
+
+        def store_window(queue, c):
+            queue.dma_start(out=out_0[block(c), :], in_=windows[c][:])
 
         def row_gradient(b, j, bank):
             product(bank, h_slot_op[b], E5M2, j, w_slot_op[b], E4M3)
@@ -219,7 +220,7 @@ def tile_attend_gsq_wx_ts_kernel(tc, xT, wT, y, wt, ts, xm, offs, out_0, out_1):
         gather(on_vector, 0, 2, HALVES[1])
         early_slots = values("early_slots", "plane0")
         w_slots = [[early_slots[:, block(b, PACK * N // 2)]] for b in range(B)]
-        turn_words(on_scalar, listed[0], 0, w_slots[0][0], banks[4])
+        turn_words(on_scalar, listed[0], 0, w_slots[0][0], banks[2])
         turn_words(on_scalar, listed[1], 0, w_slots[1][0], banks[5])
         gather(activation_copy, 0, 3, slice(0, LAST_SPLIT))
         gather(on_vector, 0, 3, slice(LAST_SPLIT, N))
@@ -233,17 +234,14 @@ def tile_attend_gsq_wx_ts_kernel(tc, xT, wT, y, wt, ts, xm, offs, out_0, out_1):
             deal_listed(on_vector, 0, w_grouped[:], half)
         for cols in HALVES:
             quantise(w_op[0], E4M3, w_grouped, cols)
-        for k in range(2):
-            product(banks[4 + k], w_op[0], E4M3, k, w_op[0], E4M3)
         interleave(on_vector, x_grouped, x_first[:, :, HALVES[0]], HALVES[0])
         interleave(on_scalar, x_grouped, x_first[:, :, HALVES[1]], HALVES[1])
         for half in (1, 0):
             quantise(x_op[0], E4M3, x_grouped, HALVES[half])
-        laid = placed(5 * VALUES // 2, BF16, "laid_beside_group0", 4 * KIB)
-        w_grouped = laid[:, 0:VALUES]
-        late_slots = [laid[:, 2 * VALUES:], placed(VALUES // 2, BF16, "late_slots", 2 * KIB)]
+        w_grouped = placed(VALUES, BF16, "w_grouped1", 4 * KIB)
+        late_slots = placed(VALUES, BF16, "late_slots", 0)
         for b in range(B):
-            w_slots[b].append(late_slots[b])
+            w_slots[b].append(late_slots[:, block(b, VALUES // 2)])
             turn_words(on_vector, listed[b], 1, w_slots[b][1], banks[6 + b])
 
         weighted = tile([P, PACK, N], F32, "weighted0", "weighted")
@@ -272,9 +270,9 @@ def tile_attend_gsq_wx_ts_kernel(tc, xT, wT, y, wt, ts, xm, offs, out_0, out_1):
         interleave(on_scalar, x_grouped[:], x_second[:, :, block(0)], block(0))
         xm_stage = half_values("xm_stage")
         interleave(on_scalar, xm_stage[:], xm_first[0][:], HALVES[0])
-        h_grouped = laid[:, VALUES:2 * VALUES]
+        h_halves = [placed(VALUES // 2, BF16, "h_half%d" % half, (26 - 11 * half) * KIB) for half in range(2)]
         for half in range(2):
-            turn_words(on_scalar, h_rows[0], half, h_grouped[:, block(half, VALUES // 2)], banks[half])
+            turn_words(on_scalar, h_rows[0], half, h_halves[half], banks[half])
         codes = tile([P, 5, N // 2], U32, "codes_after_group0", "scored0")
         w_op.append(operand("w_d1", N, flat(codes[:, 0:2])))
         x_op.append(operand("x1", N, flat(codes[:, 2:4])))
@@ -283,19 +281,17 @@ def tile_attend_gsq_wx_ts_kernel(tc, xT, wT, y, wt, ts, xm, offs, out_0, out_1):
         quantise(w_op[1], E4M3, w_grouped, WHOLE)
         quantise(x_op[1], E4M3, x_grouped, WHOLE)
         quantise(xm_op[0][0], E4M3, xm_stage, HALVES[0])
-        quantise(h_op[0], E5M2, h_grouped, WHOLE)
-        w_slot_op = [operand("w_i0", N, tile([P, N], U32, "w_i0_codes", "scored_last0")[:])]
         for half in range(2):
-            quantise(half_of(w_slot_op[0], half), E4M3, w_slots[0][half], HALVES[0])
+            quantise(half_of(h_op[0], half), E5M2, h_halves[half], HALVES[0])
 
-        scored = scored_rows(1, placed((PACK - 1) * N, F32, "scored1", 4 * KIB))
+        scored = scored_rows(1, placed((PACK - 1) * N, F32, "scored1", 16 * KIB))
         for s in range(2):
             product(banks[2 + s], w_op[1], E4M3, s, x_op[1], E4M3)
         stages = [tile([P, PACK, N], F32, "staged%d" % b, ("x_raw0", "plane3")[b]) for b in range(B)]
         staged = [[stages[b][:, c, :] for c in range(PACK)] for b in range(B)]
-        laid = placed(7 * VALUES // 2, BF16, "laid_beside_group1", 11 * KIB)
+        laid = placed(3 * VALUES, BF16, "laid_beside_group1", 4 * KIB)
         h_slots, h_grouped, xm_grouped = (laid[:, block(k, VALUES)] for k in range(3))
-        xm_stage = laid[:, 3 * VALUES:]
+        xm_stage = placed(VALUES // 2, BF16, "xm_second_half", 26 * KIB)
         for c in range(2):
             table_gradient(on_scalar, 0, c, banks[1 - c])
         interleave(on_scalar, xm_stage, xm_first[1][:], HALVES[0])
@@ -316,44 +312,52 @@ def tile_attend_gsq_wx_ts_kernel(tc, xT, wT, y, wt, ts, xm, offs, out_0, out_1):
             interleave(copy_on_gpsimd, xm_grouped, xm_second[:, :, cols], cols)
         for cols in HALVES:
             interleave(copy_on_gpsimd, h_slots, h_by_slot[0][:, :, cols], cols)
-        codes = placed(5 * N // 2, U32, "codes_after_group1", 4 * KIB).rearrange("p (a c) -> p a c", a=5)
+        codes = placed(9 * N // 2, U32, "codes_after_group1", 16 * KIB).rearrange("p (a c) -> p a c", a=9)
         xm_op[0].append(operand("xm01", N // 2, codes[:, 0]))
         xm_whole = operand("xm1", N, flat(codes[:, 1:3]))
         xm_op.append([half_of(xm_whole, half) for half in range(2)])
         h_slot_op = [operand("h_i0", N, flat(codes[:, 3:5])), operand("h_i1")]
         h_op.append(operand("h_r1"))
+        w_slot_op = [operand("w_i%d" % b, N, flat(codes[:, 5 + 2 * b:7 + 2 * b])) for b in range(B)]
         turn_words(on_vector, h_rows[1], 0, h_grouped[:, block(0, VALUES // 2)], banks[4])
         quantise(xm_op[0][1], E4M3, xm_stage, HALVES[0])
         quantise(xm_whole, E4M3, xm_grouped, WHOLE)
         turn_words(on_vector, h_rows[1], 1, h_grouped[:, block(1, VALUES // 2)], banks[5])
+        for half in range(2):
+            quantise(half_of(w_slot_op[0], half), E4M3, w_slots[0][half], HALVES[0])
         quantise(h_slot_op[0], E5M2, h_slots, WHOLE)
-        staged[0][2] = tile([P, N], F32, "first_placed")[:]
         table_gradient(on_vector, 0, 2, banks[6])
         quantise(h_op[1], E5M2, h_grouped, WHOLE)
 
         rows_stage = [tile([P, PACK, N], F32, "rows_stage%d" % b, ("plane1", "weighted")[b]) for b in range(B)]
         place(on_vector, 0, 2, WHOLE)
-        h_slots = placed(VALUES, BF16, "h_slots1", 11 * KIB)
+        h_slots = placed(VALUES, BF16, "h_slots1", 4 * KIB)
         for cols in HALVES:
             interleave(copy_on_gpsimd, h_slots, h_by_slot[1][:, :, cols], cols)
-        for j in range(PACK):
+        for j in range(PACK - 1):
             row_gradient(0, j, banks[j])
             store_rows(nc.sync, 0, block(j, 1))
             if j == 1:
                 table_gradient(on_scalar, 1, 2, banks[7])
-        w_slot_op.append(operand("w_i1", N, tile([P, N], U32, "w_i1_codes", "first_placed")[:]))
         for half in range(2):
             quantise(half_of(w_slot_op[1], half), E4M3, w_slots[1][half], HALVES[0])
         place(on_vector, 1, 2, WHOLE)
+        store_window(nc.sync, 2)
         quantise(h_slot_op[1], E5M2, h_slots, WHOLE)
         table_gradient(on_scalar, 1, 0, banks[4])
-        table_gradient(on_scalar, 1, 3, banks[5])
+        row_gradient(0, PACK - 1, banks[3])
         place(activation_copy, 1, 0, HALVES[0])
-        table_gradient(on_scalar, 0, 3, banks[3])
+        store_rows(nc.scalar, 0, block(PACK - 1, 1))
+        both = tile([P, B, N], F32, "both_groups", "x_raw1")
         for b in range(B):
-            place(on_vector, b, 3, WHOLE)
+            staged[b][3] = both[:, b, :]
+            table_gradient(on_scalar, b, 3, banks[(2, 5)[b]])
+        on_vector(windows[3][:].indirect(offsets[:]), flat(both[:]))
+        store_window(nc.sync, 3)
         place(activation_copy, 1, 0, HALVES[1])
-        for j in range(PACK - 1):
+        row_gradient(1, 0, banks[0])
+        store_window(nc.scalar, 0)
+        for j in range(1, PACK - 1):
             row_gradient(1, j, banks[j])
         table_gradient(on_scalar, 1, 1, banks[0])
         store_rows(nc.scalar, 1, slice(0, PACK - 1))
@@ -361,3 +365,4 @@ def tile_attend_gsq_wx_ts_kernel(tc, xT, wT, y, wt, ts, xm, offs, out_0, out_1):
         place(activation_copy, 1, 1, HALVES[0])
         store_rows(nc.scalar, 1, slice(PACK - 1, PACK))
         place(on_vector, 1, 1, HALVES[1])
+        store_window(nc.sync, 1)

from contextlib import ExitStack

import concourse.mybir as mybir

F32 = mybir.dt.float32
BF16 = mybir.dt.bfloat16
I32 = mybir.dt.int32
U32 = mybir.dt.uint32
U16 = mybir.dt.uint16
U8 = mybir.dt.uint8
E4M3 = mybir.dt.float8_e4m3fn_x4
E5M2 = mybir.dt.float8_e5m2_x4
COPY = mybir.ActivationFunctionType.Copy
MULT = mybir.AluOpType.mult
ADD = mybir.AluOpType.add
NOT_EQUAL = mybir.AluOpType.not_equal

P = 128
PACK = 4
B = 2
N = 512
T = 2048
BANKS = 8
OFFSET_ROWS = 16
WORDS = N // 2
LAST_SPLIT = 192
VALUES = PACK * N
X_SPLIT = 320
KIB = 1024
WHOLE_PACK = slice(0, PACK)
WHOLE = slice(0, N)
HALVES = (slice(0, N // 2), slice(N // 2, N))


def tile_attend_gsq_wx_ts_kernel(tc, xT, wT, y, wt, ts, xm, offs, out_0, out_1):
    nc = tc.nc
    with ExitStack() as ctx:
        sbuf = ctx.enter_context(tc.tile_pool(name="sbuf", bufs=1))
        shared = ctx.enter_context(tc.tile_pool(name="shared", bufs=1))
        psum = ctx.enter_context(tc.psum_pool(name="psum", bufs=1))

        def tile(shape, dtype, name, tag=None):
            return sbuf.tile(shape, dtype, name=name, tag=tag or name, align_bytes=64)

        def placed(columns, dtype, name, offset):
            return shared.tile([P, columns], dtype, name=name, align_bytes=64, offset=offset)[:]

        def flat(ap):
            return ap.rearrange("p a c -> p (a c)")

        def block(k, width=P):
            return slice(k * width, (k + 1) * width)

        def by_partition(rows):
            return rows.rearrange("(p t) c -> p t c", t=PACK)

        def values(name, tag=None):
            return tile([P, PACK * N], BF16, name, tag)

        def half_values(name, tag=None):
            return tile([P, PACK * N // 2], BF16, name, tag)

        def half_of(op, half):
            return op[0][:, HALVES[half]], op[1][:, HALVES[half]]

        def operand(name, width=N, codes=None):
            codes = tile([P, width], U32, name + "_codes")[:] if codes is None else codes
            return codes, tile([P, width], U8, name + "_scales")[:]

        def entries(b, cols):
            return offsets[:, (b * N + cols.start) // OFFSET_ROWS:(b * N + cols.stop) // OFFSET_ROWS]

        def copy_on_gpsimd(out, in_):
            nc.gpsimd.tensor_scalar(out=out, in0=in_, scalar1=1.0, scalar2=0.0, op0=MULT, op1=ADD)

        def activation_copy(out, in_):
            nc.scalar.activation(out=out, in_=in_, func=COPY)

        on_vector = nc.vector.tensor_copy
        on_scalar = nc.scalar.copy

        def interleave(copy, grouped, rows, cols):
            copy(out=grouped.rearrange("p (c t) -> p c t", t=PACK)[:, cols, :],
                 in_=rows.rearrange("p t c -> p c t"))

        def quantise(op, fmt, grouped, cols):
            nc.vector.quantize_mx(out=op[0][:, cols].bitcast(fmt), scales=op[1][:, cols],
                                  in_=grouped[:, PACK * cols.start:PACK * cols.stop])

        def product(bank, still, still_fmt, k, moving, moving_fmt):
            nc.tensor.matmul_mx(out=flat(bank[:]),
                                lhsT=still[0][:, block(k)].bitcast(still_fmt), lhsT_scale=still[1][:, block(k)],
                                rhs=moving[0].bitcast(moving_fmt), rhs_scale=moving[1],
                                start=True, stop=True)

        zeros = tile([P, P], F32, "zeros", "window0")
        nc.vector.memset(zeros[:], 0.0)
        ts_window = tile([P, T], F32, "ts_window")
        nc.sync.dma_start(out=ts_window[P - 1:P, :], in_=ts[0:1, :])
        wt_rows = tile([P, B, PACK], F32, "wt_rows")
        nc.scalar.dma_start(out=wt_rows[:], in_=wt.rearrange("b (p t) o -> p b (t o)", t=PACK))
        ident = tile([P, P], F32, "ident")
        nc.gpsimd.affine_select(out=ident[:], in_=zeros[:], pattern=[[-1, P]], compare_op=NOT_EQUAL, fill=1.0,
                                base=0, channel_multiplier=1)
        nc.gpsimd.memset(ts_window[0:P - 1, :].bitcast(I32), 0)

        def load_plane(t):
            plane = tile([P, T], F32, "plane%d" % t)
            nc.sync.dma_start(out=plane[:], in_=by_partition(wT)[:, t, :])
            return plane

        def load(src, name, rows=WHOLE_PACK, cols=WHOLE):
            raw = tile([P, rows.stop - rows.start, cols.stop - cols.start], F32, name)
            nc.sync.dma_start(out=raw[:], in_=by_partition(src)[:, rows, cols])
            return raw

        offsets = sbuf.tile([P, B * N // OFFSET_ROWS], U16, name="offsets")
        nc.sync.dma_start(offsets[:], offs)
        planes = [load_plane(t) for t in range(PACK)]
        x_first = load(xT[0], "x_raw0")
        y_raw = [[load(y[b], "y_raw%d%d" % (b, k), rows=block(k, 2)) for k in range(2)] for b in range(B)]
        x_second = load(xT[1], "x_raw1")
        xm_first = [load(xm[0], "xm_raw0%d" % k, cols=HALVES[k]) for k in range(2)]
        xm_second = load(xm[1], "xm_raw1")

        windows = [tile([P, T], F32, "window%d" % c) for c in range(PACK)]
        for c in range(PACK):
            nc.gpsimd.memset(windows[c][:].bitcast(I32), 0)
        banks = [psum.tile([P, PACK, P], F32, name="bank%d" % k, tag="bank%d" % k) for k in range(BANKS)]

        listed = [values("listed%d" % b) for b in range(B)]
        h_rows = [values("h_rows%d" % b) for b in range(B)]
        ts_listed = tile([P, B * N], F32, "ts_listed")
        wt_spread = tile([P, B, N], F32, "wt_spread")

        def gather(copy, b, t, cols):
            copy(out=listed[b][:, t * N + cols.start:t * N + cols.stop], in_=planes[t][:].indirect(entries(b, cols)))

        def deal_listed(copy, b, grouped, half):
            copy(out=grouped.rearrange("p (s m t) -> p s m t", s=PACK, t=PACK)[:, block(half, 2)],
                 in_=listed[b][:].rearrange("p (t m s) -> p s m t", t=PACK, s=PACK)[:, block(half, 2)])

        def turn_words(copy, rows, half, grouped, bank):
            words = rows[:].bitcast(F32)
            for e in range(2):
                first = (2 * half + e) * WORDS
                for u in range(2):
                    nc.tensor.transpose(bank[:, 2 * e + u, :], words[:, first + u:first + WORDS:2], ident[:])
            copy(out=grouped.bitcast(F32).rearrange("p (e m u) -> p e m u", e=2, u=2),
                 in_=bank[:].rearrange("p (e u) m -> p e m u", u=2))

        def weigh_targets(b, t, weighted, on_gpsimd):
            out = weighted[t].rearrange("p (s a k) -> p a s k", s=PACK, k=PACK)
            in_ = y_raw[b][t // 2][:, t % 2, :].rearrange("p (a k s) -> p a s k", s=PACK, k=PACK)
            if on_gpsimd:
                nc.gpsimd.tensor_scalar(out=out, in0=in_, scalar1=wt_rows[:, b, t:t + 1], scalar2=0.0,
                                        op0=MULT, op1=ADD)
            else:
                nc.scalar.activation(out=out, in_=in_, func=COPY, scale=wt_rows[:, b, t:t + 1])

        def turn_targets(weighted, t, target_banks):
            for s in range(PACK):
                nc.tensor.transpose(target_banks[s][:, t, :], weighted[t][:, block(s)], ident[:])

        def scored_rows(b, first):
            return [first[:, block(s, N)] for s in range(PACK - 1)] + [tile([P, N], F32, "scored_last%d" % b)[:]]

        def weigh_scores(b, s, bank, scored):
            nc.vector.scalar_tensor_tensor(out=scored[s], in0=flat(bank[:]), scalar=ts_squared[:, b, s:s + 1],
                                           in1=wt_spread[:, b, :], op0=MULT, op1=MULT)

        def residual(b, s, bank, scored):
            nc.vector.scalar_tensor_tensor(out=h_rows[b][:, block(s, N)].rearrange("p (q t) -> p q t", t=PACK),
                                           in0=bank[:].rearrange("p t q -> p q t"), scalar=minus_ts[:, b, s:s + 1],
                                           in1=scored[s].rearrange("p (q t) -> p q t", t=PACK),
                                           op0=MULT, op1=ADD)

        def in_order(copy, staged, bank):
            copy(out=staged.rearrange("p (m a) -> p m a", a=PACK), in_=bank[:].rearrange("p a m -> p m a"))

        def table_gradient(copy, b, c, bank):
            product(bank, xm_op[b][c // 2], E4M3, c % 2, h_op[b], E5M2)
            in_order(copy, staged[b][c], bank)

        def place(scatter, b, c, cols):
            scatter(windows[c][:].indirect(entries(b, cols)), staged[b][c][:, cols])

        def store_window(queue, c):
            queue.dma_start(out=out_0[block(c), :], in_=windows[c][:])

        def row_gradient(b, j, bank):
            product(bank, h_slot_op[b], E5M2, j, w_slot_op[b], E4M3)
            in_order(on_scalar, rows_stage[b][:, j, :], bank)

        def store_rows(queue, b, blocks):
            queue.dma_start(out=out_1[b].rearrange("(j q) d -> q j d", q=P)[:, blocks, :],
                            in_=rows_stage[b][:, blocks, :])

        on_vector(ts_listed[:], ts_window[:].indirect(offsets[:]))
        for b in range(B):
            for t in range(PACK):
                nc.tensor.transpose(banks[b][:, t, :], wt_rows[:, b, t:t + 1].to_broadcast([P, P]), ident[:])
        for b in range(B):
            for s in range(PACK):
                nc.tensor.transpose(banks[2 + b][:, s, :], ts_listed[:, b * N + s:(b + 1) * N:PACK], ident[:])
        gather(activation_copy, 0, 0, WHOLE)
        gather(on_vector, 1, 0, WHOLE)
        for b in range(B):
            in_order(activation_copy, wt_spread[:, b, :], banks[b])
        gather(activation_copy, 0, 1, WHOLE)
        gather(on_vector, 1, 1, WHOLE)
        ts_columns = tile([P, 2, B, PACK], F32, "ts_columns", "plane1")
        minus_ts, ts_squared = ts_columns[:, 0], ts_columns[:, 1]
        for b in range(B):
            nc.vector.tensor_scalar(out=minus_ts[:, b, :], in0=banks[2 + b][:, :, P - 1], scalar1=-1.0, scalar2=None,
                                    op0=MULT)
        nc.vector.tensor_tensor(out=ts_squared, in0=minus_ts, in1=minus_ts, op=MULT)
        gather(activation_copy, 0, 2, HALVES[0])
        gather(on_vector, 1, 2, WHOLE)
        gather(on_vector, 0, 2, HALVES[1])
        early_slots = values("early_slots", "plane0")
        w_slots = [[early_slots[:, block(b, PACK * N // 2)]] for b in range(B)]
        turn_words(on_scalar, listed[0], 0, w_slots[0][0], banks[2])
        turn_words(on_scalar, listed[1], 0, w_slots[1][0], banks[5])
        gather(activation_copy, 0, 3, slice(0, LAST_SPLIT))
        gather(on_vector, 0, 3, slice(LAST_SPLIT, N))
        gather(activation_copy, 1, 3, slice(LAST_SPLIT, N))
        gather(on_vector, 1, 3, slice(0, LAST_SPLIT))
        w_grouped = values("w_grouped0")
        x_grouped = placed(VALUES, BF16, "x_grouped0", 2 * KIB)
        w_op = [operand("w_d0")]
        x_op = [operand("x0")]
        for half in range(2):
            deal_listed(on_vector, 0, w_grouped[:], half)
        for cols in HALVES:
            quantise(w_op[0], E4M3, w_grouped, cols)
        interleave(on_vector, x_grouped, x_first[:, :, HALVES[0]], HALVES[0])
        interleave(on_scalar, x_grouped, x_first[:, :, HALVES[1]], HALVES[1])
        for half in (1, 0):
            quantise(x_op[0], E4M3, x_grouped, HALVES[half])
        w_grouped = placed(VALUES, BF16, "w_grouped1", 4 * KIB)
        late_slots = placed(VALUES, BF16, "late_slots", 0)
        for b in range(B):
            w_slots[b].append(late_slots[:, block(b, VALUES // 2)])
            turn_words(on_vector, listed[b], 1, w_slots[b][1], banks[6 + b])

        weighted = tile([P, PACK, N], F32, "weighted0", "weighted")
        weighted = [weighted[:, t, :] for t in range(PACK)]
        scored = scored_rows(0, tile([P, (PACK - 1) * N], F32, "scored0")[:])
        for s in range(PACK):
            product(banks[4 + s], w_op[0], E4M3, s, x_op[0], E4M3)
        for t in range(PACK):
            weigh_targets(0, t, weighted, False)
            turn_targets(weighted, t, banks[0:4])
        for s in range(PACK):
            weigh_scores(0, s, banks[4 + s], scored)
        for s in range(PACK):
            residual(0, s, banks[s], scored)
        x_grouped = values("x_grouped1", "w_grouped0")
        for half in range(2):
            deal_listed(copy_on_gpsimd, 1, w_grouped, half)
        for cols in (slice(P, X_SPLIT), slice(X_SPLIT, N)):
            interleave(copy_on_gpsimd, x_grouped[:], x_second[:, :, cols], cols)
        weighted = tile([P, PACK, N], F32, "weighted1", "plane2")
        weighted = [weighted[:, t, :] for t in range(PACK)]
        target_banks = banks[4:8]
        for t in range(PACK):
            weigh_targets(1, t, weighted, False)
            turn_targets(weighted, t, target_banks)
        interleave(on_scalar, x_grouped[:], x_second[:, :, block(0)], block(0))
        xm_stage = half_values("xm_stage")
        interleave(on_scalar, xm_stage[:], xm_first[0][:], HALVES[0])
        h_halves = [placed(VALUES // 2, BF16, "h_half%d" % half, (26 - 11 * half) * KIB) for half in range(2)]
        for half in range(2):
            turn_words(on_scalar, h_rows[0], half, h_halves[half], banks[half])
        codes = tile([P, 5, N // 2], U32, "codes_after_group0", "scored0")
        w_op.append(operand("w_d1", N, flat(codes[:, 0:2])))
        x_op.append(operand("x1", N, flat(codes[:, 2:4])))
        xm_op = [[operand("xm00", N // 2, codes[:, 4])]]
        h_op = [operand("h_r0")]
        quantise(w_op[1], E4M3, w_grouped, WHOLE)
        quantise(x_op[1], E4M3, x_grouped, WHOLE)
        quantise(xm_op[0][0], E4M3, xm_stage, HALVES[0])
        for half in range(2):
            quantise(half_of(h_op[0], half), E5M2, h_halves[half], HALVES[0])

        scored = scored_rows(1, placed((PACK - 1) * N, F32, "scored1", 16 * KIB))
        for s in range(2):
            product(banks[2 + s], w_op[1], E4M3, s, x_op[1], E4M3)
        stages = [tile([P, PACK, N], F32, "staged%d" % b, ("x_raw0", "plane3")[b]) for b in range(B)]
        staged = [[stages[b][:, c, :] for c in range(PACK)] for b in range(B)]
        laid = placed(3 * VALUES, BF16, "laid_beside_group1", 4 * KIB)
        h_slots, h_grouped, xm_grouped = (laid[:, block(k, VALUES)] for k in range(3))
        xm_stage = placed(VALUES // 2, BF16, "xm_second_half", 26 * KIB)
        for c in range(2):
            table_gradient(on_scalar, 0, c, banks[1 - c])
        interleave(on_scalar, xm_stage, xm_first[1][:], HALVES[0])
        for cols in HALVES:
            for c in range(2):
                place(activation_copy, 0, c, cols)
        for s in range(2):
            weigh_scores(1, s, banks[2 + s], scored)
            product(banks[2 + s], w_op[1], E4M3, 2 + s, x_op[1], E4M3)
        for s in range(2):
            residual(1, s, target_banks[s], scored)
        for s in range(2, PACK):
            weigh_scores(1, s, banks[s], scored)
        for s in range(2, PACK):
            residual(1, s, target_banks[s], scored)
        h_by_slot = [h_rows[b][:].rearrange("p (s r) -> p s r", s=PACK) for b in range(B)]
        for cols in HALVES:
            interleave(copy_on_gpsimd, xm_grouped, xm_second[:, :, cols], cols)
        for cols in HALVES:
            interleave(copy_on_gpsimd, h_slots, h_by_slot[0][:, :, cols], cols)
        codes = placed(9 * N // 2, U32, "codes_after_group1", 16 * KIB).rearrange("p (a c) -> p a c", a=9)
        xm_op[0].append(operand("xm01", N // 2, codes[:, 0]))
        xm_whole = operand("xm1", N, flat(codes[:, 1:3]))
        xm_op.append([half_of(xm_whole, half) for half in range(2)])
        h_slot_op = [operand("h_i0", N, flat(codes[:, 3:5])), operand("h_i1")]
        h_op.append(operand("h_r1"))
        w_slot_op = [operand("w_i%d" % b, N, flat(codes[:, 5 + 2 * b:7 + 2 * b])) for b in range(B)]
        turn_words(on_vector, h_rows[1], 0, h_grouped[:, block(0, VALUES // 2)], banks[4])
        quantise(xm_op[0][1], E4M3, xm_stage, HALVES[0])
        quantise(xm_whole, E4M3, xm_grouped, WHOLE)
        turn_words(on_vector, h_rows[1], 1, h_grouped[:, block(1, VALUES // 2)], banks[5])
        for half in range(2):
            quantise(half_of(w_slot_op[0], half), E4M3, w_slots[0][half], HALVES[0])
        quantise(h_slot_op[0], E5M2, h_slots, WHOLE)
        table_gradient(on_vector, 0, 2, banks[6])
        quantise(h_op[1], E5M2, h_grouped, WHOLE)

        rows_stage = [tile([P, PACK, N], F32, "rows_stage%d" % b, ("plane1", "weighted")[b]) for b in range(B)]
        place(on_vector, 0, 2, WHOLE)
        h_slots = placed(VALUES, BF16, "h_slots1", 4 * KIB)
        for cols in HALVES:
            interleave(copy_on_gpsimd, h_slots, h_by_slot[1][:, :, cols], cols)
        for j in range(PACK - 1):
            row_gradient(0, j, banks[j])
            store_rows(nc.sync, 0, block(j, 1))
            if j == 1:
                table_gradient(on_scalar, 1, 2, banks[7])
        for half in range(2):
            quantise(half_of(w_slot_op[1], half), E4M3, w_slots[1][half], HALVES[0])
        place(on_vector, 1, 2, WHOLE)
        store_window(nc.sync, 2)
        quantise(h_slot_op[1], E5M2, h_slots, WHOLE)
        table_gradient(on_scalar, 1, 0, banks[4])
        row_gradient(0, PACK - 1, banks[3])
        place(activation_copy, 1, 0, HALVES[0])
        store_rows(nc.scalar, 0, block(PACK - 1, 1))
        both = tile([P, B, N], F32, "both_groups", "x_raw1")
        for b in range(B):
            staged[b][3] = both[:, b, :]
            table_gradient(on_scalar, b, 3, banks[(2, 5)[b]])
        on_vector(windows[3][:].indirect(offsets[:]), flat(both[:]))
        store_window(nc.sync, 3)
        place(activation_copy, 1, 0, HALVES[1])
        row_gradient(1, 0, banks[0])
        store_window(nc.scalar, 0)
        for j in range(1, PACK - 1):
            row_gradient(1, j, banks[j])
        table_gradient(on_scalar, 1, 1, banks[0])
        store_rows(nc.scalar, 1, slice(0, PACK - 1))
        row_gradient(1, PACK - 1, banks[PACK - 1])
        place(activation_copy, 1, 1, HALVES[0])
        store_rows(nc.scalar, 1, slice(PACK - 1, PACK))
        place(on_vector, 1, 1, HALVES[1])
        store_window(nc.sync, 1)
